import numpy as np
import ml_dtypes


def mxq(x, axis, fmt="e4m3"):
    dtype, down = {"e4m3": (ml_dtypes.float8_e4m3fn, 7), "e5m2": (ml_dtypes.float8_e5m2, 14)}[fmt]
    v = np.moveaxis(np.asarray(x, np.float32).astype(ml_dtypes.bfloat16).astype(np.float64), axis, -1)
    blocks = v.reshape(v.shape[:-1] + (-1, 32))
    amax = np.abs(blocks).max(-1, keepdims=True)
    byte = np.maximum(np.where(amax > 0, np.frexp(amax)[1] - 1 + 127, 0) - down, 1)
    scale = np.exp2(byte - 127.0)
    codes = (blocks / scale).astype(np.float32).astype(dtype).astype(np.float64)
    return np.moveaxis((codes * scale).reshape(v.shape), -1, axis)


WIDE = False


def mx_kscale(k):
    if not WIDE:
        return np.ones(k)
    levels = np.array([18, -18])
    if k % 512:
        return np.exp2(np.random.permutation(np.resize(levels, k // 32))).repeat(32)
    a = np.empty((k // 512, 16))
    for p in range(k // 512):
        a[p, :8] = np.random.permutation(np.resize(levels, 8))
        for g in range(8):
            far = levels[np.abs(levels - a[p, g]) >= 10]
            a[p, g + 8] = far[np.random.randint(len(far))]
    return np.exp2(a.ravel()).repeat(32)


def f64(x):
    return np.asarray(x).astype(np.float64)


def striped(idx):
    return np.tile(np.asarray(idx).reshape(-1, 16).T, (8, 1)).astype(np.uint16)


def unstriped(offs):
    return offs[:16].T.reshape(-1).astype(np.int64)


B, N, T, D, DV, R = 2, 512, 2048, 512, 512, 512


def setup_inputs():
    n = np.random.standard_normal
    idx = np.random.permutation(T)[:B * N]
    s = mx_kscale(D)[:, None]
    z = mx_kscale(R)[:, None]
    v = mx_kscale(DV)[:, None]
    q = n((B, D, R))
    do = n((B, DV, R))
    return {
        "qT": (q * s).astype(np.float32),
        "kT": (n((D, T)) * (1.00 / np.sqrt(D)) / s).astype(np.float32),
        "vT": (n((DV, T)) / np.sqrt(DV) / v).astype(np.float32),
        "doT": (do * v).astype(np.float32),
        "rw": (np.random.uniform(0.5, 1.5, (B, R, 1)) * 1.0 / np.sqrt(R) * z).astype(np.float32),
        "qm": (q.transpose(0, 2, 1) / z).astype(np.float32),
        "offs": striped(idx),
    }


def reference(qT, kT, vT, doT, rw, qm, offs):
    idx = unstriped(offs)
    pick = lambda x: x[:, idx].reshape(x.shape[0], B, N).transpose(1, 0, 2)
    a = mxq(f64(qT), 1, "e4m3").transpose(0, 2, 1) @ mxq(pick(f64(kT)), 1, "e4m3")
    p = np.tanh(a)
    dp = mxq(f64(doT), 1, "e5m2").transpose(0, 2, 1) @ mxq(pick(f64(vT)), 1, "e4m3")
    ds = f64(rw) * dp * (1.0 - p * p)
    dk = mxq(f64(qm), 1, "e4m3").transpose(0, 2, 1) @ mxq(ds, 1, "e5m2")
    gk = np.zeros((D, T))
    gk[:, idx] = dk.transpose(1, 0, 2).reshape(D, B * N)
    return gk

@@ -1,0 +1,198 @@
+from contextlib import ExitStack
+
+import concourse.mybir as mybir
+
+B, N, T, D, R = 2, 512, 2048, 512, 512
+FLOPS = 3 * 2 * B * N * D * R
+
+F32 = mybir.dt.float32
+BF16 = mybir.dt.bfloat16
+U32 = mybir.dt.uint32
+U16 = mybir.dt.uint16
+U8 = mybir.dt.uint8
+E4M3 = mybir.dt.float8_e4m3fn_x4
+E5M2 = mybir.dt.float8_e5m2_x4
+ACT = mybir.ActivationFunctionType
+ALU = mybir.AluOpType
+
+P = 128
+PACK = 4
+COLS = N // 16
+
+ENG = {"k0":"S","q0":"V","v0":"S","do0":"V","ds0":"V","qm0":"S","k1":"G","v1":"S","q1":"S","do1":"S","ds1":"S","qm1":"G"}
+WENG = ["S","S"]
+PIECES = {"V":1,"S":1,"G":4}
+SCAT = [256,512]
+
+
+def tile_attend_gat_tnh_k_kernel(tc, qT, kT, vT, doT, rw, qm, offs, out):
+    nc = tc.nc
+    with ExitStack() as ctx:
+        keep = ctx.enter_context(tc.tile_pool(name="keep", bufs=1))
+        work = ctx.enter_context(tc.tile_pool(name="work", bufs=1))
+        psum = ctx.enter_context(tc.psum_pool(name="psum", bufs=8))
+
+        offsets = keep.tile([P, B * COLS], U16, name="offsets")
+        nc.sync.dma_start(offsets[:], offs)
+
+        def load_planes(pool_ap, label):
+            rows = pool_ap.rearrange("(p j) t -> p j t", j=PACK)
+            planes = []
+            for j in range(PACK):
+                plane = work.tile([P, T], F32, name="%s%d" % (label, j), tag="raw", bufs=11)
+                nc.sync.dma_start(out=plane[:], in_=rows[:, j, :])
+                planes.append(plane)
+            return planes
+
+        def load_rows(src, label):
+            raw = work.tile([P, PACK, N], F32, name=label, tag="raw", bufs=11)
+            nc.sync.dma_start(out=raw[:], in_=src.rearrange("(p j) w -> p j w", j=PACK))
+            return raw
+
+        k_planes = load_planes(kT, "kp")
+        raw = {"q0": load_rows(qT[0], "q0")}
+        gate = keep.tile([P, B, PACK], F32, name="gate")
+        nc.sync.dma_start(out=gate[:], in_=rw.rearrange("b (p t) o -> p b (t o)", t=PACK))
+        v_planes = load_planes(vT, "vp")
+        raw["do0"] = load_rows(doT[0], "do0")
+        raw["qm0"] = load_rows(qm[0], "qm0")
+        raw["q1"] = load_rows(qT[1], "q1")
+        raw["do1"] = load_rows(doT[1], "do1")
+        raw["qm1"] = load_rows(qm[1], "qm1")
+
+        placed = []
+        for j in range(D // P):
+            tile = keep.tile([P, T], F32, name="placed%d" % j)
+            nc.gpsimd.memset(tile[:], 0.0)
+            placed.append(tile)
+        neg_gate = keep.tile([P, B, PACK], F32, name="neg_gate")
+        nc.gpsimd.tensor_scalar(neg_gate[:], gate[:], -1.0, 0.0, ALU.mult, ALU.add)
+
+        def gather(dst, planes, j, seqs):
+            lo, hi = seqs[0], seqs[-1] + 1
+            nc.vector.tensor_copy(
+                dst[:, j, lo * N : hi * N], planes[j][:].indirect(offsets[:, lo * COLS : hi * COLS])
+            )
+
+        packed = {}
+        grouped = {}
+
+        def interleave(label, src, turned):
+            dst = work.tile([P, PACK * N], BF16, name="g_" + label, tag="grouped", bufs=4, align_bytes=64)
+            if turned:
+                o = dst[:].rearrange("p (t m j) -> p m t j", t=PACK, j=PACK)
+                i = src.rearrange("p j (m t) -> p m t j", t=PACK)
+            else:
+                o = dst[:].rearrange("p (c i j) -> p c j i", i=PACK, j=PACK)
+                i = src.rearrange("p j (c i) -> p c j i", i=PACK)
+            eng = ENG[label]
+            step = P // PIECES[eng]
+            for c in range(0, P, step):
+                oo, ii = o[:, c : c + step], i[:, c : c + step]
+                if eng == "V":
+                    nc.vector.tensor_copy(oo, ii)
+                elif eng == "S":
+                    nc.scalar.copy(oo, ii)
+                else:
+                    nc.gpsimd.tensor_scalar(oo, ii, 1.0, 0.0, ALU.mult, ALU.add)
+            grouped[label] = dst
+
+        def quantize(label, fmt):
+            codes = keep.tile([P, N], U32, name="c_" + label, align_bytes=64)
+            scales = keep.tile([P, N], U8, name="s_" + label, align_bytes=64)
+            nc.vector.quantize_mx(out=codes[:].bitcast(fmt), scales=scales[:], in_=grouped[label][:])
+            packed[label] = (codes, scales, fmt)
+
+        def product(left, right, t):
+            lc, ls, lf = packed[left]
+            rc, rs, rf = packed[right]
+            bank = psum.tile([P, N], F32, name="bank", tag="bank")
+            cols = slice(t * P, (t + 1) * P)
+            nc.tensor.matmul_mx(
+                out=bank[:], lhsT=lc[:, cols].bitcast(lf), lhsT_scale=ls[:, cols],
+                rhs=rc[:].bitcast(rf), rhs_scale=rs[:], start=True, stop=True,
+            )
+            return bank
+
+        def weights(b):
+            w = work.tile([P, PACK, N], F32, name="w%d" % b, tag="w", bufs=2)
+            banks = [product("q%d" % b, "k%d" % b, t) for t in range(PACK)]
+            for t in range(PACK):
+                nc.scalar.activation(w[:, t, :], banks[t][:], ACT.Tanh)
+            for t in range(PACK):
+                nc.scalar.activation(w[:, t, :], w[:, t, :], ACT.Square)
+            for t in range(PACK):
+                if WENG[b] == "S":
+                    nc.scalar.activation(
+                        w[:, t, :], w[:, t, :], ACT.Identity, bias=gate[:, b, t : t + 1], scale=neg_gate[:, b, t : t + 1]
+                    )
+                else:
+                    nc.gpsimd.tensor_scalar(
+                        w[:, t, :], w[:, t, :], neg_gate[:, b, t : t + 1], gate[:, b, t : t + 1], ALU.mult, ALU.add
+                    )
+            return w
+
+        def score_grad(b, w):
+            banks = [product("do%d" % b, "v%d" % b, t) for t in range(PACK)]
+            for t in range(PACK):
+                nc.vector.tensor_tensor(w[:, t, :], banks[t][:], w[:, t, :], ALU.mult)
+            interleave("ds%d" % b, w[:], False)
+            quantize("ds%d" % b, E5M2)
+
+        def key_grad(b):
+            staged = []
+            for j in range(D // P):
+                bank = product("qm%d" % b, "ds%d" % b, j)
+                st = work.tile([P, N], F32, name="dk%d_%d" % (b, j), tag="dk", bufs=6)
+                nc.scalar.copy(st[:], bank[:])
+                staged.append(st)
+            return staged
+
+        def scatter(b, j, st):
+            n = SCAT[b]
+            for c in range(0, N, n):
+                lo = b * COLS + c // 16
+                nc.vector.tensor_copy(placed[j][:].indirect(offsets[:, lo : lo + n // 16]), st[:, c : c + n])
+
+        kg = work.tile([P, PACK, B * N], F32, name="kg")
+        vg = work.tile([P, PACK, B * N], F32, name="vg")
+
+        for j in range(PACK - 1):
+            gather(kg, k_planes, j, [0, 1])
+        gather(kg, k_planes, PACK - 1, [0])
+        interleave("k0", kg[:, :, 0:N], False)
+        gather(kg, k_planes, PACK - 1, [1])
+        interleave("q0", raw["q0"][:], True)
+        quantize("q0", E4M3)
+        quantize("k0", E4M3)
+        w0 = weights(0)
+        for j in range(PACK - 1):
+            gather(vg, v_planes, j, [0, 1])
+        gather(vg, v_planes, PACK - 1, [0])
+        interleave("v0", vg[:, :, 0:N], False)
+        interleave("do0", raw["do0"][:], True)
+        quantize("do0", E5M2)
+        quantize("v0", E4M3)
+        score_grad(0, w0)
+        interleave("qm0", raw["qm0"][:], False)
+        quantize("qm0", E4M3)
+        dk0 = key_grad(0)
+        gather(vg, v_planes, PACK - 1, [1])
+        interleave("k1", kg[:, :, N : 2 * N], False)
+        quantize("k1", E4M3)
+        interleave("v1", vg[:, :, N : 2 * N], False)
+        quantize("v1", E4M3)
+        interleave("q1", raw["q1"][:], True)
+        quantize("q1", E4M3)
+        w1 = weights(1)
+        interleave("do1", raw["do1"][:], True)
+        quantize("do1", E5M2)
+        score_grad(1, w1)
+        interleave("qm1", raw["qm1"][:], False)
+        quantize("qm1", E4M3)
+        dk1 = key_grad(1)
+        for j in range(D // P):
+            scatter(0, j, dk0[j])
+        for j in range(D // P):
+            scatter(1, j, dk1[j])
+            nc.sync.dma_start(out=out[j * P : (j + 1) * P, :], in_=placed[j][:])

@@ -19,10 +19,10 @@ P = 128
 PACK = 4
 COLS = N // 16
 
-ENG = {"k0":"S","q0":"V","v0":"S","do0":"V","ds0":"V","qm0":"S","k1":"G","v1":"S","q1":"S","do1":"S","ds1":"S","qm1":"G"}
-WENG = ["S","S"]
-PIECES = {"V":1,"S":1,"G":4}
-SCAT = [256,512]
+ENG = {"k0":"S","q0":"V","v0":"V","do0":"S","qm0":"S","k1":"S","v1":"S","q1":"S","do1":"S","qm1":"S"}
+PIECES = {"V":1,"S":1,"G":4,"q1":2,"do1":4,"qm0":2,"k1":2,"v1":4,"qm1":2}
+RING = {"k0":0,"q0":1,"k1":2,"v0":3,"do0":4,"qm0":0,"ds0":5,"q1":6,"v1":1,"do1":7,"qm1":6,"ds1":0}
+CODES = {"k0":0,"q0":1,"v0":2,"do0":3,"qm0":4,"ds0":5,"k1":2,"q1":1,"v1":0,"do1":3,"qm1":3,"ds1":6}
 
 
 def tile_attend_gat_tnh_k_kernel(tc, qT, kT, vT, doT, rw, qm, offs, out):
@@ -30,35 +30,35 @@ def tile_attend_gat_tnh_k_kernel(tc, qT, kT, vT, doT, rw, qm, offs, out):
     with ExitStack() as ctx:
         keep = ctx.enter_context(tc.tile_pool(name="keep", bufs=1))
         work = ctx.enter_context(tc.tile_pool(name="work", bufs=1))
-        psum = ctx.enter_context(tc.psum_pool(name="psum", bufs=8))
+        psum = ctx.enter_context(tc.psum_pool(name="psum", bufs=1))
 
         offsets = keep.tile([P, B * COLS], U16, name="offsets")
         nc.sync.dma_start(offsets[:], offs)
 
-        def load_planes(pool_ap, label):
+        def load_plane(pool_ap, label, j):
             rows = pool_ap.rearrange("(p j) t -> p j t", j=PACK)
-            planes = []
-            for j in range(PACK):
-                plane = work.tile([P, T], F32, name="%s%d" % (label, j), tag="raw", bufs=11)
-                nc.sync.dma_start(out=plane[:], in_=rows[:, j, :])
-                planes.append(plane)
-            return planes
+            plane = work.tile([P, T], F32, name="%s%d" % (label, j), tag="raw", bufs=8)
+            nc.sync.dma_start(out=plane[:], in_=rows[:, j, :])
+            return plane[:]
 
         def load_rows(src, label):
-            raw = work.tile([P, PACK, N], F32, name=label, tag="raw", bufs=11)
-            nc.sync.dma_start(out=raw[:], in_=src.rearrange("(p j) w -> p j w", j=PACK))
-            return raw
+            tile = work.tile([P, PACK, N], F32, name=label, tag="raw", bufs=8)
+            nc.sync.dma_start(out=tile[:], in_=src.rearrange("(p j) w -> p j w", j=PACK))
+            return tile
 
-        k_planes = load_planes(kT, "kp")
+        k_planes = [load_plane(kT, "kp", j) for j in range(PACK)]
         raw = {"q0": load_rows(qT[0], "q0")}
         gate = keep.tile([P, B, PACK], F32, name="gate")
         nc.sync.dma_start(out=gate[:], in_=rw.rearrange("b (p t) o -> p b (t o)", t=PACK))
-        v_planes = load_planes(vT, "vp")
-        raw["do0"] = load_rows(doT[0], "do0")
-        raw["qm0"] = load_rows(qm[0], "qm0")
-        raw["q1"] = load_rows(qT[1], "q1")
-        raw["do1"] = load_rows(doT[1], "do1")
-        raw["qm1"] = load_rows(qm[1], "qm1")
+        v_planes = [load_plane(vT, "vp", j) for j in range(2)]
+        v_pair = keep.tile([P, 2, T], F32, name="v_pair")
+        nc.sync.dma_start(out=v_pair[:], in_=vT.rearrange("(p j) t -> p j t", j=PACK)[:, 2:4, :])
+        v_planes += [v_pair[:, 0, :], v_pair[:, 1, :]]
+        wide = keep.tile([P, 6, N], F32, name="wide")
+        nc.sync.dma_start(out=wide[:, 2:6, :], in_=doT[0].rearrange("(p j) w -> p j w", j=PACK))
+        raw["do0"] = wide[:, 2:6, :]
+        for label, src in (("qm0", qm[0]), ("q1", qT[1]), ("do1", doT[1]), ("qm1", qm[1])):
+            raw[label] = load_rows(src, label)
 
         placed = []
         for j in range(D // P):
@@ -71,22 +71,27 @@ def tile_attend_gat_tnh_k_kernel(tc, qT, kT, vT, doT, rw, qm, offs, out):
         def gather(dst, planes, j, seqs):
             lo, hi = seqs[0], seqs[-1] + 1
             nc.vector.tensor_copy(
-                dst[:, j, lo * N : hi * N], planes[j][:].indirect(offsets[:, lo * COLS : hi * COLS])
+                dst[:, j, lo * N : hi * N], planes[j].indirect(offsets[:, lo * COLS : hi * COLS])
             )
 
-        packed = {}
-        grouped = {}
+        ring = [keep.tile([P, PACK * N], BF16, name="ring%d" % i, align_bytes=64)[:] for i in range(6)]
+        sq_tiles = [keep.tile([P, N * PACK], F32, name="sq%d" % b, align_bytes=64) for b in range(B)]
+        ring += [sq_tiles[0][:, 0 : 2 * N].bitcast(BF16), sq_tiles[0][:, 2 * N : 4 * N].bitcast(BF16)]
+        code_tiles = [keep.tile([P, N], U32, name="codes%d" % i, align_bytes=64) for i in range(max(CODES.values()) + 1)]
+        scale_tiles = [keep.tile([P, N], U8, name="scales%d" % i, align_bytes=64) for i in range(max(CODES.values()) + 1)]
+        banks = [psum.tile([P, N], F32, name="bank%d" % i) for i in range(8)]
+        fmts = {}
 
         def interleave(label, src, turned):
-            dst = work.tile([P, PACK * N], BF16, name="g_" + label, tag="grouped", bufs=4, align_bytes=64)
+            dst = ring[RING[label]]
             if turned:
-                o = dst[:].rearrange("p (t m j) -> p m t j", t=PACK, j=PACK)
+                o = dst.rearrange("p (t m j) -> p m t j", t=PACK, j=PACK)
                 i = src.rearrange("p j (m t) -> p m t j", t=PACK)
             else:
-                o = dst[:].rearrange("p (c i j) -> p c j i", i=PACK, j=PACK)
+                o = dst.rearrange("p (c i j) -> p c j i", i=PACK, j=PACK)
                 i = src.rearrange("p j (c i) -> p c j i", i=PACK)
             eng = ENG[label]
-            step = P // PIECES[eng]
+            step = P // PIECES.get(label, PIECES[eng])
             for c in range(0, P, step):
                 oo, ii = o[:, c : c + step], i[:, c : c + step]
                 if eng == "V":
@@ -95,104 +100,110 @@ def tile_attend_gat_tnh_k_kernel(tc, qT, kT, vT, doT, rw, qm, offs, out):
                     nc.scalar.copy(oo, ii)
                 else:
                     nc.gpsimd.tensor_scalar(oo, ii, 1.0, 0.0, ALU.mult, ALU.add)
-            grouped[label] = dst
 
         def quantize(label, fmt):
-            codes = keep.tile([P, N], U32, name="c_" + label, align_bytes=64)
-            scales = keep.tile([P, N], U8, name="s_" + label, align_bytes=64)
-            nc.vector.quantize_mx(out=codes[:].bitcast(fmt), scales=scales[:], in_=grouped[label][:])
-            packed[label] = (codes, scales, fmt)
+            nc.vector.quantize_mx(
+                out=code_tiles[CODES[label]][:].bitcast(fmt), scales=scale_tiles[CODES[label]][:], in_=ring[RING[label]]
+            )
+            fmts[label] = fmt
 
-        def product(left, right, t):
-            lc, ls, lf = packed[left]
-            rc, rs, rf = packed[right]
-            bank = psum.tile([P, N], F32, name="bank", tag="bank")
+        def product(dst, left, t, right, lo, hi):
+            lc, ls = code_tiles[CODES[left]], scale_tiles[CODES[left]]
+            rc, rs = code_tiles[CODES[right]], scale_tiles[CODES[right]]
             cols = slice(t * P, (t + 1) * P)
             nc.tensor.matmul_mx(
-                out=bank[:], lhsT=lc[:, cols].bitcast(lf), lhsT_scale=ls[:, cols],
-                rhs=rc[:].bitcast(rf), rhs_scale=rs[:], start=True, stop=True,
+                out=dst, lhsT=lc[:, cols].bitcast(fmts[left]), lhsT_scale=ls[:, cols],
+                rhs=rc[:, lo:hi].bitcast(fmts[right]), rhs_scale=rs[:, lo:hi], start=True, stop=True,
             )
-            return bank
 
-        def weights(b):
-            w = work.tile([P, PACK, N], F32, name="w%d" % b, tag="w", bufs=2)
-            banks = [product("q%d" % b, "k%d" % b, t) for t in range(PACK)]
-            for t in range(PACK):
-                nc.scalar.activation(w[:, t, :], banks[t][:], ACT.Tanh)
-            for t in range(PACK):
-                nc.scalar.activation(w[:, t, :], w[:, t, :], ACT.Square)
-            for t in range(PACK):
-                if WENG[b] == "S":
-                    nc.scalar.activation(
-                        w[:, t, :], w[:, t, :], ACT.Identity, bias=gate[:, b, t : t + 1], scale=neg_gate[:, b, t : t + 1]
-                    )
-                else:
-                    nc.gpsimd.tensor_scalar(
-                        w[:, t, :], w[:, t, :], neg_gate[:, b, t : t + 1], gate[:, b, t : t + 1], ALU.mult, ALU.add
-                    )
-            return w
+        def squares(b, bk):
+            sq = sq_tiles[b]
+            for c in range(N // P):
+                for t in range(PACK):
+                    product(bk[c][:, t * P : (t + 1) * P], "q%d" % b, t, "k%d" % b, c * P, (c + 1) * P)
+                nc.scalar.activation(
+                    sq[:, c * N : (c + 1) * N].rearrange("p (n t) -> p n t", t=PACK),
+                    bk[c][:].rearrange("p (t n) -> p n t", t=PACK),
+                    ACT.Tanh,
+                )
+            for h in range(2):
+                half = sq[:, h * 2 * N : (h + 1) * 2 * N]
+                nc.scalar.activation(half, half, ACT.Square)
+            return sq
 
-        def score_grad(b, w):
-            banks = [product("do%d" % b, "v%d" % b, t) for t in range(PACK)]
+        def score_grad(b, sq, bk, g):
             for t in range(PACK):
-                nc.vector.tensor_tensor(w[:, t, :], banks[t][:], w[:, t, :], ALU.mult)
-            interleave("ds%d" % b, w[:], False)
+                product(bk[t][:], "do%d" % b, t, "v%d" % b, 0, N)
+            ds = ring[RING["ds%d" % b]]
+            g = [x.rearrange("p a b -> p (a b)").rearrange("p (t n) -> p t n", t=PACK) for x in g]
+            for h in range(2):
+                lo, hi = h * N // 2, (h + 1) * N // 2
+                for t in range(PACK):
+                    nc.scalar.activation(g[h][:, t, :], bk[t][:, lo:hi], ACT.Copy, scale=neg_gate[:, b, t : t + 1])
+                nc.vector.scalar_tensor_tensor(
+                    ds[:, lo * PACK : hi * PACK].rearrange("p (n t) -> p n t", t=PACK),
+                    sq[:, lo * PACK : hi * PACK].rearrange("p (n t) -> p n t", t=PACK),
+                    1.0,
+                    g[h].rearrange("p t n -> p n t"),
+                    ALU.subtract,
+                    ALU.mult,
+                )
             quantize("ds%d" % b, E5M2)
 
-        def key_grad(b):
-            staged = []
+        def key_grad(b, bk):
             for j in range(D // P):
-                bank = product("qm%d" % b, "ds%d" % b, j)
-                st = work.tile([P, N], F32, name="dk%d_%d" % (b, j), tag="dk", bufs=6)
-                nc.scalar.copy(st[:], bank[:])
-                staged.append(st)
-            return staged
+                product(bk[j][:], "qm%d" % b, j, "ds%d" % b, 0, N)
 
-        def scatter(b, j, st):
-            n = SCAT[b]
-            for c in range(0, N, n):
-                lo = b * COLS + c // 16
-                nc.vector.tensor_copy(placed[j][:].indirect(offsets[:, lo : lo + n // 16]), st[:, c : c + n])
+        def place(b, j, bank, st):
+            nc.scalar.copy(st, bank[:])
+            nc.vector.tensor_copy(placed[j][:].indirect(offsets[:, b * COLS : (b + 1) * COLS]), st)
 
-        kg = work.tile([P, PACK, B * N], F32, name="kg")
-        vg = work.tile([P, PACK, B * N], F32, name="vg")
+        kg = keep.tile([P, PACK, B * N], F32, name="kg")
+        vg = [keep.tile([P, PACK, N], F32, name="vg0"), wide[:, 0:PACK, :]]
+
+        def gather_v(j, b):
+            nc.vector.tensor_copy(vg[b][:, j, :], v_planes[j].indirect(offsets[:, b * COLS : (b + 1) * COLS]))
+
 
         for j in range(PACK - 1):
             gather(kg, k_planes, j, [0, 1])
-        gather(kg, k_planes, PACK - 1, [0])
+        gather(kg, k_planes, 3, [0])
         interleave("k0", kg[:, :, 0:N], False)
-        gather(kg, k_planes, PACK - 1, [1])
+        gather(kg, k_planes, 3, [1])
         interleave("q0", raw["q0"][:], True)
         quantize("q0", E4M3)
         quantize("k0", E4M3)
-        w0 = weights(0)
-        for j in range(PACK - 1):
-            gather(vg, v_planes, j, [0, 1])
-        gather(vg, v_planes, PACK - 1, [0])
-        interleave("v0", vg[:, :, 0:N], False)
+        sq0 = squares(0, banks[0:4])
+        for j, b in ((0, 0), (0, 1), (1, 0), (1, 1), (2, 0), (3, 0)):
+            gather_v(j, b)
+        interleave("v0", vg[0][:], False)
+        quantize("v0", E4M3)
         interleave("do0", raw["do0"][:], True)
         quantize("do0", E5M2)
-        quantize("v0", E4M3)
-        score_grad(0, w0)
+        score_grad(0, sq0, banks[4:8], [raw["q0"][:, 0:2, :], wide[:, 3:5, :]])
         interleave("qm0", raw["qm0"][:], False)
         quantize("qm0", E4M3)
-        dk0 = key_grad(0)
-        gather(vg, v_planes, PACK - 1, [1])
+        key_grad(0, banks[0:4])
+        gather_v(2, 1)
         interleave("k1", kg[:, :, N : 2 * N], False)
         quantize("k1", E4M3)
-        interleave("v1", vg[:, :, N : 2 * N], False)
-        quantize("v1", E4M3)
         interleave("q1", raw["q1"][:], True)
         quantize("q1", E4M3)
-        w1 = weights(1)
+        gather_v(3, 1)
+        place(0, 0, banks[0], kg[:, 0, 0:N])
         interleave("do1", raw["do1"][:], True)
         quantize("do1", E5M2)
-        score_grad(1, w1)
+        interleave("v1", vg[1][:], False)
+        quantize("v1", E4M3)
+        place(0, 1, banks[1], wide[:, 3, :])
+        place(0, 2, banks[2], wide[:, 2, :])
+        sq1 = squares(1, banks[4:8])
+        score_grad(1, sq1, banks[4:8], [raw["qm0"][:, 0:2, :], raw["qm0"][:, 2:4, :]])
         interleave("qm1", raw["qm1"][:], False)
         quantize("qm1", E4M3)
-        dk1 = key_grad(1)
+        last = [banks[0], banks[1], banks[4], banks[5]]
+        key_grad(1, last)
+        place(0, 3, banks[3], sq1[:, 2 * N : 3 * N])
         for j in range(D // P):
-            scatter(0, j, dk0[j])
-        for j in range(D // P):
-            scatter(1, j, dk1[j])
+            place(1, j, last[j], vg[0][:, j, :])
             nc.sync.dma_start(out=out[j * P : (j + 1) * P, :], in_=placed[j][:])

@@ -19,10 +19,10 @@ P = 128
 PACK = 4
 COLS = N // 16
 
-ENG = {"k0":"S","q0":"V","v0":"V","do0":"S","qm0":"S","k1":"S","v1":"S","q1":"S","do1":"S","qm1":"S"}
-PIECES = {"V":1,"S":1,"G":4,"q1":2,"do1":4,"qm0":2,"k1":2,"v1":4,"qm1":2}
-RING = {"k0":0,"q0":1,"k1":2,"v0":3,"do0":4,"qm0":0,"ds0":5,"q1":6,"v1":1,"do1":7,"qm1":6,"ds1":0}
-CODES = {"k0":0,"q0":1,"v0":2,"do0":3,"qm0":4,"ds0":5,"k1":2,"q1":1,"v1":0,"do1":3,"qm1":3,"ds1":6}
+ENG = {"k0":"S","q0":"V","v0":"V","do0":"S","qm0":"S","k1":"S","v1":"G","q1":"S","do1":"S","qm1":"S"}
+PIECES = {"V":1,"S":1,"G":4,"q1":2,"do1":1,"qm0":1,"k1":1,"v1":4,"qm1":1,"do0":1}
+RING = {"k0":0,"q0":1,"k1":2,"v0":3,"do0":4,"qm0":0,"ds0":5,"q1":1,"v1":7,"do1":1,"qm1":1,"ds1":0}
+CODES = {"k0":0,"q0":1,"v0":2,"do0":3,"qm0":4,"ds0":5,"k1":2,"q1":3,"v1":0,"do1":4,"qm1":3,"ds1":6}
 
 
 def tile_attend_gat_tnh_k_kernel(tc, qT, kT, vT, doT, rw, qm, offs, out):
@@ -85,12 +85,15 @@ def tile_attend_gat_tnh_k_kernel(tc, qT, kT, vT, doT, rw, qm, offs, out):
         def interleave(label, src, turned):
             dst = ring[RING[label]]
             if turned:
-                o = dst.rearrange("p (t m j) -> p m t j", t=PACK, j=PACK)
-                i = src.rearrange("p j (m t) -> p m t j", t=PACK)
+                o = dst.rearrange("p (t m j) -> p m j t", t=PACK, j=PACK)
+                i = src.rearrange("p j (m t) -> p m j t", t=PACK)
             else:
                 o = dst.rearrange("p (c i j) -> p c j i", i=PACK, j=PACK)
                 i = src.rearrange("p j (c i) -> p c j i", i=PACK)
             eng = ENG[label]
+            if eng == "G":
+                o = dst.rearrange("p (c i j) -> p c i j", i=PACK, j=PACK)
+                i = src.rearrange("p j (c i) -> p c i j", i=PACK)
             step = P // PIECES.get(label, PIECES[eng])
             for c in range(0, P, step):
                 oo, ii = o[:, c : c + step], i[:, c : c + step]
@@ -180,7 +183,7 @@ def tile_attend_gat_tnh_k_kernel(tc, qT, kT, vT, doT, rw, qm, offs, out):
         quantize("v0", E4M3)
         interleave("do0", raw["do0"][:], True)
         quantize("do0", E5M2)
-        score_grad(0, sq0, banks[4:8], [raw["q0"][:, 0:2, :], wide[:, 3:5, :]])
+        score_grad(0, sq0, banks[4:8], [raw["q0"][:, 0:2, :], wide[:, 4:6, :]])
         interleave("qm0", raw["qm0"][:], False)
         quantize("qm0", E4M3)
         key_grad(0, banks[0:4])
@@ -191,11 +194,11 @@ def tile_attend_gat_tnh_k_kernel(tc, qT, kT, vT, doT, rw, qm, offs, out):
         quantize("q1", E4M3)
         gather_v(3, 1)
         place(0, 0, banks[0], kg[:, 0, 0:N])
-        interleave("do1", raw["do1"][:], True)
-        quantize("do1", E5M2)
         interleave("v1", vg[1][:], False)
         quantize("v1", E4M3)
-        place(0, 1, banks[1], wide[:, 3, :])
+        interleave("do1", raw["do1"][:], True)
+        quantize("do1", E5M2)
+        place(0, 1, banks[1], raw["q1"][:, 0, :])
         place(0, 2, banks[2], wide[:, 2, :])
         sq1 = squares(1, banks[4:8])
         score_grad(1, sq1, banks[4:8], [raw["qm0"][:, 0:2, :], raw["qm0"][:, 2:4, :]])

@@ -19,10 +19,10 @@ P = 128
 PACK = 4
 COLS = N // 16
 
-ENG = {"k0":"S","q0":"V","v0":"V","do0":"S","qm0":"S","k1":"S","v1":"G","q1":"S","do1":"S","qm1":"S"}
-PIECES = {"V":1,"S":1,"G":4,"q1":2,"do1":1,"qm0":1,"k1":1,"v1":4,"qm1":1,"do0":1}
-RING = {"k0":0,"q0":1,"k1":2,"v0":3,"do0":4,"qm0":0,"ds0":5,"q1":1,"v1":7,"do1":1,"qm1":1,"ds1":0}
-CODES = {"k0":0,"q0":1,"v0":2,"do0":3,"qm0":4,"ds0":5,"k1":2,"q1":3,"v1":0,"do1":4,"qm1":3,"ds1":6}
+ENG = {"k0":"S","q0":"V","v0":"V","do0":"S","qm0":"S","k1":"G","v1":"G","q1":"S","do1":"S","qm1":"S"}
+PIECES = {"V":1,"S":1,"G":4,"q1":2,"do1":1,"qm0":4,"k1":1,"v1":4,"qm1":4,"do0":1}
+RING = {"k0":0,"q0":1,"k1":0,"v0":3,"do0":4,"qm0":3,"ds0":5,"q1":1,"v1":5,"do1":3,"qm1":5,"ds1":0}
+CODES = {"k0":0,"q0":1,"v0":2,"do0":3,"qm0":4,"ds0":5,"k1":2,"q1":8,"v1":4,"do1":5,"qm1":1,"ds1":6}
 
 
 def tile_attend_gat_tnh_k_kernel(tc, qT, kT, vT, doT, rw, qm, offs, out):
@@ -37,12 +37,12 @@ def tile_attend_gat_tnh_k_kernel(tc, qT, kT, vT, doT, rw, qm, offs, out):
 
         def load_plane(pool_ap, label, j):
             rows = pool_ap.rearrange("(p j) t -> p j t", j=PACK)
-            plane = work.tile([P, T], F32, name="%s%d" % (label, j), tag="raw", bufs=8)
+            plane = work.tile([P, T], F32, name="%s%d" % (label, j), tag="raw", bufs=8, align_bytes=64)
             nc.sync.dma_start(out=plane[:], in_=rows[:, j, :])
             return plane[:]
 
         def load_rows(src, label):
-            tile = work.tile([P, PACK, N], F32, name=label, tag="raw", bufs=8)
+            tile = work.tile([P, PACK, N], F32, name=label, tag="raw", bufs=8, align_bytes=64)
             nc.sync.dma_start(out=tile[:], in_=src.rearrange("(p j) w -> p j w", j=PACK))
             return tile
 
@@ -104,6 +104,17 @@ def tile_attend_gat_tnh_k_kernel(tc, qT, kT, vT, doT, rw, qm, offs, out):
                 else:
                     nc.gpsimd.tensor_scalar(oo, ii, 1.0, 0.0, ALU.mult, ALU.add)
 
+        def half_rows(label, h, dst):
+            src = raw[label][:, :, h * N // 2 : (h + 1) * N // 2]
+            nc.scalar.copy(
+                dst.rearrange("p (c i j) -> p c j i", i=PACK, j=PACK), src.rearrange("p j (c i) -> p c j i", i=PACK)
+            )
+            cols = slice(h * N // 2, (h + 1) * N // 2)
+            nc.vector.quantize_mx(
+                out=code_tiles[CODES[label]][:, cols].bitcast(E4M3), scales=scale_tiles[CODES[label]][:, cols], in_=dst
+            )
+            fmts[label] = E4M3
+
         def quantize(label, fmt):
             nc.vector.quantize_mx(
                 out=code_tiles[CODES[label]][:].bitcast(fmt), scales=scale_tiles[CODES[label]][:], in_=ring[RING[label]]
@@ -132,6 +143,8 @@ def tile_attend_gat_tnh_k_kernel(tc, qT, kT, vT, doT, rw, qm, offs, out):
             for h in range(2):
                 half = sq[:, h * 2 * N : (h + 1) * 2 * N]
                 nc.scalar.activation(half, half, ACT.Square)
+                if b == 1 and h == 0:
+                    nc.gpsimd.tensor_scalar(half, half, 1.0, -1.0, ALU.mult, ALU.add)
             return sq
 
         def score_grad(b, sq, bk, g):
@@ -143,6 +156,15 @@ def tile_attend_gat_tnh_k_kernel(tc, qT, kT, vT, doT, rw, qm, offs, out):
                 lo, hi = h * N // 2, (h + 1) * N // 2
                 for t in range(PACK):
                     nc.scalar.activation(g[h][:, t, :], bk[t][:, lo:hi], ACT.Copy, scale=neg_gate[:, b, t : t + 1])
+                if b == 1 and h == 0:
+                    for c in range(lo, hi, 128):
+                        nc.gpsimd.tensor_tensor(
+                            ds[:, c * PACK : (c + 128) * PACK].rearrange("p (n t) -> p n t", t=PACK),
+                            sq[:, c * PACK : (c + 128) * PACK].rearrange("p (n t) -> p n t", t=PACK),
+                            g[h][:, :, c - lo : c - lo + 128].rearrange("p t n -> p n t"),
+                            ALU.mult,
+                        )
+                    continue
                 nc.vector.scalar_tensor_tensor(
                     ds[:, lo * PACK : hi * PACK].rearrange("p (n t) -> p n t", t=PACK),
                     sq[:, lo * PACK : hi * PACK].rearrange("p (n t) -> p n t", t=PACK),
@@ -184,8 +206,8 @@ def tile_attend_gat_tnh_k_kernel(tc, qT, kT, vT, doT, rw, qm, offs, out):
         interleave("do0", raw["do0"][:], True)
         quantize("do0", E5M2)
         score_grad(0, sq0, banks[4:8], [raw["q0"][:, 0:2, :], wide[:, 4:6, :]])
-        interleave("qm0", raw["qm0"][:], False)
-        quantize("qm0", E4M3)
+        half_rows("qm0", 0, ring[RING["qm0"]][:, 0 : 2 * N])
+        half_rows("qm0", 1, sq0[:, 0:N].bitcast(BF16))
         key_grad(0, banks[0:4])
         gather_v(2, 1)
         interleave("k1", kg[:, :, N : 2 * N], False)
@@ -194,19 +216,19 @@ def tile_attend_gat_tnh_k_kernel(tc, qT, kT, vT, doT, rw, qm, offs, out):
         quantize("q1", E4M3)
         gather_v(3, 1)
         place(0, 0, banks[0], kg[:, 0, 0:N])
-        interleave("v1", vg[1][:], False)
-        quantize("v1", E4M3)
         interleave("do1", raw["do1"][:], True)
         quantize("do1", E5M2)
-        place(0, 1, banks[1], raw["q1"][:, 0, :])
-        place(0, 2, banks[2], wide[:, 2, :])
+        interleave("v1", vg[1][:], False)
+        quantize("v1", E4M3)
+        place(0, 1, banks[1], raw["do1"][:, 0, :])
+        place(0, 2, banks[2], raw["do1"][:, 1, :])
         sq1 = squares(1, banks[4:8])
         score_grad(1, sq1, banks[4:8], [raw["qm0"][:, 0:2, :], raw["qm0"][:, 2:4, :]])
         interleave("qm1", raw["qm1"][:], False)
         quantize("qm1", E4M3)
         last = [banks[0], banks[1], banks[4], banks[5]]
         key_grad(1, last)
-        place(0, 3, banks[3], sq1[:, 2 * N : 3 * N])
+        place(0, 3, banks[3], raw["qm1"][:, 1, :])
         for j in range(D // P):
             place(1, j, last[j], vg[0][:, j, :])
             nc.sync.dma_start(out=out[j * P : (j + 1) * P, :], in_=placed[j][:])

@@ -18,11 +18,7 @@ ALU = mybir.AluOpType
 P = 128
 PACK = 4
 COLS = N // 16
-
-ENG = {"k0":"S","q0":"V","v0":"V","do0":"S","qm0":"S","k1":"G","v1":"G","q1":"S","do1":"S","qm1":"S"}
-PIECES = {"V":1,"S":1,"G":4,"q1":2,"do1":1,"qm0":4,"k1":1,"v1":4,"qm1":4,"do0":1}
-RING = {"k0":0,"q0":1,"k1":0,"v0":3,"do0":4,"qm0":3,"ds0":5,"q1":1,"v1":5,"do1":3,"qm1":5,"ds1":0}
-CODES = {"k0":0,"q0":1,"v0":2,"do0":3,"qm0":4,"ds0":5,"k1":2,"q1":8,"v1":4,"do1":5,"qm1":1,"ds1":6}
+RAW_BUFS = 10
 
 
 def tile_attend_gat_tnh_k_kernel(tc, qT, kT, vT, doT, rw, qm, offs, out):
@@ -37,198 +33,229 @@ def tile_attend_gat_tnh_k_kernel(tc, qT, kT, vT, doT, rw, qm, offs, out):
 
         def load_plane(pool_ap, label, j):
             rows = pool_ap.rearrange("(p j) t -> p j t", j=PACK)
-            plane = work.tile([P, T], F32, name="%s%d" % (label, j), tag="raw", bufs=8, align_bytes=64)
+            plane = work.tile([P, T], F32, name="%s%d" % (label, j), tag="raw", bufs=RAW_BUFS, align_bytes=64)
             nc.sync.dma_start(out=plane[:], in_=rows[:, j, :])
             return plane[:]
 
         def load_rows(src, label):
-            tile = work.tile([P, PACK, N], F32, name=label, tag="raw", bufs=8, align_bytes=64)
+            tile = work.tile([P, PACK, N], F32, name=label, tag="raw", bufs=RAW_BUFS, align_bytes=64)
             nc.sync.dma_start(out=tile[:], in_=src.rearrange("(p j) w -> p j w", j=PACK))
-            return tile
+            return tile[:]
 
-        k_planes = [load_plane(kT, "kp", j) for j in range(PACK)]
-        raw = {"q0": load_rows(qT[0], "q0")}
-        gate = keep.tile([P, B, PACK], F32, name="gate")
-        nc.sync.dma_start(out=gate[:], in_=rw.rearrange("b (p t) o -> p b (t o)", t=PACK))
-        v_planes = [load_plane(vT, "vp", j) for j in range(2)]
-        v_pair = keep.tile([P, 2, T], F32, name="v_pair")
-        nc.sync.dma_start(out=v_pair[:], in_=vT.rearrange("(p j) t -> p j t", j=PACK)[:, 2:4, :])
-        v_planes += [v_pair[:, 0, :], v_pair[:, 1, :]]
-        wide = keep.tile([P, 6, N], F32, name="wide")
-        nc.sync.dma_start(out=wide[:, 2:6, :], in_=doT[0].rearrange("(p j) w -> p j w", j=PACK))
-        raw["do0"] = wide[:, 2:6, :]
-        for label, src in (("qm0", qm[0]), ("q1", qT[1]), ("do1", doT[1]), ("qm1", qm[1])):
-            raw[label] = load_rows(src, label)
+        def staging(name):
+            return keep.tile([P, PACK * N], BF16, name=name, align_bytes=64)[:]
 
-        placed = []
-        for j in range(D // P):
-            tile = keep.tile([P, T], F32, name="placed%d" % j)
-            nc.gpsimd.memset(tile[:], 0.0)
-            placed.append(tile)
-        neg_gate = keep.tile([P, B, PACK], F32, name="neg_gate")
-        nc.gpsimd.tensor_scalar(neg_gate[:], gate[:], -1.0, 0.0, ALU.mult, ALU.add)
+        def operand(name):
+            codes = keep.tile([P, N], U32, name=name + "_c", align_bytes=64)
+            scales = keep.tile([P, N], U8, name=name + "_s", align_bytes=64)
+            return codes, scales
 
-        def gather(dst, planes, j, seqs):
-            lo, hi = seqs[0], seqs[-1] + 1
-            nc.vector.tensor_copy(
-                dst[:, j, lo * N : hi * N], planes[j].indirect(offsets[:, lo * COLS : hi * COLS])
-            )
+        def gather(dst, plane, lo, hi):
+            nc.vector.tensor_copy(dst, plane.indirect(offsets[:, lo * COLS : hi * COLS]))
 
-        ring = [keep.tile([P, PACK * N], BF16, name="ring%d" % i, align_bytes=64)[:] for i in range(6)]
-        sq_tiles = [keep.tile([P, N * PACK], F32, name="sq%d" % b, align_bytes=64) for b in range(B)]
-        ring += [sq_tiles[0][:, 0 : 2 * N].bitcast(BF16), sq_tiles[0][:, 2 * N : 4 * N].bitcast(BF16)]
-        code_tiles = [keep.tile([P, N], U32, name="codes%d" % i, align_bytes=64) for i in range(max(CODES.values()) + 1)]
-        scale_tiles = [keep.tile([P, N], U8, name="scales%d" % i, align_bytes=64) for i in range(max(CODES.values()) + 1)]
-        banks = [psum.tile([P, N], F32, name="bank%d" % i) for i in range(8)]
-        fmts = {}
-
-        def interleave(label, src, turned):
-            dst = ring[RING[label]]
-            if turned:
-                o = dst.rearrange("p (t m j) -> p m j t", t=PACK, j=PACK)
-                i = src.rearrange("p j (m t) -> p m j t", t=PACK)
+        def move(eng, o, i):
+            if eng == "V":
+                nc.vector.tensor_copy(o, i)
+            elif eng == "S":
+                nc.scalar.copy(o, i)
             else:
-                o = dst.rearrange("p (c i j) -> p c j i", i=PACK, j=PACK)
-                i = src.rearrange("p j (c i) -> p c j i", i=PACK)
-            eng = ENG[label]
-            if eng == "G":
-                o = dst.rearrange("p (c i j) -> p c i j", i=PACK, j=PACK)
-                i = src.rearrange("p j (c i) -> p c i j", i=PACK)
-            step = P // PIECES.get(label, PIECES[eng])
+                nc.gpsimd.tensor_scalar(o, i, 1.0, 0.0, ALU.mult, ALU.add)
+
+        def group(eng, dst, src, lo=0, hi=N, pieces=1):
+            order = "p c i j" if eng == "G" else "p c j i"
+            o = dst.rearrange("p (c i j) -> " + order, i=PACK, j=PACK)
+            i = src.rearrange("p j (c i) -> " + order, i=PACK)
+            step = (hi - lo) // PACK // pieces
+            for c in range(lo // PACK, hi // PACK, step):
+                move(eng, o[:, c : c + step], i[:, c : c + step])
+
+        def deal(eng, dst, src, pieces=1):
+            o = dst.rearrange("p (t m j) -> p m j t", t=PACK, j=PACK)
+            i = src.rearrange("p j (m t) -> p m j t", t=PACK)
+            step = P // pieces
             for c in range(0, P, step):
-                oo, ii = o[:, c : c + step], i[:, c : c + step]
-                if eng == "V":
-                    nc.vector.tensor_copy(oo, ii)
-                elif eng == "S":
-                    nc.scalar.copy(oo, ii)
-                else:
-                    nc.gpsimd.tensor_scalar(oo, ii, 1.0, 0.0, ALU.mult, ALU.add)
+                move(eng, o[:, c : c + step], i[:, c : c + step])
 
-        def half_rows(label, h, dst):
-            src = raw[label][:, :, h * N // 2 : (h + 1) * N // 2]
-            nc.scalar.copy(
-                dst.rearrange("p (c i j) -> p c j i", i=PACK, j=PACK), src.rearrange("p j (c i) -> p c j i", i=PACK)
-            )
-            cols = slice(h * N // 2, (h + 1) * N // 2)
+        def deal_t(eng, dst, src, t0, t1):
+            o = dst.rearrange("p (t m j) -> p t m j", t=PACK, j=PACK)[:, t0:t1]
+            i = src.rearrange("p j (m t) -> p t m j", t=PACK)[:, t0:t1]
+            move(eng, o, i)
+
+        def quantize(op, fmt, src, lo=0, hi=N):
             nc.vector.quantize_mx(
-                out=code_tiles[CODES[label]][:, cols].bitcast(E4M3), scales=scale_tiles[CODES[label]][:, cols], in_=dst
+                out=op[0][:, lo:hi].bitcast(fmt), scales=op[1][:, lo:hi], in_=src[:, lo * PACK : hi * PACK]
             )
-            fmts[label] = E4M3
 
-        def quantize(label, fmt):
-            nc.vector.quantize_mx(
-                out=code_tiles[CODES[label]][:].bitcast(fmt), scales=scale_tiles[CODES[label]][:], in_=ring[RING[label]]
-            )
-            fmts[label] = fmt
-
-        def product(dst, left, t, right, lo, hi):
-            lc, ls = code_tiles[CODES[left]], scale_tiles[CODES[left]]
-            rc, rs = code_tiles[CODES[right]], scale_tiles[CODES[right]]
+        def product(dst, left, lfmt, t, right, rfmt, lo=0, hi=N):
             cols = slice(t * P, (t + 1) * P)
             nc.tensor.matmul_mx(
-                out=dst, lhsT=lc[:, cols].bitcast(fmts[left]), lhsT_scale=ls[:, cols],
-                rhs=rc[:, lo:hi].bitcast(fmts[right]), rhs_scale=rs[:, lo:hi], start=True, stop=True,
+                out=dst, lhsT=left[0][:, cols].bitcast(lfmt), lhsT_scale=left[1][:, cols],
+                rhs=right[0][:, lo:hi].bitcast(rfmt), rhs_scale=right[1][:, lo:hi], start=True, stop=True,
             )
 
-        def squares(b, bk):
-            sq = sq_tiles[b]
+        def tanh_scores(sq, bk, q_op, k_op):
             for c in range(N // P):
                 for t in range(PACK):
-                    product(bk[c][:, t * P : (t + 1) * P], "q%d" % b, t, "k%d" % b, c * P, (c + 1) * P)
+                    product(bk[c][:, t * P : (t + 1) * P], q_op, E4M3, t, k_op, E4M3, c * P, (c + 1) * P)
                 nc.scalar.activation(
                     sq[:, c * N : (c + 1) * N].rearrange("p (n t) -> p n t", t=PACK),
                     bk[c][:].rearrange("p (t n) -> p n t", t=PACK),
                     ACT.Tanh,
                 )
-            for h in range(2):
-                half = sq[:, h * 2 * N : (h + 1) * 2 * N]
-                nc.scalar.activation(half, half, ACT.Square)
-                if b == 1 and h == 0:
-                    nc.gpsimd.tensor_scalar(half, half, 1.0, -1.0, ALU.mult, ALU.add)
-            return sq
 
-        def score_grad(b, sq, bk, g):
+        def square(sq, h):
+            half = sq[:, h * 2 * N : (h + 1) * 2 * N]
+            nc.scalar.activation(half, half, ACT.Square)
+
+        def less_one(sq, h):
+            half = sq[:, h * 2 * N : (h + 1) * 2 * N]
+            nc.gpsimd.tensor_scalar(half, half, 1.0, -1.0, ALU.mult, ALU.add)
+
+        def dp_products(bk, do_op, v_op, ts=range(PACK)):
+            for t in ts:
+                product(bk[t][:], do_op, E5M2, t, v_op, E4M3)
+
+        def gated(g, bk, b, h):
             for t in range(PACK):
-                product(bk[t][:], "do%d" % b, t, "v%d" % b, 0, N)
-            ds = ring[RING["ds%d" % b]]
-            g = [x.rearrange("p a b -> p (a b)").rearrange("p (t n) -> p t n", t=PACK) for x in g]
-            for h in range(2):
-                lo, hi = h * N // 2, (h + 1) * N // 2
-                for t in range(PACK):
-                    nc.scalar.activation(g[h][:, t, :], bk[t][:, lo:hi], ACT.Copy, scale=neg_gate[:, b, t : t + 1])
-                if b == 1 and h == 0:
-                    for c in range(lo, hi, 128):
-                        nc.gpsimd.tensor_tensor(
-                            ds[:, c * PACK : (c + 128) * PACK].rearrange("p (n t) -> p n t", t=PACK),
-                            sq[:, c * PACK : (c + 128) * PACK].rearrange("p (n t) -> p n t", t=PACK),
-                            g[h][:, :, c - lo : c - lo + 128].rearrange("p t n -> p n t"),
-                            ALU.mult,
-                        )
-                    continue
-                nc.vector.scalar_tensor_tensor(
-                    ds[:, lo * PACK : hi * PACK].rearrange("p (n t) -> p n t", t=PACK),
-                    sq[:, lo * PACK : hi * PACK].rearrange("p (n t) -> p n t", t=PACK),
-                    1.0,
-                    g[h].rearrange("p t n -> p n t"),
-                    ALU.subtract,
+                nc.scalar.activation(
+                    g[:, t, :], bk[t][:, h * N // 2 : (h + 1) * N // 2], ACT.Copy, scale=neg_gate[:, b, t : t + 1]
+                )
+
+        def ds_vector(ds, sq, g, h):
+            cols = slice(h * 2 * N, (h + 1) * 2 * N)
+            nc.vector.scalar_tensor_tensor(
+                ds[:, cols].rearrange("p (n t) -> p n t", t=PACK),
+                sq[:, cols].rearrange("p (n t) -> p n t", t=PACK),
+                1.0,
+                g.rearrange("p t n -> p n t"),
+                ALU.subtract,
+                ALU.mult,
+            )
+
+        def ds_gpsimd(ds, sq, g, h):
+            for c in range(2):
+                cols = slice(h * 2 * N + c * N, h * 2 * N + (c + 1) * N)
+                nc.gpsimd.tensor_tensor(
+                    ds[:, cols].rearrange("p (n t) -> p n t", t=PACK),
+                    sq[:, cols].rearrange("p (n t) -> p n t", t=PACK),
+                    g[:, :, c * P : (c + 1) * P].rearrange("p t n -> p n t"),
                     ALU.mult,
                 )
-            quantize("ds%d" % b, E5M2)
 
-        def key_grad(b, bk):
-            for j in range(D // P):
-                product(bk[j][:], "qm%d" % b, j, "ds%d" % b, 0, N)
+        def halves(x):
+            flat = x.rearrange("p a b -> p (a b)")
+            return [flat[:, h * 2 * N : (h + 1) * 2 * N].rearrange("p (t n) -> p t n", t=PACK) for h in range(2)]
+
+        def key_grad(bank, qm_op, j, ds_op):
+            product(bank[:], qm_op, E4M3, j, ds_op, E5M2)
 
         def place(b, j, bank, st):
             nc.scalar.copy(st, bank[:])
             nc.vector.tensor_copy(placed[j][:].indirect(offsets[:, b * COLS : (b + 1) * COLS]), st)
 
+        kp = [load_plane(kT, "kp", j) for j in range(PACK)]
+        q0 = load_rows(qT[0], "q0")
+        vp = [load_plane(vT, "vp", 0)]
+        gate = keep.tile([P, B, PACK], F32, name="gate")
+        nc.sync.dma_start(out=gate[:], in_=rw.rearrange("b (p t) o -> p b (t o)", t=PACK))
+        q1 = load_rows(qT[1], "q1")
+        vp += [load_plane(vT, "vp", j) for j in range(1, PACK)]
+        do0 = load_rows(doT[0], "do0")
+        qm0 = load_rows(qm[0], "qm0")
+        do1 = load_rows(doT[1], "do1")
+        qm1 = load_rows(qm[1], "qm1")
+        placed = []
+        for j in range(D // P):
+            tile = keep.tile([P, T], F32, name="placed%d" % j)
+            nc.gpsimd.memset(tile[:], 0.0)
+            placed.append(tile)
         kg = keep.tile([P, PACK, B * N], F32, name="kg")
-        vg = [keep.tile([P, PACK, N], F32, name="vg0"), wide[:, 0:PACK, :]]
-
-        def gather_v(j, b):
-            nc.vector.tensor_copy(vg[b][:, j, :], v_planes[j].indirect(offsets[:, b * COLS : (b + 1) * COLS]))
-
+        vg = [keep.tile([P, PACK, N], F32, name="vg%d" % b) for b in range(B)]
+        sq = [keep.tile([P, N * PACK], F32, name="sq%d" % b, align_bytes=64)[:] for b in range(B)]
+        st = [staging("st%d" % i) for i in range(8)]
+        ops = {x: operand(x) for x in ("k0", "k1", "q0", "q1", "v0", "v1", "do0", "do1", "qm0", "qm1", "ds0", "ds1")}
+        banks = [psum.tile([P, N], F32, name="bank%d" % i) for i in range(8)]
+        neg_gate = keep.tile([P, B, PACK], F32, name="neg_gate")
+        nc.gpsimd.tensor_scalar(neg_gate[:], gate[:], -1.0, 0.0, ALU.mult, ALU.add)
+        H = N // 2
 
         for j in range(PACK - 1):
-            gather(kg, k_planes, j, [0, 1])
-        gather(kg, k_planes, 3, [0])
-        interleave("k0", kg[:, :, 0:N], False)
-        gather(kg, k_planes, 3, [1])
-        interleave("q0", raw["q0"][:], True)
-        quantize("q0", E4M3)
-        quantize("k0", E4M3)
-        sq0 = squares(0, banks[0:4])
-        for j, b in ((0, 0), (0, 1), (1, 0), (1, 1), (2, 0), (3, 0)):
-            gather_v(j, b)
-        interleave("v0", vg[0][:], False)
-        quantize("v0", E4M3)
-        interleave("do0", raw["do0"][:], True)
-        quantize("do0", E5M2)
-        score_grad(0, sq0, banks[4:8], [raw["q0"][:, 0:2, :], wide[:, 4:6, :]])
-        half_rows("qm0", 0, ring[RING["qm0"]][:, 0 : 2 * N])
-        half_rows("qm0", 1, sq0[:, 0:N].bitcast(BF16))
-        key_grad(0, banks[0:4])
-        gather_v(2, 1)
-        interleave("k1", kg[:, :, N : 2 * N], False)
-        quantize("k1", E4M3)
-        interleave("q1", raw["q1"][:], True)
-        quantize("q1", E4M3)
-        gather_v(3, 1)
+            gather(kg[:, j, :], kp[j], 0, 2)
+        gather(kg[:, 3, 0:N], kp[3], 0, 1)
+        gather(kg[:, 3, N : 2 * N], kp[3], 1, 2)
+        group("S", st[0], kg[:, :, 0:N])
+        group("S", st[2], kg[:, :, N : 2 * N])
+        deal("V", st[1], q0)
+        quantize(ops["k0"], E4M3, st[0])
+        quantize(ops["q0"], E4M3, st[1])
+        quantize(ops["k1"], E4M3, st[2])
+        gather(vg[0][:, 0, :], vp[0], 0, 1)
+        gather(vg[1][:, 0, :], vp[0], 1, 2)
+        for h in range(2):
+            half = st[2][:, 0 : 2 * N]
+            move("G", half.rearrange("p (t m j) -> p t m j", t=2, j=PACK), q1.rearrange("p j (m t) -> p t m j", t=PACK)[:, 2 * h : 2 * h + 2])
+            nc.vector.quantize_mx(out=ops["q1"][0][:, h * H : (h + 1) * H].bitcast(E4M3), scales=ops["q1"][1][:, h * H : (h + 1) * H], in_=half)
+        for t in range(PACK):
+            product(banks[t][:], ops["q0"], E4M3, t, ops["k0"], E4M3)
+            nc.scalar.activation(sq[0][:, t * N : (t + 1) * N], banks[t][:], ACT.Tanh)
+        for t in range(PACK):
+            row = sq[0][:, t * N : (t + 1) * N]
+            nc.scalar.activation(row, row, ACT.Square)
+            nc.scalar.activation(row, row, ACT.Identity, bias=gate[:, 0, t : t + 1], scale=neg_gate[:, 0, t : t + 1])
+        for j in range(1, PACK):
+            gather(vg[0][:, j, :], vp[j], 0, 1)
+            gather(vg[1][:, j, :], vp[j], 1, 2)
+        group("S", st[3], vg[0][:], 0, H)
+        group("G", st[3], vg[0][:], H, N)
+        deal_t("V", st[4], do0, 0, 2)
+        deal_t("S", st[4], do0, 2, 4)
+        quantize(ops["v0"], E4M3, st[3])
+        quantize(ops["do0"], E5M2, st[4], 0, H)
+        quantize(ops["do0"], E5M2, st[4], H, N)
+        dp_products(banks[0:4], ops["do0"], ops["v0"])
+        group("G", st[4], vg[1][:])
+        for t in range(PACK):
+            nc.vector.tensor_tensor(st[0][:, t * N : (t + 1) * N], banks[t][:], sq[0][:, t * N : (t + 1) * N], ALU.mult)
+        group("V", st[5], st[0].rearrange("p (j n) -> p j n", j=PACK))
+        quantize(ops["ds0"], E5M2, st[5])
+        tanh_scores(sq[1], banks[4:8], ops["q1"], ops["k1"])
+        group("S", st[2], qm0, 0, N, 2)
+        quantize(ops["qm0"], E4M3, st[2], 0, H)
+        quantize(ops["qm0"], E4M3, st[2], H, N)
+        for j in range(4):
+            key_grad(banks[j], ops["qm0"], j, ops["ds0"])
+        quantize(ops["v1"], E4M3, st[4])
         place(0, 0, banks[0], kg[:, 0, 0:N])
-        interleave("do1", raw["do1"][:], True)
-        quantize("do1", E5M2)
-        interleave("v1", vg[1][:], False)
-        quantize("v1", E4M3)
-        place(0, 1, banks[1], raw["do1"][:, 0, :])
-        place(0, 2, banks[2], raw["do1"][:, 1, :])
-        sq1 = squares(1, banks[4:8])
-        score_grad(1, sq1, banks[4:8], [raw["qm0"][:, 0:2, :], raw["qm0"][:, 2:4, :]])
-        interleave("qm1", raw["qm1"][:], False)
-        quantize("qm1", E4M3)
-        last = [banks[0], banks[1], banks[4], banks[5]]
-        key_grad(1, last)
-        place(0, 3, banks[3], raw["qm1"][:, 1, :])
+        deal("S", st[3], do1, 4)
+        quantize(ops["do1"], E5M2, st[3])
+        dp_products(banks[4:8], ops["do1"], ops["v1"])
+        lo = [st[3].bitcast(F32), sq[1][:, 2 * N : 4 * N]]
+        for c in range(2):
+            part = sq[1][:, c * N : (c + 1) * N]
+            nc.scalar.activation(part, part, ACT.Square)
+        nc.gpsimd.tensor_scalar(lo[0], sq[1][:, 0 : 2 * N], 1.0, -1.0, ALU.mult, ALU.add)
+        for c in range(2, 4):
+            part = sq[1][:, c * N : (c + 1) * N]
+            nc.scalar.activation(part, part, ACT.Square)
+        less_one(sq[1], 1)
+        place(0, 1, banks[1], kg[:, 1, 0:N])
+        g1 = halves(do0)
+        for h in range(2):
+            gated(g1[h], banks[4:8], 1, h)
+            for c in range(2):
+                nc.gpsimd.tensor_tensor(
+                    st[7][:, h * 2 * N + c * N : h * 2 * N + (c + 1) * N].rearrange("p (n t) -> p n t", t=PACK),
+                    lo[h][:, c * N : (c + 1) * N].rearrange("p (n t) -> p n t", t=PACK),
+                    g1[h][:, :, c * P : (c + 1) * P].rearrange("p t n -> p n t"),
+                    ALU.mult,
+                )
+        place(0, 2, banks[2], kg[:, 2, 0:N])
+        group("S", st[6], qm1)
+        quantize(ops["qm1"], E4M3, st[6])
+        quantize(ops["ds1"], E5M2, st[7])
         for j in range(D // P):
-            place(1, j, last[j], vg[0][:, j, :])
+            key_grad(banks[4 + j], ops["qm1"], j, ops["ds1"])
+        place(0, 3, banks[3], sq[1][:, 3 * N : 4 * N])
+        for j in range(D // P):
+            place(1, j, banks[4 + j], vg[0][:, j, :])
             nc.sync.dma_start(out=out[j * P : (j + 1) * P, :], in_=placed[j][:])

@@ -18,7 +18,7 @@ ALU = mybir.AluOpType
 P = 128
 PACK = 4
 COLS = N // 16
-RAW_BUFS = 10
+RAW_BUFS = 8
 
 
 def tile_attend_gat_tnh_k_kernel(tc, qT, kT, vT, doT, rw, qm, offs, out):
@@ -155,12 +155,14 @@ def tile_attend_gat_tnh_k_kernel(tc, qT, kT, vT, doT, rw, qm, offs, out):
 
         kp = [load_plane(kT, "kp", j) for j in range(PACK)]
         q0 = load_rows(qT[0], "q0")
-        vp = [load_plane(vT, "vp", 0)]
         gate = keep.tile([P, B, PACK], F32, name="gate")
         nc.sync.dma_start(out=gate[:], in_=rw.rearrange("b (p t) o -> p b (t o)", t=PACK))
-        q1 = load_rows(qT[1], "q1")
-        vp += [load_plane(vT, "vp", j) for j in range(1, PACK)]
+        vp = [load_plane(vT, "vp", j) for j in range(2)]
+        v_last = keep.tile([P, 2 * T], F32, name="v_last")
+        for j in range(2):
+            nc.sync.dma_start(out=v_last[:, j * T : (j + 1) * T], in_=vT.rearrange("(p j) t -> p j t", j=PACK)[:, 2 + j, :])
         do0 = load_rows(doT[0], "do0")
+        q1 = load_rows(qT[1], "q1")
         qm0 = load_rows(qm[0], "qm0")
         do1 = load_rows(doT[1], "do1")
         qm1 = load_rows(qm[1], "qm1")
@@ -170,92 +172,109 @@ def tile_attend_gat_tnh_k_kernel(tc, qT, kT, vT, doT, rw, qm, offs, out):
             nc.gpsimd.memset(tile[:], 0.0)
             placed.append(tile)
         kg = keep.tile([P, PACK, B * N], F32, name="kg")
-        vg = [keep.tile([P, PACK, N], F32, name="vg%d" % b) for b in range(B)]
+        shared = keep.tile([P, 5 * N], F32, name="shared", align_bytes=64)
+        vg = [keep.tile([P, PACK, N], F32, name="vg0")[:], shared[:, 0 : 4 * N].rearrange("p (j n) -> p j n", j=PACK)]
         sq = [keep.tile([P, N * PACK], F32, name="sq%d" % b, align_bytes=64)[:] for b in range(B)]
-        st = [staging("st%d" % i) for i in range(8)]
+        st = [staging("st%d" % i) for i in range(7)]
+        st += [shared[:, 3 * N : 5 * N].bitcast(BF16)]
         ops = {x: operand(x) for x in ("k0", "k1", "q0", "q1", "v0", "v1", "do0", "do1", "qm0", "qm1", "ds0", "ds1")}
         banks = [psum.tile([P, N], F32, name="bank%d" % i) for i in range(8)]
         neg_gate = keep.tile([P, B, PACK], F32, name="neg_gate")
         nc.gpsimd.tensor_scalar(neg_gate[:], gate[:], -1.0, 0.0, ALU.mult, ALU.add)
         H = N // 2
 
+        def deal_half(eng, dst, src, h):
+            o = dst.rearrange("p (t m j) -> p m j t", t=PACK, j=PACK)
+            i = src.rearrange("p j (m t) -> p m j t", t=PACK)
+            move(eng, o[:, h * P // 2 : (h + 1) * P // 2], i[:, h * P // 2 : (h + 1) * P // 2])
+
         for j in range(PACK - 1):
             gather(kg[:, j, :], kp[j], 0, 2)
         gather(kg[:, 3, 0:N], kp[3], 0, 1)
         gather(kg[:, 3, N : 2 * N], kp[3], 1, 2)
         group("S", st[0], kg[:, :, 0:N])
-        group("S", st[2], kg[:, :, N : 2 * N])
         deal("V", st[1], q0)
         quantize(ops["k0"], E4M3, st[0])
         quantize(ops["q0"], E4M3, st[1])
+        group("S", st[2], kg[:, :, N : 2 * N])
         quantize(ops["k1"], E4M3, st[2])
-        gather(vg[0][:, 0, :], vp[0], 0, 1)
-        gather(vg[1][:, 0, :], vp[0], 1, 2)
-        for h in range(2):
-            half = st[2][:, 0 : 2 * N]
-            move("G", half.rearrange("p (t m j) -> p t m j", t=2, j=PACK), q1.rearrange("p j (m t) -> p t m j", t=PACK)[:, 2 * h : 2 * h + 2])
-            nc.vector.quantize_mx(out=ops["q1"][0][:, h * H : (h + 1) * H].bitcast(E4M3), scales=ops["q1"][1][:, h * H : (h + 1) * H], in_=half)
         for t in range(PACK):
             product(banks[t][:], ops["q0"], E4M3, t, ops["k0"], E4M3)
             nc.scalar.activation(sq[0][:, t * N : (t + 1) * N], banks[t][:], ACT.Tanh)
+        square(sq[0], 0)
+        square(sq[0], 1)
         for t in range(PACK):
             row = sq[0][:, t * N : (t + 1) * N]
-            nc.scalar.activation(row, row, ACT.Square)
             nc.scalar.activation(row, row, ACT.Identity, bias=gate[:, 0, t : t + 1], scale=neg_gate[:, 0, t : t + 1])
-        for j in range(1, PACK):
+        for j in range(2):
             gather(vg[0][:, j, :], vp[j], 0, 1)
             gather(vg[1][:, j, :], vp[j], 1, 2)
-        group("S", st[3], vg[0][:], 0, H)
-        group("G", st[3], vg[0][:], H, N)
-        deal_t("V", st[4], do0, 0, 2)
-        deal_t("S", st[4], do0, 2, 4)
+        gather(vg[0][:, 2, :], v_last[:, 0:T], 0, 1)
+        gather(vg[0][:, 3, :], v_last[:, T : 2 * T], 0, 1)
+        group("S", st[3], vg[0], 0, H)
+        group("V", st[3], vg[0], H, N)
+        gather(vg[1][:, 2, :], v_last[:], 1, 2)
+        deal_half("V", st[7], do0, 0)
+        deal_half("S", st[7], do0, 1)
         quantize(ops["v0"], E4M3, st[3])
-        quantize(ops["do0"], E5M2, st[4], 0, H)
-        quantize(ops["do0"], E5M2, st[4], H, N)
+        quantize(ops["do0"], E5M2, st[7])
         dp_products(banks[0:4], ops["do0"], ops["v0"])
-        group("G", st[4], vg[1][:])
+        gather(vg[1][:, 3, :], v_last[:, T : 2 * T], 1, 2)
         for t in range(PACK):
             nc.vector.tensor_tensor(st[0][:, t * N : (t + 1) * N], banks[t][:], sq[0][:, t * N : (t + 1) * N], ALU.mult)
         group("V", st[5], st[0].rearrange("p (j n) -> p j n", j=PACK))
         quantize(ops["ds0"], E5M2, st[5])
-        tanh_scores(sq[1], banks[4:8], ops["q1"], ops["k1"])
-        group("S", st[2], qm0, 0, N, 2)
+        deal("S", st[1], q1)
+        group("G", st[2], qm0, 0, H)
+        quantize(ops["q1"], E4M3, st[1], 0, H)
         quantize(ops["qm0"], E4M3, st[2], 0, H)
-        quantize(ops["qm0"], E4M3, st[2], H, N)
-        for j in range(4):
-            key_grad(banks[j], ops["qm0"], j, ops["ds0"])
-        quantize(ops["v1"], E4M3, st[4])
+        key_grad(banks[0], ops["qm0"], 0, ops["ds0"])
+        quantize(ops["q1"], E4M3, st[1], H, N)
+        group("S", st[4], vg[1])
         place(0, 0, banks[0], kg[:, 0, 0:N])
         deal("S", st[3], do1, 4)
+        quantize(ops["v1"], E4M3, st[4])
         quantize(ops["do1"], E5M2, st[3])
-        dp_products(banks[4:8], ops["do1"], ops["v1"])
-        lo = [st[3].bitcast(F32), sq[1][:, 2 * N : 4 * N]]
-        for c in range(2):
-            part = sq[1][:, c * N : (c + 1) * N]
-            nc.scalar.activation(part, part, ACT.Square)
-        nc.gpsimd.tensor_scalar(lo[0], sq[1][:, 0 : 2 * N], 1.0, -1.0, ALU.mult, ALU.add)
-        for c in range(2, 4):
-            part = sq[1][:, c * N : (c + 1) * N]
-            nc.scalar.activation(part, part, ACT.Square)
-        less_one(sq[1], 1)
-        place(0, 1, banks[1], kg[:, 1, 0:N])
+        group("G", st[3], qm0, H, N)
+        quantize(ops["qm0"], E4M3, st[3], H, N)
+        p1 = [sq[1][:, 0 : 2 * N], keep.tile([P, 2 * N], F32, name="p_late", align_bytes=64)[:]]
+        for c in range(N // P):
+            for t in range(PACK):
+                product(banks[4 + c][:, t * P : (t + 1) * P], ops["q1"], E4M3, t, ops["k1"], E4M3, c * P, (c + 1) * P)
+            nc.scalar.activation(
+                p1[c // 2][:, (c % 2) * N : (c % 2 + 1) * N].rearrange("p (n t) -> p n t", t=PACK),
+                banks[4 + c][:].rearrange("p (t n) -> p n t", t=PACK),
+                ACT.Tanh,
+            )
+        key_grad(banks[7], ops["qm0"], 1, ops["ds0"])
+        dp_products(banks[0:4], ops["do1"], ops["v1"])
+        square(sq[1], 0)
+        place(0, 1, banks[7], kg[:, 1, 0:N])
+        key_grad(banks[7], ops["qm0"], 2, ops["ds0"])
+        lo = st[3].bitcast(F32)
+        nc.gpsimd.tensor_scalar(lo, sq[1][:, 0 : 2 * N], 1.0, -1.0, ALU.mult, ALU.add)
         g1 = halves(do0)
-        for h in range(2):
-            gated(g1[h], banks[4:8], 1, h)
-            for c in range(2):
-                nc.gpsimd.tensor_tensor(
-                    st[7][:, h * 2 * N + c * N : h * 2 * N + (c + 1) * N].rearrange("p (n t) -> p n t", t=PACK),
-                    lo[h][:, c * N : (c + 1) * N].rearrange("p (n t) -> p n t", t=PACK),
-                    g1[h][:, :, c * P : (c + 1) * P].rearrange("p t n -> p n t"),
-                    ALU.mult,
-                )
-        place(0, 2, banks[2], kg[:, 2, 0:N])
-        group("S", st[6], qm1)
-        quantize(ops["qm1"], E4M3, st[6])
-        quantize(ops["ds1"], E5M2, st[7])
+        gated(g1[0], banks[0:4], 1, 0)
+        for c in range(2):
+            nc.gpsimd.tensor_tensor(
+                st[6][:, c * N : (c + 1) * N].rearrange("p (n t) -> p n t", t=PACK),
+                lo[:, c * N : (c + 1) * N].rearrange("p (n t) -> p n t", t=PACK),
+                g1[0][:, :, c * P : (c + 1) * P].rearrange("p t n -> p n t"),
+                ALU.mult,
+            )
+        nc.scalar.activation(sq[1][:, 2 * N : 4 * N], p1[1], ACT.Square)
+        place(0, 2, banks[7], kg[:, 1, N : 2 * N])
+        key_grad(banks[7], ops["qm0"], 3, ops["ds0"])
+        gated(g1[1], banks[0:4], 1, 1)
+        ds_vector(st[6], sq[1], g1[1], 1)
+        late = p1[1].bitcast(BF16)
+        group("S", late, qm1, 0, N, 2)
+        quantize(ops["qm1"], E4M3, late)
+        quantize(ops["ds1"], E5M2, st[6])
+        last = [banks[4], banks[5], banks[6], banks[0]]
         for j in range(D // P):
-            key_grad(banks[4 + j], ops["qm1"], j, ops["ds1"])
-        place(0, 3, banks[3], sq[1][:, 3 * N : 4 * N])
+            key_grad(last[j], ops["qm1"], j, ops["ds1"])
+        place(0, 3, banks[7], sq[1][:, 3 * N : 4 * N])
         for j in range(D // P):
-            place(1, j, banks[4 + j], vg[0][:, j, :])
+            place(1, j, last[j], vg[0][:, j, :])
             nc.sync.dma_start(out=out[j * P : (j + 1) * P, :], in_=placed[j][:])

@@ -156,7 +156,7 @@ def tile_attend_gat_tnh_k_kernel(tc, qT, kT, vT, doT, rw, qm, offs, out):
         kp = [load_plane(kT, "kp", j) for j in range(PACK)]
         q0 = load_rows(qT[0], "q0")
         gate = keep.tile([P, B, PACK], F32, name="gate")
-        nc.sync.dma_start(out=gate[:], in_=rw.rearrange("b (p t) o -> p b (t o)", t=PACK))
+        nc.scalar.dma_start(out=gate[:], in_=rw.rearrange("b (p t) o -> p b (t o)", t=PACK))
         vp = [load_plane(vT, "vp", j) for j in range(2)]
         v_last = keep.tile([P, 2 * T], F32, name="v_last")
         for j in range(2):
@@ -178,6 +178,7 @@ def tile_attend_gat_tnh_k_kernel(tc, qT, kT, vT, doT, rw, qm, offs, out):
         st = [staging("st%d" % i) for i in range(7)]
         st += [shared[:, 3 * N : 5 * N].bitcast(BF16)]
         ops = {x: operand(x) for x in ("k0", "k1", "q0", "q1", "v0", "v1", "do0", "do1", "qm0", "qm1", "ds0", "ds1")}
+        ops["k1"] = ops["k0"]
         banks = [psum.tile([P, N], F32, name="bank%d" % i) for i in range(8)]
         neg_gate = keep.tile([P, B, PACK], F32, name="neg_gate")
         nc.gpsimd.tensor_scalar(neg_gate[:], gate[:], -1.0, 0.0, ALU.mult, ALU.add)
@@ -197,10 +198,10 @@ def tile_attend_gat_tnh_k_kernel(tc, qT, kT, vT, doT, rw, qm, offs, out):
         quantize(ops["k0"], E4M3, st[0])
         quantize(ops["q0"], E4M3, st[1])
         group("S", st[2], kg[:, :, N : 2 * N])
-        quantize(ops["k1"], E4M3, st[2])
         for t in range(PACK):
             product(banks[t][:], ops["q0"], E4M3, t, ops["k0"], E4M3)
             nc.scalar.activation(sq[0][:, t * N : (t + 1) * N], banks[t][:], ACT.Tanh)
+        quantize(ops["k1"], E4M3, st[2])
         square(sq[0], 0)
         square(sq[0], 1)
         for t in range(PACK):
@@ -222,35 +223,37 @@ def tile_attend_gat_tnh_k_kernel(tc, qT, kT, vT, doT, rw, qm, offs, out):
         gather(vg[1][:, 3, :], v_last[:, T : 2 * T], 1, 2)
         for t in range(PACK):
             nc.vector.tensor_tensor(st[0][:, t * N : (t + 1) * N], banks[t][:], sq[0][:, t * N : (t + 1) * N], ALU.mult)
-        group("V", st[5], st[0].rearrange("p (j n) -> p j n", j=PACK))
+        nc.vector.tensor_copy(st[5].rearrange("p (n j) -> p n j", j=PACK), st[0].rearrange("p (j n) -> p n j", j=PACK))
         quantize(ops["ds0"], E5M2, st[5])
         deal("S", st[1], q1)
-        group("G", st[2], qm0, 0, H)
+        early = sq[0][:, 0 : 2 * N].bitcast(BF16)
+        group("G", early, qm0, 0, H)
         quantize(ops["q1"], E4M3, st[1], 0, H)
-        quantize(ops["qm0"], E4M3, st[2], 0, H)
+        quantize(ops["qm0"], E4M3, early, 0, H)
         key_grad(banks[0], ops["qm0"], 0, ops["ds0"])
         quantize(ops["q1"], E4M3, st[1], H, N)
         group("S", st[4], vg[1])
-        place(0, 0, banks[0], kg[:, 0, 0:N])
-        deal("S", st[3], do1, 4)
+        deal("S", st[3], do1)
+        place(0, 0, banks[0], do1[:, 0, :])
         quantize(ops["v1"], E4M3, st[4])
         quantize(ops["do1"], E5M2, st[3])
         group("G", st[3], qm0, H, N)
         quantize(ops["qm0"], E4M3, st[3], H, N)
-        p1 = [sq[1][:, 0 : 2 * N], keep.tile([P, 2 * N], F32, name="p_late", align_bytes=64)[:]]
+        p_late = keep.tile([P, 2 * N], F32, name="p_late", align_bytes=64)[:]
+        p1 = [do1[:, 1, :], do1[:, 2, :], do1[:, 3, :], p_late[:, 0:N]]
         for c in range(N // P):
             for t in range(PACK):
-                product(banks[4 + c][:, t * P : (t + 1) * P], ops["q1"], E4M3, t, ops["k1"], E4M3, c * P, (c + 1) * P)
+                product(banks[4 + c % 3][:, t * P : (t + 1) * P], ops["q1"], E4M3, t, ops["k1"], E4M3, c * P, (c + 1) * P)
             nc.scalar.activation(
-                p1[c // 2][:, (c % 2) * N : (c % 2 + 1) * N].rearrange("p (n t) -> p n t", t=PACK),
-                banks[4 + c][:].rearrange("p (t n) -> p n t", t=PACK),
+                p1[c].rearrange("p (n t) -> p n t", t=PACK),
+                banks[4 + c % 3][:].rearrange("p (t n) -> p n t", t=PACK),
                 ACT.Tanh,
             )
-        key_grad(banks[7], ops["qm0"], 1, ops["ds0"])
+        key_grad(banks[5], ops["qm0"], 1, ops["ds0"])
+        place(0, 1, banks[5], kg[:, 1, 0:N])
+        key_grad(banks[5], ops["qm0"], 2, ops["ds0"])
         dp_products(banks[0:4], ops["do1"], ops["v1"])
-        square(sq[1], 0)
-        place(0, 1, banks[7], kg[:, 1, 0:N])
-        key_grad(banks[7], ops["qm0"], 2, ops["ds0"])
+        nc.scalar.activation(sq[1][:, 0 : 2 * N].rearrange("p (a b) -> p a b", a=2), do1[:, 1:3, :], ACT.Square)
         lo = st[3].bitcast(F32)
         nc.gpsimd.tensor_scalar(lo, sq[1][:, 0 : 2 * N], 1.0, -1.0, ALU.mult, ALU.add)
         g1 = halves(do0)
@@ -262,19 +265,20 @@ def tile_attend_gat_tnh_k_kernel(tc, qT, kT, vT, doT, rw, qm, offs, out):
                 g1[0][:, :, c * P : (c + 1) * P].rearrange("p t n -> p n t"),
                 ALU.mult,
             )
-        nc.scalar.activation(sq[1][:, 2 * N : 4 * N], p1[1], ACT.Square)
-        place(0, 2, banks[7], kg[:, 1, N : 2 * N])
-        key_grad(banks[7], ops["qm0"], 3, ops["ds0"])
+        place(0, 2, banks[5], kg[:, 1, N : 2 * N])
+        key_grad(banks[5], ops["qm0"], 3, ops["ds0"])
+        for c in range(2, 4):
+            nc.scalar.activation(sq[1][:, c * N : (c + 1) * N], p1[c], ACT.Square)
         gated(g1[1], banks[0:4], 1, 1)
         ds_vector(st[6], sq[1], g1[1], 1)
-        late = p1[1].bitcast(BF16)
-        group("S", late, qm1, 0, N, 2)
+        late = p_late.bitcast(BF16)
+        group("S", late, qm1)
         quantize(ops["qm1"], E4M3, late)
         quantize(ops["ds1"], E5M2, st[6])
-        last = [banks[4], banks[5], banks[6], banks[0]]
+        last = [banks[4], banks[6], banks[7], banks[0]]
         for j in range(D // P):
             key_grad(last[j], ops["qm1"], j, ops["ds1"])
-        place(0, 3, banks[7], sq[1][:, 3 * N : 4 * N])
+        place(0, 3, banks[5], sq[1][:, 3 * N : 4 * N])
         for j in range(D // P):
             place(1, j, last[j], vg[0][:, j, :])
             nc.sync.dma_start(out=out[j * P : (j + 1) * P, :], in_=placed[j][:])

@@ -212,8 +212,7 @@ def tile_attend_gat_tnh_k_kernel(tc, qT, kT, vT, doT, rw, qm, offs, out):
             gather(vg[1][:, j, :], vp[j], 1, 2)
         gather(vg[0][:, 2, :], v_last[:, 0:T], 0, 1)
         gather(vg[0][:, 3, :], v_last[:, T : 2 * T], 0, 1)
-        group("S", st[3], vg[0], 0, H)
-        group("V", st[3], vg[0], H, N)
+        group("V", st[3], vg[0])
         gather(vg[1][:, 2, :], v_last[:], 1, 2)
         deal_half("V", st[7], do0, 0)
         deal_half("S", st[7], do0, 1)

@@ -214,8 +214,7 @@ def tile_attend_gat_tnh_k_kernel(tc, qT, kT, vT, doT, rw, qm, offs, out):
         gather(vg[0][:, 3, :], v_last[:, T : 2 * T], 0, 1)
         group("V", st[3], vg[0])
         gather(vg[1][:, 2, :], v_last[:], 1, 2)
-        deal_half("V", st[7], do0, 0)
-        deal_half("S", st[7], do0, 1)
+        deal("S", st[7], do0)
         quantize(ops["v0"], E4M3, st[3])
         quantize(ops["do0"], E5M2, st[7])
         dp_products(banks[0:4], ops["do0"], ops["v0"])
@@ -233,30 +232,31 @@ def tile_attend_gat_tnh_k_kernel(tc, qT, kT, vT, doT, rw, qm, offs, out):
         quantize(ops["q1"], E4M3, st[1], H, N)
         group("S", st[4], vg[1])
         deal("S", st[3], do1)
-        place(0, 0, banks[0], do1[:, 0, :])
+        place(0, 0, banks[0], kg[:, 0, 0:N])
         quantize(ops["v1"], E4M3, st[4])
         quantize(ops["do1"], E5M2, st[3])
         group("G", st[3], qm0, H, N)
         quantize(ops["qm0"], E4M3, st[3], H, N)
-        p_late = keep.tile([P, 2 * N], F32, name="p_late", align_bytes=64)[:]
-        p1 = [do1[:, 1, :], do1[:, 2, :], do1[:, 3, :], p_late[:, 0:N]]
+        p1 = [do1[:, c, :] for c in range(PACK)]
         for c in range(N // P):
             for t in range(PACK):
-                product(banks[4 + c % 3][:, t * P : (t + 1) * P], ops["q1"], E4M3, t, ops["k1"], E4M3, c * P, (c + 1) * P)
+                product(banks[4 + c][:, t * P : (t + 1) * P], ops["q1"], E4M3, t, ops["k1"], E4M3, c * P, (c + 1) * P)
             nc.scalar.activation(
                 p1[c].rearrange("p (n t) -> p n t", t=PACK),
-                banks[4 + c % 3][:].rearrange("p (t n) -> p n t", t=PACK),
+                banks[4 + c][:].rearrange("p (t n) -> p n t", t=PACK),
                 ACT.Tanh,
             )
-        key_grad(banks[5], ops["qm0"], 1, ops["ds0"])
-        place(0, 1, banks[5], kg[:, 1, 0:N])
-        key_grad(banks[5], ops["qm0"], 2, ops["ds0"])
-        dp_products(banks[0:4], ops["do1"], ops["v1"])
-        nc.scalar.activation(sq[1][:, 0 : 2 * N].rearrange("p (a b) -> p a b", a=2), do1[:, 1:3, :], ACT.Square)
+        key_grad(banks[4], ops["qm0"], 1, ops["ds0"])
+        nc.scalar.activation(sq[1][:, 0:N], p1[0], ACT.Square)
+        place(0, 1, banks[4], kg[:, 1, 0:N])
+        key_grad(banks[4], ops["qm0"], 2, ops["ds0"])
+        dp1 = banks[1:4] + banks[0:1]
+        dp_products(dp1, ops["do1"], ops["v1"])
+        nc.scalar.activation(sq[1][:, N : 2 * N], p1[1], ACT.Square)
         lo = st[3].bitcast(F32)
         nc.gpsimd.tensor_scalar(lo, sq[1][:, 0 : 2 * N], 1.0, -1.0, ALU.mult, ALU.add)
         g1 = halves(do0)
-        gated(g1[0], banks[0:4], 1, 0)
+        gated(g1[0], dp1, 1, 0)
         for c in range(2):
             nc.gpsimd.tensor_tensor(
                 st[6][:, c * N : (c + 1) * N].rearrange("p (n t) -> p n t", t=PACK),
@@ -264,20 +264,20 @@ def tile_attend_gat_tnh_k_kernel(tc, qT, kT, vT, doT, rw, qm, offs, out):
                 g1[0][:, :, c * P : (c + 1) * P].rearrange("p t n -> p n t"),
                 ALU.mult,
             )
-        place(0, 2, banks[5], kg[:, 1, N : 2 * N])
-        key_grad(banks[5], ops["qm0"], 3, ops["ds0"])
-        for c in range(2, 4):
-            nc.scalar.activation(sq[1][:, c * N : (c + 1) * N], p1[c], ACT.Square)
-        gated(g1[1], banks[0:4], 1, 1)
+        place(0, 2, banks[4], kg[:, 1, N : 2 * N])
+        key_grad(banks[4], ops["qm0"], 3, ops["ds0"])
+        p_late = do1[:, 2:4, :].rearrange("p a b -> p (a b)")
+        nc.scalar.activation(sq[1][:, 2 * N : 4 * N], p_late, ACT.Square)
+        gated(g1[1], dp1, 1, 1)
         ds_vector(st[6], sq[1], g1[1], 1)
         late = p_late.bitcast(BF16)
         group("S", late, qm1)
         quantize(ops["qm1"], E4M3, late)
         quantize(ops["ds1"], E5M2, st[6])
-        last = [banks[4], banks[6], banks[7], banks[0]]
+        last = [banks[5], banks[6], banks[7], banks[0]]
         for j in range(D // P):
             key_grad(last[j], ops["qm1"], j, ops["ds1"])
-        place(0, 3, banks[5], sq[1][:, 3 * N : 4 * N])
+        place(0, 3, banks[4], sq[1][:, 3 * N : 4 * N])
         for j in range(D // P):
             place(1, j, last[j], vg[0][:, j, :])
             nc.sync.dma_start(out=out[j * P : (j + 1) * P, :], in_=placed[j][:])

@@ -154,10 +154,11 @@ def tile_attend_gat_tnh_k_kernel(tc, qT, kT, vT, doT, rw, qm, offs, out):
             nc.vector.tensor_copy(placed[j][:].indirect(offsets[:, b * COLS : (b + 1) * COLS]), st)
 
         kp = [load_plane(kT, "kp", j) for j in range(PACK)]
+        vp = [load_plane(vT, "vp", 0)]
         q0 = load_rows(qT[0], "q0")
         gate = keep.tile([P, B, PACK], F32, name="gate")
         nc.scalar.dma_start(out=gate[:], in_=rw.rearrange("b (p t) o -> p b (t o)", t=PACK))
-        vp = [load_plane(vT, "vp", j) for j in range(2)]
+        vp += [load_plane(vT, "vp", 1)]
         v_last = keep.tile([P, 2 * T], F32, name="v_last")
         for j in range(2):
             nc.sync.dma_start(out=v_last[:, j * T : (j + 1) * T], in_=vT.rearrange("(p j) t -> p j t", j=PACK)[:, 2 + j, :])
@@ -194,20 +195,19 @@ def tile_attend_gat_tnh_k_kernel(tc, qT, kT, vT, doT, rw, qm, offs, out):
         gather(kg[:, 3, 0:N], kp[3], 0, 1)
         gather(kg[:, 3, N : 2 * N], kp[3], 1, 2)
         group("S", st[0], kg[:, :, 0:N])
-        deal("V", st[1], q0)
+        deal("S", st[1], q0)
+        gather(vg[0][:, 0, :], vp[0], 0, 1)
+        gather(vg[1][:, 0, :], vp[0], 1, 2)
         quantize(ops["k0"], E4M3, st[0])
         quantize(ops["q0"], E4M3, st[1])
-        group("S", st[2], kg[:, :, N : 2 * N])
+        group("G", st[1], kg[:, :, N : 2 * N])
         for t in range(PACK):
             product(banks[t][:], ops["q0"], E4M3, t, ops["k0"], E4M3)
             nc.scalar.activation(sq[0][:, t * N : (t + 1) * N], banks[t][:], ACT.Tanh)
-        quantize(ops["k1"], E4M3, st[2])
+        quantize(ops["k1"], E4M3, st[1])
         square(sq[0], 0)
         square(sq[0], 1)
-        for t in range(PACK):
-            row = sq[0][:, t * N : (t + 1) * N]
-            nc.scalar.activation(row, row, ACT.Identity, bias=gate[:, 0, t : t + 1], scale=neg_gate[:, 0, t : t + 1])
-        for j in range(2):
+        for j in range(1, 2):
             gather(vg[0][:, j, :], vp[j], 0, 1)
             gather(vg[1][:, j, :], vp[j], 1, 2)
         gather(vg[0][:, 2, :], v_last[:, 0:T], 0, 1)
@@ -215,16 +215,18 @@ def tile_attend_gat_tnh_k_kernel(tc, qT, kT, vT, doT, rw, qm, offs, out):
         group("V", st[3], vg[0])
         gather(vg[1][:, 2, :], v_last[:], 1, 2)
         deal("S", st[7], do0)
+        for t in range(PACK):
+            nc.scalar.activation(do0[:, t, :], sq[0][:, t * N : (t + 1) * N], ACT.Identity, bias=gate[:, 0, t : t + 1], scale=neg_gate[:, 0, t : t + 1])
         quantize(ops["v0"], E4M3, st[3])
         quantize(ops["do0"], E5M2, st[7])
         dp_products(banks[0:4], ops["do0"], ops["v0"])
         gather(vg[1][:, 3, :], v_last[:, T : 2 * T], 1, 2)
         for t in range(PACK):
-            nc.vector.tensor_tensor(st[0][:, t * N : (t + 1) * N], banks[t][:], sq[0][:, t * N : (t + 1) * N], ALU.mult)
+            nc.vector.tensor_tensor(st[0][:, t * N : (t + 1) * N], banks[t][:], do0[:, t, :], ALU.mult)
         nc.vector.tensor_copy(st[5].rearrange("p (n j) -> p n j", j=PACK), st[0].rearrange("p (j n) -> p n j", j=PACK))
         quantize(ops["ds0"], E5M2, st[5])
         deal("S", st[1], q1)
-        early = sq[0][:, 0 : 2 * N].bitcast(BF16)
+        early = do0.rearrange("p a b -> p (a b)")[:, 0 : 2 * N].bitcast(BF16)
         group("G", early, qm0, 0, H)
         quantize(ops["q1"], E4M3, st[1], 0, H)
         quantize(ops["qm0"], E4M3, early, 0, H)

@@ -17,7 +17,8 @@ ALU = mybir.AluOpType
 
 P = 128
 PACK = 4
-COLS = N // 16
+HALF = N // 2
+LIST_COLS = N // 16
 RAW_BUFS = 8
 
 
@@ -25,261 +26,247 @@ def tile_attend_gat_tnh_k_kernel(tc, qT, kT, vT, doT, rw, qm, offs, out):
     nc = tc.nc
     with ExitStack() as ctx:
         keep = ctx.enter_context(tc.tile_pool(name="keep", bufs=1))
-        work = ctx.enter_context(tc.tile_pool(name="work", bufs=1))
+        ring = ctx.enter_context(tc.tile_pool(name="ring", bufs=1))
         psum = ctx.enter_context(tc.psum_pool(name="psum", bufs=1))
 
-        offsets = keep.tile([P, B * COLS], U16, name="offsets")
-        nc.sync.dma_start(offsets[:], offs)
-
         def load_plane(pool_ap, label, j):
-            rows = pool_ap.rearrange("(p j) t -> p j t", j=PACK)
-            plane = work.tile([P, T], F32, name="%s%d" % (label, j), tag="raw", bufs=RAW_BUFS, align_bytes=64)
-            nc.sync.dma_start(out=plane[:], in_=rows[:, j, :])
+            plane = ring.tile([P, T], F32, name="%s%d" % (label, j), tag="raw", bufs=RAW_BUFS, align_bytes=64)
+            nc.sync.dma_start(out=plane[:], in_=pool_ap.rearrange("(p j) t -> p j t", j=PACK)[:, j, :])
             return plane[:]
 
         def load_rows(src, label):
-            tile = work.tile([P, PACK, N], F32, name=label, tag="raw", bufs=RAW_BUFS, align_bytes=64)
-            nc.sync.dma_start(out=tile[:], in_=src.rearrange("(p j) w -> p j w", j=PACK))
-            return tile[:]
+            rows = ring.tile([P, PACK, N], F32, name=label, tag="raw", bufs=RAW_BUFS, align_bytes=64)
+            nc.sync.dma_start(out=rows[:], in_=src.rearrange("(p j) w -> p j w", j=PACK))
+            return rows[:]
 
-        def staging(name):
-            return keep.tile([P, PACK * N], BF16, name=name, align_bytes=64)[:]
+        def packed_tile(name):
+            return keep.tile([P, N * PACK], BF16, name=name, align_bytes=64)[:]
 
-        def operand(name):
-            codes = keep.tile([P, N], U32, name=name + "_c", align_bytes=64)
-            scales = keep.tile([P, N], U8, name=name + "_s", align_bytes=64)
+        def mx_tiles(name):
+            codes = keep.tile([P, N], U32, name=name + "_codes", align_bytes=64)
+            scales = keep.tile([P, N], U8, name=name + "_scales", align_bytes=64)
             return codes, scales
 
-        def gather(dst, plane, lo, hi):
-            nc.vector.tensor_copy(dst, plane.indirect(offsets[:, lo * COLS : hi * COLS]))
+        def lists(first, end):
+            return offsets[:, first * LIST_COLS : end * LIST_COLS]
 
-        def move(eng, o, i):
-            if eng == "V":
-                nc.vector.tensor_copy(o, i)
-            elif eng == "S":
-                nc.scalar.copy(o, i)
-            else:
-                nc.gpsimd.tensor_scalar(o, i, 1.0, 0.0, ALU.mult, ALU.add)
+        def gather(dst, window, first, end):
+            nc.vector.tensor_copy(dst, window.indirect(lists(first, end)))
 
-        def group(eng, dst, src, lo=0, hi=N, pieces=1):
-            order = "p c i j" if eng == "G" else "p c j i"
-            o = dst.rearrange("p (c i j) -> " + order, i=PACK, j=PACK)
-            i = src.rearrange("p j (c i) -> " + order, i=PACK)
-            step = (hi - lo) // PACK // pieces
-            for c in range(lo // PACK, hi // PACK, step):
-                move(eng, o[:, c : c + step], i[:, c : c + step])
+        def pack_views(order, dst, src, lo, hi):
+            cs = slice(lo // PACK, hi // PACK)
+            return (
+                dst.rearrange("p (c i j) -> " + order, i=PACK, j=PACK)[:, cs],
+                src.rearrange("p j (c i) -> " + order, i=PACK)[:, cs],
+            )
 
-        def deal(eng, dst, src, pieces=1):
-            o = dst.rearrange("p (t m j) -> p m j t", t=PACK, j=PACK)
-            i = src.rearrange("p j (m t) -> p m j t", t=PACK)
-            step = P // pieces
-            for c in range(0, P, step):
-                move(eng, o[:, c : c + step], i[:, c : c + step])
+        def pack(copy, dst, src):
+            copy(*pack_views("p c j i", dst, src, 0, N))
 
-        def deal_t(eng, dst, src, t0, t1):
-            o = dst.rearrange("p (t m j) -> p t m j", t=PACK, j=PACK)[:, t0:t1]
-            i = src.rearrange("p j (m t) -> p t m j", t=PACK)[:, t0:t1]
-            move(eng, o, i)
+        def pack_gpsimd(dst, src, lo=0, hi=N):
+            nc.gpsimd.tensor_scalar(*pack_views("p c i j", dst, src, lo, hi), 1.0, 0.0, ALU.mult, ALU.add)
 
-        def quantize(op, fmt, src, lo=0, hi=N):
+        def deal(dst, src):
+            nc.scalar.copy(
+                dst.rearrange("p (t m j) -> p m j t", t=PACK, j=PACK), src.rearrange("p j (m t) -> p m j t", t=PACK)
+            )
+
+        def quantize(mx, fmt, src, lo=0, hi=N):
+            codes, scales = mx
             nc.vector.quantize_mx(
-                out=op[0][:, lo:hi].bitcast(fmt), scales=op[1][:, lo:hi], in_=src[:, lo * PACK : hi * PACK]
+                out=codes[:, lo:hi].bitcast(fmt), scales=scales[:, lo:hi], in_=src[:, lo * PACK : hi * PACK]
             )
 
-        def product(dst, left, lfmt, t, right, rfmt, lo=0, hi=N):
-            cols = slice(t * P, (t + 1) * P)
+        def product(dst, left, left_fmt, block, right, right_fmt, lo=0, hi=N):
+            cols = slice(block * P, (block + 1) * P)
             nc.tensor.matmul_mx(
-                out=dst, lhsT=left[0][:, cols].bitcast(lfmt), lhsT_scale=left[1][:, cols],
-                rhs=right[0][:, lo:hi].bitcast(rfmt), rhs_scale=right[1][:, lo:hi], start=True, stop=True,
+                out=dst,
+                lhsT=left[0][:, cols].bitcast(left_fmt),
+                lhsT_scale=left[1][:, cols],
+                rhs=right[0][:, lo:hi].bitcast(right_fmt),
+                rhs_scale=right[1][:, lo:hi],
+                start=True,
+                stop=True,
             )
 
-        def tanh_scores(sq, bk, q_op, k_op):
-            for c in range(N // P):
-                for t in range(PACK):
-                    product(bk[c][:, t * P : (t + 1) * P], q_op, E4M3, t, k_op, E4M3, c * P, (c + 1) * P)
-                nc.scalar.activation(
-                    sq[:, c * N : (c + 1) * N].rearrange("p (n t) -> p n t", t=PACK),
-                    bk[c][:].rearrange("p (t n) -> p n t", t=PACK),
-                    ACT.Tanh,
-                )
+        def key_grad(bank, b, j):
+            product(bank[:], qm_mx[b], E4M3, j, ds_mx[b], E5M2)
 
-        def square(sq, h):
-            half = sq[:, h * 2 * N : (h + 1) * 2 * N]
-            nc.scalar.activation(half, half, ACT.Square)
+        def place(b, j, bank, stage):
+            nc.scalar.copy(stage, bank[:])
+            nc.vector.tensor_copy(placed[j][:].indirect(lists(b, b + 1)), stage)
 
-        def less_one(sq, h):
-            half = sq[:, h * 2 * N : (h + 1) * 2 * N]
-            nc.gpsimd.tensor_scalar(half, half, 1.0, -1.0, ALU.mult, ALU.add)
+        def slot_major(x):
+            return x.rearrange("p (n t) -> p n t", t=PACK)
 
-        def dp_products(bk, do_op, v_op, ts=range(PACK)):
-            for t in ts:
-                product(bk[t][:], do_op, E5M2, t, v_op, E4M3)
-
-        def gated(g, bk, b, h):
-            for t in range(PACK):
-                nc.scalar.activation(
-                    g[:, t, :], bk[t][:, h * N // 2 : (h + 1) * N // 2], ACT.Copy, scale=neg_gate[:, b, t : t + 1]
-                )
-
-        def ds_vector(ds, sq, g, h):
-            cols = slice(h * 2 * N, (h + 1) * 2 * N)
-            nc.vector.scalar_tensor_tensor(
-                ds[:, cols].rearrange("p (n t) -> p n t", t=PACK),
-                sq[:, cols].rearrange("p (n t) -> p n t", t=PACK),
-                1.0,
-                g.rearrange("p t n -> p n t"),
-                ALU.subtract,
-                ALU.mult,
-            )
-
-        def ds_gpsimd(ds, sq, g, h):
-            for c in range(2):
-                cols = slice(h * 2 * N + c * N, h * 2 * N + (c + 1) * N)
-                nc.gpsimd.tensor_tensor(
-                    ds[:, cols].rearrange("p (n t) -> p n t", t=PACK),
-                    sq[:, cols].rearrange("p (n t) -> p n t", t=PACK),
-                    g[:, :, c * P : (c + 1) * P].rearrange("p t n -> p n t"),
-                    ALU.mult,
-                )
-
-        def halves(x):
-            flat = x.rearrange("p a b -> p (a b)")
-            return [flat[:, h * 2 * N : (h + 1) * 2 * N].rearrange("p (t n) -> p t n", t=PACK) for h in range(2)]
-
-        def key_grad(bank, qm_op, j, ds_op):
-            product(bank[:], qm_op, E4M3, j, ds_op, E5M2)
-
-        def place(b, j, bank, st):
-            nc.scalar.copy(st, bank[:])
-            nc.vector.tensor_copy(placed[j][:].indirect(offsets[:, b * COLS : (b + 1) * COLS]), st)
-
-        kp = [load_plane(kT, "kp", j) for j in range(PACK)]
-        vp = [load_plane(vT, "vp", 0)]
-        q0 = load_rows(qT[0], "q0")
+        offsets = keep.tile([P, B * LIST_COLS], U16, name="offsets")
+        nc.sync.dma_start(offsets[:], offs)
+        k_planes = [load_plane(kT, "k_plane", j) for j in range(PACK)]
+        v_planes = [load_plane(vT, "v_plane", 0)]
+        q0_rows = load_rows(qT[0], "q0_rows")
         gate = keep.tile([P, B, PACK], F32, name="gate")
         nc.scalar.dma_start(out=gate[:], in_=rw.rearrange("b (p t) o -> p b (t o)", t=PACK))
-        vp += [load_plane(vT, "vp", 1)]
+        v_planes.append(load_plane(vT, "v_plane", 1))
         v_last = keep.tile([P, 2 * T], F32, name="v_last")
         for j in range(2):
-            nc.sync.dma_start(out=v_last[:, j * T : (j + 1) * T], in_=vT.rearrange("(p j) t -> p j t", j=PACK)[:, 2 + j, :])
-        do0 = load_rows(doT[0], "do0")
-        q1 = load_rows(qT[1], "q1")
-        qm0 = load_rows(qm[0], "qm0")
-        do1 = load_rows(doT[1], "do1")
-        qm1 = load_rows(qm[1], "qm1")
+            v_planes.append(v_last[:, j * T : (j + 1) * T])
+            nc.sync.dma_start(out=v_planes[2 + j], in_=vT.rearrange("(p j) t -> p j t", j=PACK)[:, 2 + j, :])
+        do0_rows = load_rows(doT[0], "do0_rows")
+        q1_rows = load_rows(qT[1], "q1_rows")
+        qm0_rows = load_rows(qm[0], "qm0_rows")
+        do1_rows = load_rows(doT[1], "do1_rows")
+        qm1_rows = load_rows(qm[1], "qm1_rows")
+
         placed = []
         for j in range(D // P):
             tile = keep.tile([P, T], F32, name="placed%d" % j)
             nc.gpsimd.memset(tile[:], 0.0)
             placed.append(tile)
-        kg = keep.tile([P, PACK, B * N], F32, name="kg")
-        shared = keep.tile([P, 5 * N], F32, name="shared", align_bytes=64)
-        vg = [keep.tile([P, PACK, N], F32, name="vg0")[:], shared[:, 0 : 4 * N].rearrange("p (j n) -> p j n", j=PACK)]
-        sq = [keep.tile([P, N * PACK], F32, name="sq%d" % b, align_bytes=64)[:] for b in range(B)]
-        st = [staging("st%d" % i) for i in range(7)]
-        st += [shared[:, 3 * N : 5 * N].bitcast(BF16)]
-        ops = {x: operand(x) for x in ("k0", "k1", "q0", "q1", "v0", "v1", "do0", "do1", "qm0", "qm1", "ds0", "ds1")}
-        ops["k1"] = ops["k0"]
+
+        keys = keep.tile([P, PACK, B * N], F32, name="keys")
+        values1_tile = keep.tile([P, (PACK + 1) * N], F32, name="values1_tile", align_bytes=64)
+        values0 = keep.tile([P, PACK, N], F32, name="values0")[:]
+        values1 = values1_tile[:, 0 : PACK * N].rearrange("p (j n) -> p j n", j=PACK)
+        squares = [keep.tile([P, N * PACK], F32, name="squares%d" % b, align_bytes=64)[:] for b in range(B)]
+        k0_packed, q0_packed, q1_packed, v0_packed, v1_packed, ds0_packed, ds1_packed = (
+            packed_tile(name + "_packed") for name in ("k0", "q0", "q1", "v0", "v1", "ds0", "ds1")
+        )
+        do0_packed = values1_tile[:, 3 * N : 5 * N].bitcast(BF16)
+        k_mx = mx_tiles("k")
+        q_mx, v_mx, do_mx, qm_mx, ds_mx = (
+            [mx_tiles("%s%d" % (name, b)) for b in range(B)] for name in ("q", "v", "do", "qm", "ds")
+        )
         banks = [psum.tile([P, N], F32, name="bank%d" % i) for i in range(8)]
         neg_gate = keep.tile([P, B, PACK], F32, name="neg_gate")
-        nc.gpsimd.tensor_scalar(neg_gate[:], gate[:], -1.0, 0.0, ALU.mult, ALU.add)
-        H = N // 2
-
-        def deal_half(eng, dst, src, h):
-            o = dst.rearrange("p (t m j) -> p m j t", t=PACK, j=PACK)
-            i = src.rearrange("p j (m t) -> p m j t", t=PACK)
-            move(eng, o[:, h * P // 2 : (h + 1) * P // 2], i[:, h * P // 2 : (h + 1) * P // 2])
+        nc.scalar.activation(neg_gate[:], gate[:], ACT.Copy, scale=-1.0)
 
         for j in range(PACK - 1):
-            gather(kg[:, j, :], kp[j], 0, 2)
-        gather(kg[:, 3, 0:N], kp[3], 0, 1)
-        gather(kg[:, 3, N : 2 * N], kp[3], 1, 2)
-        group("S", st[0], kg[:, :, 0:N])
-        deal("S", st[1], q0)
-        gather(vg[0][:, 0, :], vp[0], 0, 1)
-        gather(vg[1][:, 0, :], vp[0], 1, 2)
-        quantize(ops["k0"], E4M3, st[0])
-        quantize(ops["q0"], E4M3, st[1])
-        group("G", st[1], kg[:, :, N : 2 * N])
+            gather(keys[:, j, :], k_planes[j], 0, B)
+        gather(keys[:, 3, 0:N], k_planes[3], 0, 1)
+        gather(keys[:, 3, N : 2 * N], k_planes[3], 1, 2)
+        pack_gpsimd(k0_packed, keys[:, :, 0:N])
+        deal(q0_packed, q0_rows)
+        gather(values0[:, 0, :], v_planes[0], 0, 1)
+        gather(values1[:, 0, :], v_planes[0], 1, 2)
+        quantize(k_mx, E4M3, k0_packed)
+        quantize(q_mx[0], E4M3, q0_packed)
+        k1_packed = q0_packed
+        pack_gpsimd(k1_packed, keys[:, :, N : 2 * N])
+
+        square0 = [squares[0][:, t * N : (t + 1) * N] for t in range(PACK)]
         for t in range(PACK):
-            product(banks[t][:], ops["q0"], E4M3, t, ops["k0"], E4M3)
-            nc.scalar.activation(sq[0][:, t * N : (t + 1) * N], banks[t][:], ACT.Tanh)
-        quantize(ops["k1"], E4M3, st[1])
-        square(sq[0], 0)
-        square(sq[0], 1)
-        for j in range(1, 2):
-            gather(vg[0][:, j, :], vp[j], 0, 1)
-            gather(vg[1][:, j, :], vp[j], 1, 2)
-        gather(vg[0][:, 2, :], v_last[:, 0:T], 0, 1)
-        gather(vg[0][:, 3, :], v_last[:, T : 2 * T], 0, 1)
-        group("V", st[3], vg[0])
-        gather(vg[1][:, 2, :], v_last[:], 1, 2)
-        deal("S", st[7], do0)
+            product(banks[t][:], q_mx[0], E4M3, t, k_mx, E4M3)
+            nc.scalar.activation(square0[t], banks[t][:], ACT.Tanh)
+        quantize(k_mx, E4M3, k1_packed)
+        for h in range(2):
+            pair = squares[0][:, h * 2 * N : (h + 1) * 2 * N]
+            nc.scalar.activation(pair, pair, ACT.Square)
+        after_k1 = k1_packed.bitcast(F32)
+        weight = [after_k1[:, 0:N], after_k1[:, N : 2 * N], do0_rows[:, 2, :], do0_rows[:, 3, :]]
+        for t in range(2):
+            nc.gpsimd.tensor_scalar(
+                weight[t], square0[t], neg_gate[:, 0, t : t + 1], gate[:, 0, t : t + 1], ALU.mult, ALU.add
+            )
+
+        gather(values0[:, 1, :], v_planes[1], 0, 1)
+        gather(values1[:, 1, :], v_planes[1], 1, 2)
+        gather(values0[:, 2, :], v_planes[2], 0, 1)
+        gather(values0[:, 3, :], v_planes[3], 0, 1)
+        pack(nc.vector.tensor_copy, v0_packed, values0)
+        gather(values1[:, 2, :], v_last[:], 1, 2)
+        deal(do0_packed, do0_rows)
+        for t in range(2, PACK):
+            nc.scalar.activation(
+                weight[t], square0[t], ACT.Identity, bias=gate[:, 0, t : t + 1], scale=neg_gate[:, 0, t : t + 1]
+            )
+        quantize(v_mx[0], E4M3, v0_packed)
+        quantize(do_mx[0], E5M2, do0_packed)
         for t in range(PACK):
-            nc.scalar.activation(do0[:, t, :], sq[0][:, t * N : (t + 1) * N], ACT.Identity, bias=gate[:, 0, t : t + 1], scale=neg_gate[:, 0, t : t + 1])
-        quantize(ops["v0"], E4M3, st[3])
-        quantize(ops["do0"], E5M2, st[7])
-        dp_products(banks[0:4], ops["do0"], ops["v0"])
-        gather(vg[1][:, 3, :], v_last[:, T : 2 * T], 1, 2)
+            product(banks[t][:], do_mx[0], E5M2, t, v_mx[0], E4M3)
+        gather(values1[:, 3, :], v_planes[3], 1, 2)
+
+        ds0_rows = k0_packed
         for t in range(PACK):
-            nc.vector.tensor_tensor(st[0][:, t * N : (t + 1) * N], banks[t][:], do0[:, t, :], ALU.mult)
-        nc.vector.tensor_copy(st[5].rearrange("p (n j) -> p n j", j=PACK), st[0].rearrange("p (j n) -> p n j", j=PACK))
-        quantize(ops["ds0"], E5M2, st[5])
-        deal("S", st[1], q1)
-        early = do0.rearrange("p a b -> p (a b)")[:, 0 : 2 * N].bitcast(BF16)
-        group("G", early, qm0, 0, H)
-        quantize(ops["q1"], E4M3, st[1], 0, H)
-        quantize(ops["qm0"], E4M3, early, 0, H)
-        key_grad(banks[0], ops["qm0"], 0, ops["ds0"])
-        quantize(ops["q1"], E4M3, st[1], H, N)
-        group("S", st[4], vg[1])
-        deal("S", st[3], do1)
-        place(0, 0, banks[0], kg[:, 0, 0:N])
-        quantize(ops["v1"], E4M3, st[4])
-        quantize(ops["do1"], E5M2, st[3])
-        group("G", st[3], qm0, H, N)
-        quantize(ops["qm0"], E4M3, st[3], H, N)
-        p1 = [do1[:, c, :] for c in range(PACK)]
+            nc.vector.tensor_tensor(ds0_rows[:, t * N : (t + 1) * N], banks[t][:], weight[t], ALU.mult)
+        nc.vector.tensor_copy(slot_major(ds0_packed), ds0_rows.rearrange("p (t n) -> p n t", t=PACK))
+        quantize(ds_mx[0], E5M2, ds0_packed)
+
+        deal(q1_packed, q1_rows)
+        qm0_first = k1_packed
+        pack_gpsimd(qm0_first, qm0_rows, 0, HALF)
+        quantize(q_mx[1], E4M3, q1_packed, 0, HALF)
+        quantize(qm_mx[0], E4M3, qm0_first, 0, HALF)
+        key_grad(banks[0], 0, 0)
+        quantize(q_mx[1], E4M3, q1_packed, HALF, N)
+        pack(nc.scalar.copy, v1_packed, values1)
+        do1_packed = v0_packed
+        deal(do1_packed, do1_rows)
+        place(0, 0, banks[0], keys[:, 0, 0:N])
+        quantize(v_mx[1], E4M3, v1_packed)
+        quantize(do_mx[1], E5M2, do1_packed)
+        qm0_second = do1_packed
+        pack_gpsimd(qm0_second, qm0_rows, HALF, N)
+        quantize(qm_mx[0], E4M3, qm0_second, HALF, N)
+
         for c in range(N // P):
             for t in range(PACK):
-                product(banks[4 + c][:, t * P : (t + 1) * P], ops["q1"], E4M3, t, ops["k1"], E4M3, c * P, (c + 1) * P)
+                product(banks[4 + c][:, t * P : (t + 1) * P], q_mx[1], E4M3, t, k_mx, E4M3, c * P, (c + 1) * P)
             nc.scalar.activation(
-                p1[c].rearrange("p (n t) -> p n t", t=PACK),
-                banks[4 + c][:].rearrange("p (t n) -> p n t", t=PACK),
-                ACT.Tanh,
+                slot_major(do1_rows[:, c, :]), banks[4 + c][:].rearrange("p (t n) -> p n t", t=PACK), ACT.Tanh
             )
-        key_grad(banks[4], ops["qm0"], 1, ops["ds0"])
-        nc.scalar.activation(sq[1][:, 0:N], p1[0], ACT.Square)
-        place(0, 1, banks[4], kg[:, 1, 0:N])
-        key_grad(banks[4], ops["qm0"], 2, ops["ds0"])
-        dp1 = banks[1:4] + banks[0:1]
-        dp_products(dp1, ops["do1"], ops["v1"])
-        nc.scalar.activation(sq[1][:, N : 2 * N], p1[1], ACT.Square)
-        lo = st[3].bitcast(F32)
-        nc.gpsimd.tensor_scalar(lo, sq[1][:, 0 : 2 * N], 1.0, -1.0, ALU.mult, ALU.add)
-        g1 = halves(do0)
-        gated(g1[0], dp1, 1, 0)
+        key_grad(banks[4], 0, 1)
+        nc.scalar.activation(squares[1][:, 0:N], do1_rows[:, 0, :], ACT.Square)
+        place(0, 1, banks[4], keys[:, 1, 0:N])
+        key_grad(banks[4], 0, 2)
+        dp1_banks = banks[1:4] + banks[0:1]
+        for t in range(PACK):
+            product(dp1_banks[t][:], do_mx[1], E5M2, t, v_mx[1], E4M3)
+        nc.scalar.activation(squares[1][:, N : 2 * N], do1_rows[:, 1, :], ACT.Square)
+
+        flat = do0_rows.rearrange("p a b -> p (a b)")
+        gated = [flat[:, h * 2 * N : (h + 1) * 2 * N].rearrange("p (t n) -> p t n", t=PACK) for h in range(2)]
+
+        def gate_dp(h):
+            for t in range(PACK):
+                nc.scalar.activation(
+                    gated[h][:, t, :],
+                    dp1_banks[t][:, h * HALF : (h + 1) * HALF],
+                    ACT.Copy,
+                    scale=neg_gate[:, 1, t : t + 1],
+                )
+
+        less_one = qm0_second.bitcast(F32)
+        nc.gpsimd.tensor_scalar(less_one, squares[1][:, 0 : 2 * N], 1.0, -1.0, ALU.mult, ALU.add)
+        gate_dp(0)
         for c in range(2):
             nc.gpsimd.tensor_tensor(
-                st[6][:, c * N : (c + 1) * N].rearrange("p (n t) -> p n t", t=PACK),
-                lo[:, c * N : (c + 1) * N].rearrange("p (n t) -> p n t", t=PACK),
-                g1[0][:, :, c * P : (c + 1) * P].rearrange("p t n -> p n t"),
+                slot_major(ds1_packed[:, c * N : (c + 1) * N]),
+                slot_major(less_one[:, c * N : (c + 1) * N]),
+                gated[0][:, :, c * P : (c + 1) * P].rearrange("p t n -> p n t"),
                 ALU.mult,
             )
-        place(0, 2, banks[4], kg[:, 1, N : 2 * N])
-        key_grad(banks[4], ops["qm0"], 3, ops["ds0"])
-        p_late = do1[:, 2:4, :].rearrange("p a b -> p (a b)")
-        nc.scalar.activation(sq[1][:, 2 * N : 4 * N], p_late, ACT.Square)
-        gated(g1[1], dp1, 1, 1)
-        ds_vector(st[6], sq[1], g1[1], 1)
-        late = p_late.bitcast(BF16)
-        group("S", late, qm1)
-        quantize(ops["qm1"], E4M3, late)
-        quantize(ops["ds1"], E5M2, st[6])
-        last = [banks[5], banks[6], banks[7], banks[0]]
+        place(0, 2, banks[4], keys[:, 1, N : 2 * N])
+        key_grad(banks[4], 0, 3)
+        tanh_second = do1_rows[:, 2:4, :].rearrange("p a b -> p (a b)")
+        nc.scalar.activation(squares[1][:, 2 * N : 4 * N], tanh_second, ACT.Square)
+        gate_dp(1)
+        nc.vector.scalar_tensor_tensor(
+            slot_major(ds1_packed[:, 2 * N : 4 * N]),
+            slot_major(squares[1][:, 2 * N : 4 * N]),
+            1.0,
+            gated[1].rearrange("p t n -> p n t"),
+            ALU.subtract,
+            ALU.mult,
+        )
+        qm1_packed = tanh_second.bitcast(BF16)
+        pack(nc.scalar.copy, qm1_packed, qm1_rows)
+        quantize(qm_mx[1], E4M3, qm1_packed)
+        quantize(ds_mx[1], E5M2, ds1_packed)
+
+        dk1_banks = banks[5:8] + banks[0:1]
         for j in range(D // P):
-            key_grad(last[j], ops["qm1"], j, ops["ds1"])
-        place(0, 3, banks[4], sq[1][:, 3 * N : 4 * N])
+            key_grad(dk1_banks[j], 1, j)
+        place(0, 3, banks[4], squares[1][:, 3 * N : 4 * N])
         for j in range(D // P):
-            place(1, j, last[j], vg[0][:, j, :])
+            place(1, j, dk1_banks[j], values0[:, j, :])
             nc.sync.dma_start(out=out[j * P : (j + 1) * P, :], in_=placed[j][:])

@@ -123,7 +123,9 @@ def tile_attend_gat_tnh_k_kernel(tc, qT, kT, vT, doT, rw, qm, offs, out):
             nc.gpsimd.memset(tile[:], 0.0)
             placed.append(tile)
 
-        keys = keep.tile([P, PACK, B * N], F32, name="keys")
+        keys = keep.tile([P, PACK, B * N], BF16, name="keys")
+        cast_plane = keep.tile([P, T], BF16, name="cast_plane")
+        stage = keep.tile([P, 3, N], F32, name="stage")
         values1_tile = keep.tile([P, (PACK + 1) * N], F32, name="values1_tile", align_bytes=64)
         values0 = keep.tile([P, PACK, N], F32, name="values0")[:]
         values1 = values1_tile[:, 0 : PACK * N].rearrange("p (j n) -> p j n", j=PACK)
@@ -141,7 +143,12 @@ def tile_attend_gat_tnh_k_kernel(tc, qT, kT, vT, doT, rw, qm, offs, out):
         nc.scalar.activation(neg_gate[:], gate[:], ACT.Copy, scale=-1.0)
 
         for j in range(PACK - 1):
-            gather(keys[:, j, :], k_planes[j], 0, B)
+            if j == 2:
+                nc.scalar.copy(cast_plane[:], k_planes[j])
+                for b in range(B):
+                    nc.scalar.activation(keys[:, j, b * N : (b + 1) * N], cast_plane[:].indirect(lists(b, b + 1)), ACT.Copy)
+            else:
+                gather(keys[:, j, :], k_planes[j], 0, B)
         gather(keys[:, 3, 0:N], k_planes[3], 0, 1)
         gather(keys[:, 3, N : 2 * N], k_planes[3], 1, 2)
         pack_gpsimd(k0_packed, keys[:, :, 0:N])
@@ -201,7 +208,7 @@ def tile_attend_gat_tnh_k_kernel(tc, qT, kT, vT, doT, rw, qm, offs, out):
         pack(nc.scalar.copy, v1_packed, values1)
         do1_packed = v0_packed
         deal(do1_packed, do1_rows)
-        place(0, 0, banks[0], keys[:, 0, 0:N])
+        place(0, 0, banks[0], stage[:, 0, :])
         quantize(v_mx[1], E4M3, v1_packed)
         quantize(do_mx[1], E5M2, do1_packed)
         qm0_second = do1_packed
@@ -216,7 +223,7 @@ def tile_attend_gat_tnh_k_kernel(tc, qT, kT, vT, doT, rw, qm, offs, out):
             )
         key_grad(banks[4], 0, 1)
         nc.scalar.activation(squares[1][:, 0:N], do1_rows[:, 0, :], ACT.Square)
-        place(0, 1, banks[4], keys[:, 1, 0:N])
+        place(0, 1, banks[4], stage[:, 1, :])
         key_grad(banks[4], 0, 2)
         dp1_banks = banks[1:4] + banks[0:1]
         for t in range(PACK):
@@ -245,7 +252,7 @@ def tile_attend_gat_tnh_k_kernel(tc, qT, kT, vT, doT, rw, qm, offs, out):
                 gated[0][:, :, c * P : (c + 1) * P].rearrange("p t n -> p n t"),
                 ALU.mult,
             )
-        place(0, 2, banks[4], keys[:, 1, N : 2 * N])
+        place(0, 2, banks[4], stage[:, 2, :])
         key_grad(banks[4], 0, 3)
         tanh_second = do1_rows[:, 2:4, :].rearrange("p a b -> p (a b)")
         nc.scalar.activation(squares[1][:, 2 * N : 4 * N], tanh_second, ACT.Square)

@@ -8,6 +8,7 @@ FLOPS = 3 * 2 * B * N * D * R
 F32 = mybir.dt.float32
 BF16 = mybir.dt.bfloat16
 U32 = mybir.dt.uint32
+I32 = mybir.dt.int32
 U16 = mybir.dt.uint16
 U8 = mybir.dt.uint8
 E4M3 = mybir.dt.float8_e4m3fn_x4
@@ -129,6 +130,8 @@ def tile_attend_gat_tnh_k_kernel(tc, qT, kT, vT, doT, rw, qm, offs, out):
         values1_tile = keep.tile([P, (PACK + 1) * N], F32, name="values1_tile", align_bytes=64)
         values0 = keep.tile([P, PACK, N], F32, name="values0")[:]
         values1 = values1_tile[:, 0 : PACK * N].rearrange("p (j n) -> p j n", j=PACK)
+        pairs0 = packed_tile("pairs0")
+        pair_rows = pairs0.rearrange("p (u n e) -> p u e n", u=2, e=2)
         squares = [keep.tile([P, N * PACK], F32, name="squares%d" % b, align_bytes=64)[:] for b in range(B)]
         k0_packed, q0_packed, q1_packed, v0_packed, v1_packed, ds0_packed, ds1_packed = (
             packed_tile(name + "_packed") for name in ("k0", "q0", "q1", "v0", "v1", "ds0", "ds1")
@@ -153,7 +156,7 @@ def tile_attend_gat_tnh_k_kernel(tc, qT, kT, vT, doT, rw, qm, offs, out):
         gather(keys[:, 3, N : 2 * N], k_planes[3], 1, 2)
         pack_gpsimd(k0_packed, keys[:, :, 0:N])
         deal(q0_packed, q0_rows)
-        gather(values0[:, 0, :], v_planes[0], 0, 1)
+        gather(pair_rows[:, 0, 0, :], v_planes[0], 0, 1)
         gather(values1[:, 0, :], v_planes[0], 1, 2)
         quantize(k_mx, E4M3, k0_packed)
         quantize(q_mx[0], E4M3, q0_packed)
@@ -175,11 +178,14 @@ def tile_attend_gat_tnh_k_kernel(tc, qT, kT, vT, doT, rw, qm, offs, out):
                 weight[t], square0[t], neg_gate[:, 0, t : t + 1], gate[:, 0, t : t + 1], ALU.mult, ALU.add
             )
 
-        gather(values0[:, 1, :], v_planes[1], 0, 1)
+        gather(pair_rows[:, 0, 1, :], v_planes[1], 0, 1)
         gather(values1[:, 1, :], v_planes[1], 1, 2)
-        gather(values0[:, 2, :], v_planes[2], 0, 1)
-        gather(values0[:, 3, :], v_planes[3], 0, 1)
-        pack(nc.vector.tensor_copy, v0_packed, values0)
+        gather(pair_rows[:, 1, 0, :], v_planes[2], 0, 1)
+        gather(pair_rows[:, 1, 1, :], v_planes[3], 0, 1)
+        nc.vector.tensor_copy(
+            v0_packed.bitcast(I32).rearrange("p (c i u) -> p c u i", i=PACK, u=2),
+            pairs0.bitcast(I32).rearrange("p (u c i) -> p c u i", i=PACK, u=2),
+        )
         gather(values1[:, 2, :], v_last[:], 1, 2)
         deal(do0_packed, do0_rows)
         for t in range(2, PACK):

@@ -18,6 +18,7 @@ ALU = mybir.AluOpType
 
 P = 128
 PACK = 4
+QM1_TAIL = 128
 HALF = N // 2
 LIST_COLS = N // 16
 RAW_BUFS = 8
@@ -197,6 +198,8 @@ def tile_attend_gat_tnh_k_kernel(tc, qT, kT, vT, doT, rw, qm, offs, out):
         for t in range(PACK):
             product(banks[t][:], do_mx[0], E5M2, t, v_mx[0], E4M3)
         gather(values1[:, 3, :], v_planes[3], 1, 2)
+        qm0_packed = v0_packed
+        pack_gpsimd(qm0_packed, qm0_rows)
 
         ds0_rows = k0_packed
         for t in range(PACK):
@@ -205,36 +208,34 @@ def tile_attend_gat_tnh_k_kernel(tc, qT, kT, vT, doT, rw, qm, offs, out):
         quantize(ds_mx[0], E5M2, ds0_packed)
 
         deal(q1_packed, q1_rows)
-        qm0_first = k1_packed
-        pack_gpsimd(qm0_first, qm0_rows, 0, HALF)
         quantize(q_mx[1], E4M3, q1_packed, 0, HALF)
-        quantize(qm_mx[0], E4M3, qm0_first, 0, HALF)
+        quantize(qm_mx[0], E4M3, qm0_packed, 0, HALF)
         key_grad(banks[0], 0, 0)
         quantize(q_mx[1], E4M3, q1_packed, HALF, N)
+        quantize(qm_mx[0], E4M3, qm0_packed, HALF, N)
         pack(nc.scalar.copy, v1_packed, values1)
-        do1_packed = v0_packed
+        late = keep.tile([P, 3 * N], F32, name="late", align_bytes=64)
+        do1_packed = late[:, 0 : 2 * N].bitcast(BF16)
         deal(do1_packed, do1_rows)
         place(0, 0, banks[0], stage[:, 0, :])
         quantize(v_mx[1], E4M3, v1_packed)
         quantize(do_mx[1], E5M2, do1_packed)
-        qm0_second = do1_packed
-        pack_gpsimd(qm0_second, qm0_rows, HALF, N)
-        quantize(qm_mx[0], E4M3, qm0_second, HALF, N)
+        qm1_packed = late[:, 2 * QM1_TAIL : 2 * N + 2 * QM1_TAIL].bitcast(BF16)
+        pack_gpsimd(qm1_packed, qm1_rows, 0, N - QM1_TAIL)
 
         for c in range(N // P):
             for t in range(PACK):
                 product(banks[4 + c][:, t * P : (t + 1) * P], q_mx[1], E4M3, t, k_mx, E4M3, c * P, (c + 1) * P)
-            nc.scalar.activation(
-                slot_major(do1_rows[:, c, :]), banks[4 + c][:].rearrange("p (t n) -> p n t", t=PACK), ACT.Tanh
-            )
-        key_grad(banks[4], 0, 1)
-        nc.scalar.activation(squares[1][:, 0:N], do1_rows[:, 0, :], ACT.Square)
-        place(0, 1, banks[4], stage[:, 1, :])
-        key_grad(banks[4], 0, 2)
-        dp1_banks = banks[1:4] + banks[0:1]
-        for t in range(PACK):
-            product(dp1_banks[t][:], do_mx[1], E5M2, t, v_mx[1], E4M3)
-        nc.scalar.activation(squares[1][:, N : 2 * N], do1_rows[:, 1, :], ACT.Square)
+
+        def chunk(x, c):
+            return x[:, c * N : (c + 1) * N]
+
+        square1 = [chunk(squares[1], c) for c in range(PACK)]
+        tanh_row = late[:, 2 * N : 3 * N]
+
+        def square_chunk(c, tanh):
+            nc.scalar.activation(slot_major(tanh), banks[4 + c][:].rearrange("p (t n) -> p n t", t=PACK), ACT.Tanh)
+            nc.scalar.activation(square1[c], tanh, ACT.Square)
 
         flat = do0_rows.rearrange("p a b -> p (a b)")
         gated = [flat[:, h * 2 * N : (h + 1) * 2 * N].rearrange("p (t n) -> p t n", t=PACK) for h in range(2)]
@@ -248,31 +249,37 @@ def tile_attend_gat_tnh_k_kernel(tc, qT, kT, vT, doT, rw, qm, offs, out):
                     scale=neg_gate[:, 1, t : t + 1],
                 )
 
-        less_one = qm0_second.bitcast(F32)
-        nc.gpsimd.tensor_scalar(less_one, squares[1][:, 0 : 2 * N], 1.0, -1.0, ALU.mult, ALU.add)
-        gate_dp(0)
-        for c in range(2):
+        def gated_chunk(c):
+            return gated[c // 2][:, :, (c % 2) * P : (c % 2 + 1) * P].rearrange("p t n -> p n t")
+
+        def multiply_on_gpsimd(c):
             nc.gpsimd.tensor_tensor(
-                slot_major(ds1_packed[:, c * N : (c + 1) * N]),
-                slot_major(less_one[:, c * N : (c + 1) * N]),
-                gated[0][:, :, c * P : (c + 1) * P].rearrange("p t n -> p n t"),
-                ALU.mult,
+                slot_major(chunk(ds1_packed, c)), slot_major(chunk(squares[0], c)), gated_chunk(c), ALU.mult
             )
+
+        square_chunk(0, tanh_row)
+        square_chunk(1, do1_rows[:, 0, :])
+        nc.gpsimd.tensor_scalar(squares[0][:, 0 : 2 * N], squares[1][:, 0 : 2 * N], 1.0, -1.0, ALU.mult, ALU.add)
+        key_grad(banks[4], 0, 1)
+        place(0, 1, banks[4], stage[:, 1, :])
+        dp1_banks = banks[1:4] + banks[0:1]
+        for t in range(PACK):
+            product(dp1_banks[t][:], do_mx[1], E5M2, t, v_mx[1], E4M3)
+        key_grad(banks[4], 0, 2)
+        gate_dp(0)
+        multiply_on_gpsimd(0)
+        multiply_on_gpsimd(1)
+        square_chunk(2, tanh_row)
         place(0, 2, banks[4], stage[:, 2, :])
         key_grad(banks[4], 0, 3)
-        tanh_second = do1_rows[:, 2:4, :].rearrange("p a b -> p (a b)")
-        nc.scalar.activation(squares[1][:, 2 * N : 4 * N], tanh_second, ACT.Square)
+        nc.scalar.activation(chunk(squares[0], 2), square1[2], ACT.Copy, bias=-1.0)
         gate_dp(1)
+        multiply_on_gpsimd(2)
+        square_chunk(3, tanh_row)
+        nc.scalar.copy(*pack_views("p c j i", qm1_packed, qm1_rows, N - QM1_TAIL, N))
         nc.vector.scalar_tensor_tensor(
-            slot_major(ds1_packed[:, 2 * N : 4 * N]),
-            slot_major(squares[1][:, 2 * N : 4 * N]),
-            1.0,
-            gated[1].rearrange("p t n -> p n t"),
-            ALU.subtract,
-            ALU.mult,
+            slot_major(chunk(ds1_packed, 3)), slot_major(square1[3]), 1.0, gated_chunk(3), ALU.subtract, ALU.mult
         )
-        qm1_packed = tanh_second.bitcast(BF16)
-        pack(nc.scalar.copy, qm1_packed, qm1_rows)
         quantize(qm_mx[1], E4M3, qm1_packed)
         quantize(ds_mx[1], E5M2, ds1_packed)
 

@@ -214,7 +214,7 @@ def tile_attend_gat_tnh_k_kernel(tc, qT, kT, vT, doT, rw, qm, offs, out):
         quantize(q_mx[1], E4M3, q1_packed, HALF, N)
         quantize(qm_mx[0], E4M3, qm0_packed, HALF, N)
         pack(nc.scalar.copy, v1_packed, values1)
-        late = keep.tile([P, 3 * N], F32, name="late", align_bytes=64)
+        late = keep.tile([P, 4 * N], F32, name="late", align_bytes=64)
         do1_packed = late[:, 0 : 2 * N].bitcast(BF16)
         deal(do1_packed, do1_rows)
         place(0, 0, banks[0], stage[:, 0, :])
@@ -223,19 +223,17 @@ def tile_attend_gat_tnh_k_kernel(tc, qT, kT, vT, doT, rw, qm, offs, out):
         qm1_packed = late[:, 2 * QM1_TAIL : 2 * N + 2 * QM1_TAIL].bitcast(BF16)
         pack_gpsimd(qm1_packed, qm1_rows, 0, N - QM1_TAIL)
 
-        for c in range(N // P):
+        for c in range(2):
             for t in range(PACK):
                 product(banks[4 + c][:, t * P : (t + 1) * P], q_mx[1], E4M3, t, k_mx, E4M3, c * P, (c + 1) * P)
+        for t in range(PACK):
+            dst = banks[6 + t // 2][:, (t % 2) * HALF : (t % 2 + 1) * HALF]
+            product(dst, q_mx[1], E4M3, t, k_mx, E4M3, HALF, N)
 
         def chunk(x, c):
             return x[:, c * N : (c + 1) * N]
 
-        square1 = [chunk(squares[1], c) for c in range(PACK)]
-        tanh_row = late[:, 2 * N : 3 * N]
-
-        def square_chunk(c, tanh):
-            nc.scalar.activation(slot_major(tanh), banks[4 + c][:].rearrange("p (t n) -> p n t", t=PACK), ACT.Tanh)
-            nc.scalar.activation(square1[c], tanh, ACT.Square)
+        tanh_pair = do1_rows[:, 0:2, :].rearrange("p a b -> p (a b)")
 
         flat = do0_rows.rearrange("p a b -> p (a b)")
         gated = [flat[:, h * 2 * N : (h + 1) * 2 * N].rearrange("p (t n) -> p t n", t=PACK) for h in range(2)]
@@ -257,8 +255,11 @@ def tile_attend_gat_tnh_k_kernel(tc, qT, kT, vT, doT, rw, qm, offs, out):
                 slot_major(chunk(ds1_packed, c)), slot_major(chunk(squares[0], c)), gated_chunk(c), ALU.mult
             )
 
-        square_chunk(0, tanh_row)
-        square_chunk(1, do1_rows[:, 0, :])
+        for c in range(2):
+            nc.scalar.activation(
+                slot_major(chunk(tanh_pair, c)), banks[4 + c][:].rearrange("p (t n) -> p n t", t=PACK), ACT.Tanh
+            )
+        nc.scalar.activation(squares[1][:, 0 : 2 * N], tanh_pair, ACT.Square)
         nc.gpsimd.tensor_scalar(squares[0][:, 0 : 2 * N], squares[1][:, 0 : 2 * N], 1.0, -1.0, ALU.mult, ALU.add)
         key_grad(banks[4], 0, 1)
         place(0, 1, banks[4], stage[:, 1, :])
@@ -269,16 +270,20 @@ def tile_attend_gat_tnh_k_kernel(tc, qT, kT, vT, doT, rw, qm, offs, out):
         gate_dp(0)
         multiply_on_gpsimd(0)
         multiply_on_gpsimd(1)
-        square_chunk(2, tanh_row)
         place(0, 2, banks[4], stage[:, 2, :])
         key_grad(banks[4], 0, 3)
-        nc.scalar.activation(chunk(squares[0], 2), square1[2], ACT.Copy, bias=-1.0)
+        for c in range(2):
+            nc.scalar.activation(chunk(tanh_pair, c), banks[6 + c][:], ACT.Tanh)
+        nc.scalar.activation(late[:, 2 * N : 4 * N], tanh_pair, ACT.Square)
         gate_dp(1)
-        multiply_on_gpsimd(2)
-        square_chunk(3, tanh_row)
+        second = squares[1][:, 2 * N : 4 * N]
+        nc.scalar.activation(second, late[:, 2 * N : 4 * N], ACT.Copy, bias=-1.0)
         nc.scalar.copy(*pack_views("p c j i", qm1_packed, qm1_rows, N - QM1_TAIL, N))
-        nc.vector.scalar_tensor_tensor(
-            slot_major(chunk(ds1_packed, 3)), slot_major(square1[3]), 1.0, gated_chunk(3), ALU.subtract, ALU.mult
+        nc.vector.tensor_tensor(
+            ds1_packed[:, 2 * N : 4 * N].rearrange("p (c i t) -> p c t i", i=PACK, t=PACK),
+            second.rearrange("p (t c i) -> p c t i", i=PACK, t=PACK),
+            gated[1].rearrange("p t (c i) -> p c t i", i=PACK),
+            ALU.mult,
         )
         quantize(qm_mx[1], E4M3, qm1_packed)
         quantize(ds_mx[1], E5M2, ds1_packed)

@@ -21,7 +21,7 @@ PACK = 4
 QM1_TAIL = 128
 HALF = N // 2
 LIST_COLS = N // 16
-RAW_BUFS = 8
+RAW_BUFS = 7
 
 
 def tile_attend_gat_tnh_k_kernel(tc, qT, kT, vT, doT, rw, qm, offs, out):
@@ -113,7 +113,9 @@ def tile_attend_gat_tnh_k_kernel(tc, qT, kT, vT, doT, rw, qm, offs, out):
         for j in range(2):
             v_planes.append(v_last[:, j * T : (j + 1) * T])
             nc.sync.dma_start(out=v_planes[2 + j], in_=vT.rearrange("(p j) t -> p j t", j=PACK)[:, 2 + j, :])
-        do0_rows = load_rows(doT[0], "do0_rows")
+        values1_tile = keep.tile([P, 7 * N], F32, name="values1_tile", align_bytes=64)
+        do0_rows = values1_tile[:, 3 * N : 7 * N].rearrange("p (j w) -> p j w", j=PACK)
+        nc.sync.dma_start(out=do0_rows, in_=doT[0].rearrange("(p j) w -> p j w", j=PACK))
         q1_rows = load_rows(qT[1], "q1_rows")
         qm0_rows = load_rows(qm[0], "qm0_rows")
         do1_rows = load_rows(doT[1], "do1_rows")
@@ -128,7 +130,6 @@ def tile_attend_gat_tnh_k_kernel(tc, qT, kT, vT, doT, rw, qm, offs, out):
         keys = keep.tile([P, PACK, B * N], BF16, name="keys")
         cast_plane = keep.tile([P, T], BF16, name="cast_plane")
         stage = keep.tile([P, 3, N], F32, name="stage")
-        values1_tile = keep.tile([P, (PACK + 1) * N], F32, name="values1_tile", align_bytes=64)
         values0 = keep.tile([P, PACK, N], F32, name="values0")[:]
         values1 = values1_tile[:, 0 : PACK * N].rearrange("p (j n) -> p j n", j=PACK)
         pairs0 = packed_tile("pairs0")
@@ -137,74 +138,81 @@ def tile_attend_gat_tnh_k_kernel(tc, qT, kT, vT, doT, rw, qm, offs, out):
         k0_packed, q0_packed, q1_packed, v0_packed, v1_packed, ds0_packed, ds1_packed = (
             packed_tile(name + "_packed") for name in ("k0", "q0", "q1", "v0", "v1", "ds0", "ds1")
         )
-        do0_packed = values1_tile[:, 3 * N : 5 * N].bitcast(BF16)
-        k_mx = mx_tiles("k")
-        q_mx, v_mx, do_mx, qm_mx, ds_mx = (
-            [mx_tiles("%s%d" % (name, b)) for b in range(B)] for name in ("q", "v", "do", "qm", "ds")
+        do0_packed = packed_tile("do0_packed")
+        k_mx, q_mx, v_mx, do_mx, qm_mx, ds_mx = (
+            [mx_tiles("%s%d" % (name, b)) for b in range(B)] for name in ("k", "q", "v", "do", "qm", "ds")
         )
         banks = [psum.tile([P, N], F32, name="bank%d" % i) for i in range(8)]
         neg_gate = keep.tile([P, B, PACK], F32, name="neg_gate")
         nc.scalar.activation(neg_gate[:], gate[:], ACT.Copy, scale=-1.0)
 
-        for j in range(PACK - 1):
-            if j == 2:
-                nc.scalar.copy(cast_plane[:], k_planes[j])
-                for b in range(B):
-                    nc.scalar.activation(keys[:, j, b * N : (b + 1) * N], cast_plane[:].indirect(lists(b, b + 1)), ACT.Copy)
-            else:
-                gather(keys[:, j, :], k_planes[j], 0, B)
+        for j in range(2):
+            gather(keys[:, j, :], k_planes[j], 0, B)
+        nc.scalar.copy(cast_plane[:], k_planes[2])
+        nc.scalar.activation(keys[:, 2, 0:N], cast_plane[:].indirect(lists(0, 1)), ACT.Copy)
+        gather(keys[:, 2, N : 2 * N], k_planes[2], 1, 2)
         gather(keys[:, 3, 0:N], k_planes[3], 0, 1)
         gather(keys[:, 3, N : 2 * N], k_planes[3], 1, 2)
-        pack_gpsimd(k0_packed, keys[:, :, 0:N])
+        pack(nc.scalar.copy, k0_packed, keys[:, :, 0:N])
+        k1_packed = packed_tile("k1_packed")
+        pack_gpsimd(k1_packed, keys[:, :, N : 2 * N])
         deal(q0_packed, q0_rows)
         gather(pair_rows[:, 0, 0, :], v_planes[0], 0, 1)
         gather(values1[:, 0, :], v_planes[0], 1, 2)
-        quantize(k_mx, E4M3, k0_packed)
+        quantize(k_mx[0], E4M3, k0_packed)
+        quantize(k_mx[1], E4M3, k1_packed)
         quantize(q_mx[0], E4M3, q0_packed)
-        k1_packed = q0_packed
-        pack_gpsimd(k1_packed, keys[:, :, N : 2 * N])
 
         square0 = [squares[0][:, t * N : (t + 1) * N] for t in range(PACK)]
-        for t in range(PACK):
-            product(banks[t][:], q_mx[0], E4M3, t, k_mx, E4M3)
-            nc.scalar.activation(square0[t], banks[t][:], ACT.Tanh)
-        quantize(k_mx, E4M3, k1_packed)
-        for h in range(2):
-            pair = squares[0][:, h * 2 * N : (h + 1) * 2 * N]
-            nc.scalar.activation(pair, pair, ACT.Square)
-        after_k1 = k1_packed.bitcast(F32)
-        weight = [after_k1[:, 0:N], after_k1[:, N : 2 * N], do0_rows[:, 2, :], do0_rows[:, 3, :]]
-        for t in range(2):
+        after_q0 = q0_packed.bitcast(F32)
+        after_do0 = do0_packed.bitcast(F32)
+        weight = [after_q0[:, 0:N], after_q0[:, N : 2 * N], do0_rows[:, 2, :], after_do0[:, 0:N]]
+
+        def weigh(t):
             nc.gpsimd.tensor_scalar(
                 weight[t], square0[t], neg_gate[:, 0, t : t + 1], gate[:, 0, t : t + 1], ALU.mult, ALU.add
             )
+
+        for t in range(PACK):
+            product(banks[t][:], q_mx[0], E4M3, t, k_mx[0], E4M3)
+        for t in range(PACK):
+            nc.scalar.activation(square0[t], banks[t][:], ACT.Tanh)
+        for h in range(2):
+            pair = squares[0][:, h * 2 * N : (h + 1) * 2 * N]
+            nc.scalar.activation(pair, pair, ACT.Square)
+        for t in range(2):
+            weigh(t)
 
         gather(pair_rows[:, 0, 1, :], v_planes[1], 0, 1)
         gather(values1[:, 1, :], v_planes[1], 1, 2)
         gather(pair_rows[:, 1, 0, :], v_planes[2], 0, 1)
         gather(pair_rows[:, 1, 1, :], v_planes[3], 0, 1)
-        nc.vector.tensor_copy(
-            v0_packed.bitcast(I32).rearrange("p (c i u) -> p c u i", i=PACK, u=2),
-            pairs0.bitcast(I32).rearrange("p (u c i) -> p c u i", i=PACK, u=2),
-        )
+        for h in range(2):
+            runs = slice(h * HALF // PACK, (h + 1) * HALF // PACK)
+            nc.vector.tensor_copy(
+                v0_packed.bitcast(I32).rearrange("p (c i u) -> p c u i", i=PACK, u=2)[:, runs],
+                pairs0.bitcast(I32).rearrange("p (u c i) -> p c u i", i=PACK, u=2)[:, runs],
+            )
         gather(values1[:, 2, :], v_last[:], 1, 2)
         deal(do0_packed, do0_rows)
-        for t in range(2, PACK):
-            nc.scalar.activation(
-                weight[t], square0[t], ACT.Identity, bias=gate[:, 0, t : t + 1], scale=neg_gate[:, 0, t : t + 1]
-            )
-        quantize(v_mx[0], E4M3, v0_packed)
+        quantize(v_mx[0], E4M3, v0_packed, 0, HALF)
+        quantize(v_mx[0], E4M3, v0_packed, HALF, N)
         quantize(do_mx[0], E5M2, do0_packed)
         for t in range(PACK):
             product(banks[t][:], do_mx[0], E5M2, t, v_mx[0], E4M3)
         gather(values1[:, 3, :], v_planes[3], 1, 2)
+        nc.scalar.activation(weight[2], square0[2], ACT.Identity, bias=gate[:, 0, 2:3], scale=neg_gate[:, 0, 2:3])
+        weigh(3)
         qm0_packed = v0_packed
-        pack_gpsimd(qm0_packed, qm0_rows)
+        pack_gpsimd(qm0_packed, qm0_rows, 0, 448)
 
         ds0_rows = k0_packed
         for t in range(PACK):
             nc.vector.tensor_tensor(ds0_rows[:, t * N : (t + 1) * N], banks[t][:], weight[t], ALU.mult)
-        nc.vector.tensor_copy(slot_major(ds0_packed), ds0_rows.rearrange("p (t n) -> p n t", t=PACK))
+        nc.vector.tensor_copy(
+            ds0_packed.rearrange("p (c i t) -> p c t i", i=8, t=PACK),
+            ds0_rows.rearrange("p (t c i) -> p c t i", i=8, t=PACK),
+        )
         quantize(ds_mx[0], E5M2, ds0_packed)
 
         deal(q1_packed, q1_rows)
@@ -212,8 +220,9 @@ def tile_attend_gat_tnh_k_kernel(tc, qT, kT, vT, doT, rw, qm, offs, out):
         quantize(qm_mx[0], E4M3, qm0_packed, 0, HALF)
         key_grad(banks[0], 0, 0)
         quantize(q_mx[1], E4M3, q1_packed, HALF, N)
-        quantize(qm_mx[0], E4M3, qm0_packed, HALF, N)
         pack(nc.scalar.copy, v1_packed, values1)
+        nc.scalar.copy(*pack_views("p c j i", qm0_packed, qm0_rows, 448, N))
+        quantize(qm_mx[0], E4M3, qm0_packed, HALF, N)
         late = keep.tile([P, 4 * N], F32, name="late", align_bytes=64)
         do1_packed = late[:, 0 : 2 * N].bitcast(BF16)
         deal(do1_packed, do1_rows)
@@ -225,10 +234,10 @@ def tile_attend_gat_tnh_k_kernel(tc, qT, kT, vT, doT, rw, qm, offs, out):
 
         for c in range(2):
             for t in range(PACK):
-                product(banks[4 + c][:, t * P : (t + 1) * P], q_mx[1], E4M3, t, k_mx, E4M3, c * P, (c + 1) * P)
+                product(banks[4 + c][:, t * P : (t + 1) * P], q_mx[1], E4M3, t, k_mx[1], E4M3, c * P, (c + 1) * P)
         for t in range(PACK):
             dst = banks[6 + t // 2][:, (t % 2) * HALF : (t % 2 + 1) * HALF]
-            product(dst, q_mx[1], E4M3, t, k_mx, E4M3, HALF, N)
+            product(dst, q_mx[1], E4M3, t, k_mx[1], E4M3, HALF, N)
 
         def chunk(x, c):
             return x[:, c * N : (c + 1) * N]

@@ -107,7 +107,7 @@ def tile_attend_gat_tnh_k_kernel(tc, qT, kT, vT, doT, rw, qm, offs, out):
         v_planes = [load_plane(vT, "v_plane", 0)]
         q0_rows = load_rows(qT[0], "q0_rows")
         gate = keep.tile([P, B, PACK], F32, name="gate")
-        nc.scalar.dma_start(out=gate[:], in_=rw.rearrange("b (p t) o -> p b (t o)", t=PACK))
+        nc.sync.dma_start(out=gate[:], in_=rw.rearrange("b (p t) o -> p b (t o)", t=PACK))
         v_planes.append(load_plane(vT, "v_plane", 1))
         v_last = keep.tile([P, 2 * T], F32, name="v_last")
         for j in range(2):
@@ -148,7 +148,7 @@ def tile_attend_gat_tnh_k_kernel(tc, qT, kT, vT, doT, rw, qm, offs, out):
 
         for j in range(2):
             gather(keys[:, j, :], k_planes[j], 0, B)
-        nc.scalar.copy(cast_plane[:], k_planes[2])
+        nc.scalar.activation(cast_plane[:], k_planes[2], ACT.Copy)
         nc.scalar.activation(keys[:, 2, 0:N], cast_plane[:].indirect(lists(0, 1)), ACT.Copy)
         gather(keys[:, 2, N : 2 * N], k_planes[2], 1, 2)
         gather(keys[:, 3, 0:N], k_planes[3], 0, 1)

@@ -129,7 +129,7 @@ def tile_attend_gat_tnh_k_kernel(tc, qT, kT, vT, doT, rw, qm, offs, out):
 
         keys = keep.tile([P, PACK, B * N], BF16, name="keys")
         cast_plane = keep.tile([P, T], BF16, name="cast_plane")
-        stage = keep.tile([P, 3, N], F32, name="stage")
+        stage = keep.tile([P, 2, N], F32, name="stage")
         values0 = keep.tile([P, PACK, N], F32, name="values0")[:]
         values1 = values1_tile[:, 0 : PACK * N].rearrange("p (j n) -> p j n", j=PACK)
         pairs0 = packed_tile("pairs0")
@@ -223,32 +223,50 @@ def tile_attend_gat_tnh_k_kernel(tc, qT, kT, vT, doT, rw, qm, offs, out):
         pack(nc.scalar.copy, v1_packed, values1)
         nc.scalar.copy(*pack_views("p c j i", qm0_packed, qm0_rows, 448, N))
         quantize(qm_mx[0], E4M3, qm0_packed, HALF, N)
-        late = keep.tile([P, 4 * N], F32, name="late", align_bytes=64)
+        late_tile = keep.tile([P, 5 * N], F32, name="late", align_bytes=64)
+        last_factor = late_tile[:, 0:N]
+        late = late_tile[:, N : 5 * N]
         do1_packed = late[:, 0 : 2 * N].bitcast(BF16)
         deal(do1_packed, do1_rows)
-        place(0, 0, banks[0], stage[:, 0, :])
-        quantize(v_mx[1], E4M3, v1_packed)
-        quantize(do_mx[1], E5M2, do1_packed)
-        qm1_packed = late[:, 2 * QM1_TAIL : 2 * N + 2 * QM1_TAIL].bitcast(BF16)
-        pack_gpsimd(qm1_packed, qm1_rows, 0, N - QM1_TAIL)
-
-        for c in range(2):
+        for c in range(4):
             for t in range(PACK):
                 product(banks[4 + c][:, t * P : (t + 1) * P], q_mx[1], E4M3, t, k_mx[1], E4M3, c * P, (c + 1) * P)
-        for t in range(PACK):
-            dst = banks[6 + t // 2][:, (t % 2) * HALF : (t % 2 + 1) * HALF]
-            product(dst, q_mx[1], E4M3, t, k_mx[1], E4M3, HALF, N)
 
         def chunk(x, c):
             return x[:, c * N : (c + 1) * N]
 
         tanh_pair = do1_rows[:, 0:2, :].rearrange("p a b -> p (a b)")
 
+        def tanh_slot_major(c):
+            nc.scalar.activation(
+                slot_major(chunk(tanh_pair, c % 2)), banks[4 + c][:].rearrange("p (t n) -> p n t", t=PACK), ACT.Tanh
+            )
+
+        tanh_slot_major(0)
+        place(0, 0, banks[0], values0[:, 0, :])
+        quantize(v_mx[1], E4M3, v1_packed)
+        quantize(do_mx[1], E5M2, do1_packed)
+        qm1_halves = [late[:, N : 2 * N].bitcast(BF16), late_tile[:, N - P : 2 * N - P].bitcast(BF16)]
+
+        def qm1_views(order, lo, hi):
+            h = lo // HALF
+            return pack_views(order, qm1_halves[h], qm1_rows[:, :, h * HALF : (h + 1) * HALF], lo - h * HALF, hi - h * HALF)
+
+        for lo, hi in ((0, 96), (320, 512)):
+            nc.gpsimd.tensor_scalar(*qm1_views("p c i j", lo, hi), 1.0, 0.0, ALU.mult, ALU.add)
+
+        def quantize_qm1(lo, hi):
+            h = lo // HALF
+            codes, scales = qm_mx[1]
+            nc.vector.quantize_mx(
+                out=codes[:, lo:hi].bitcast(E4M3), scales=scales[:, lo:hi], in_=qm1_halves[h][:, (lo - h * HALF) * PACK : (hi - h * HALF) * PACK]
+            )
+
         flat = do0_rows.rearrange("p a b -> p (a b)")
         gated = [flat[:, h * 2 * N : (h + 1) * 2 * N].rearrange("p (t n) -> p t n", t=PACK) for h in range(2)]
 
-        def gate_dp(h):
-            for t in range(PACK):
+        def gate_dp(h, first=0, end=PACK):
+            for t in range(first, end):
                 nc.scalar.activation(
                     gated[h][:, t, :],
                     dp1_banks[t][:, h * HALF : (h + 1) * HALF],
@@ -256,51 +274,60 @@ def tile_attend_gat_tnh_k_kernel(tc, qT, kT, vT, doT, rw, qm, offs, out):
                     scale=neg_gate[:, 1, t : t + 1],
                 )
 
-        def gated_chunk(c):
-            return gated[c // 2][:, :, (c % 2) * P : (c % 2 + 1) * P].rearrange("p t n -> p n t")
-
-        def multiply_on_gpsimd(c):
+        def multiply_on_gpsimd(c, n):
             nc.gpsimd.tensor_tensor(
-                slot_major(chunk(ds1_packed, c)), slot_major(chunk(squares[0], c)), gated_chunk(c), ALU.mult
+                slot_major(chunk(ds1_packed, c))[:, 0:n],
+                slot_major(chunk(squares[0], c))[:, 0:n],
+                gated[c // 2][:, :, (c % 2) * P : (c % 2) * P + n].rearrange("p t n -> p n t"),
+                ALU.mult,
             )
 
-        for c in range(2):
-            nc.scalar.activation(
-                slot_major(chunk(tanh_pair, c)), banks[4 + c][:].rearrange("p (t n) -> p n t", t=PACK), ACT.Tanh
-            )
-        nc.scalar.activation(squares[1][:, 0 : 2 * N], tanh_pair, ACT.Square)
-        nc.gpsimd.tensor_scalar(squares[0][:, 0 : 2 * N], squares[1][:, 0 : 2 * N], 1.0, -1.0, ALU.mult, ALU.add)
         key_grad(banks[4], 0, 1)
-        place(0, 1, banks[4], stage[:, 1, :])
+        tanh_slot_major(1)
+        for c in range(2):
+            nc.scalar.activation(chunk(squares[1], c), chunk(tanh_pair, c), ACT.Square)
+        for c in range(2):
+            nc.gpsimd.tensor_scalar(chunk(squares[0], c), chunk(squares[1], c), 1.0, -1.0, ALU.mult, ALU.add)
         dp1_banks = banks[1:4] + banks[0:1]
         for t in range(PACK):
             product(dp1_banks[t][:], do_mx[1], E5M2, t, v_mx[1], E4M3)
-        key_grad(banks[4], 0, 2)
-        gate_dp(0)
-        multiply_on_gpsimd(0)
-        multiply_on_gpsimd(1)
-        place(0, 2, banks[4], stage[:, 2, :])
+        gate_dp(0, 0, 1)
+        place(0, 1, banks[4], stage[:, 0, :])
+        key_grad(banks[5], 0, 2)
         key_grad(banks[4], 0, 3)
-        for c in range(2):
-            nc.scalar.activation(chunk(tanh_pair, c), banks[6 + c][:], ACT.Tanh)
-        nc.scalar.activation(late[:, 2 * N : 4 * N], tanh_pair, ACT.Square)
+        gate_dp(0, 1, PACK)
+        multiply_on_gpsimd(0, P)
+        multiply_on_gpsimd(1, P)
+        tanh_slot_major(2)
+        nc.scalar.activation(chunk(tanh_pair, 1), banks[7][:], ACT.Tanh)
+        place(0, 2, banks[5], stage[:, 1, :])
+        for c in range(2, 4):
+            nc.scalar.activation(chunk(late, c), chunk(tanh_pair, c % 2), ACT.Square)
+        nc.scalar.activation(chunk(squares[0], 2), chunk(late, 2), ACT.Copy, bias=-1.0)
         gate_dp(1)
-        second = squares[1][:, 2 * N : 4 * N]
-        nc.scalar.activation(second, late[:, 2 * N : 4 * N], ACT.Copy, bias=-1.0)
-        nc.scalar.copy(*pack_views("p c j i", qm1_packed, qm1_rows, N - QM1_TAIL, N))
+        first_half = values0[:, 0, 0:HALF]
+        nc.scalar.copy(first_half, banks[4][:, 0:HALF])
+        nc.vector.tensor_copy(placed[3][:].indirect(offsets[:, 0 : LIST_COLS // 2]), first_half)
+        multiply_on_gpsimd(2, P)
+        nc.scalar.activation(last_factor, chunk(late, 3), ACT.Copy, bias=-1.0)
+        nc.scalar.copy(*qm1_views("p c j i", 96, HALF))
         nc.vector.tensor_tensor(
-            ds1_packed[:, 2 * N : 4 * N].rearrange("p (c i t) -> p c t i", i=PACK, t=PACK),
-            second.rearrange("p (t c i) -> p c t i", i=PACK, t=PACK),
-            gated[1].rearrange("p t (c i) -> p c t i", i=PACK),
+            ds1_packed[:, 3 * N : 4 * N].rearrange("p (c i t) -> p c t i", i=PACK, t=PACK),
+            last_factor.rearrange("p (t c i) -> p c t i", i=PACK, t=PACK),
+            gated[1][:, :, P : 2 * P].rearrange("p t (c i) -> p c t i", i=PACK),
             ALU.mult,
         )
-        quantize(qm_mx[1], E4M3, qm1_packed)
+        quantize_qm1(0, HALF)
         quantize(ds_mx[1], E5M2, ds1_packed)
+        nc.scalar.copy(*qm1_views("p c j i", 256, 320))
+        quantize_qm1(HALF, N)
 
         dk1_banks = banks[5:8] + banks[0:1]
         for j in range(D // P):
             key_grad(dk1_banks[j], 1, j)
-        place(0, 3, banks[4], squares[1][:, 3 * N : 4 * N])
+        second_half = last_factor[:, 0:HALF]
+        nc.scalar.copy(second_half, banks[4][:, HALF:N])
+        nc.vector.tensor_copy(placed[3][:].indirect(offsets[:, LIST_COLS // 2 : LIST_COLS]), second_half)
         for j in range(D // P):
             place(1, j, dk1_banks[j], values0[:, j, :])
             nc.sync.dma_start(out=out[j * P : (j + 1) * P, :], in_=placed[j][:])

@@ -102,8 +102,9 @@ def tile_attend_gat_tnh_k_kernel(tc, qT, kT, vT, doT, rw, qm, offs, out):
             return x.rearrange("p (n t) -> p n t", t=PACK)
 
         offsets = keep.tile([P, B * LIST_COLS], U16, name="offsets")
+        k_planes = [load_plane(kT, "k_plane", 0)]
         nc.sync.dma_start(offsets[:], offs)
-        k_planes = [load_plane(kT, "k_plane", j) for j in range(PACK)]
+        k_planes.extend(load_plane(kT, "k_plane", j) for j in range(1, PACK))
         v_planes = [load_plane(vT, "v_plane", 0)]
         q0_rows = load_rows(qT[0], "q0_rows")
         gate = keep.tile([P, B, PACK], F32, name="gate")
@@ -312,9 +313,9 @@ def tile_attend_gat_tnh_k_kernel(tc, qT, kT, vT, doT, rw, qm, offs, out):
         nc.scalar.activation(last_factor, chunk(late, 3), ACT.Copy, bias=-1.0)
         nc.scalar.copy(*qm1_views("p c j i", 96, HALF))
         nc.vector.tensor_tensor(
-            ds1_packed[:, 3 * N : 4 * N].rearrange("p (c i t) -> p c t i", i=PACK, t=PACK),
-            last_factor.rearrange("p (t c i) -> p c t i", i=PACK, t=PACK),
-            gated[1][:, :, P : 2 * P].rearrange("p t (c i) -> p c t i", i=PACK),
+            ds1_packed[:, 3 * N : 4 * N].rearrange("p (c i t) -> p c t i", i=8, t=PACK),
+            last_factor.rearrange("p (t c i) -> p c t i", i=8, t=PACK),
+            gated[1][:, :, P : 2 * P].rearrange("p t (c i) -> p c t i", i=8),
             ALU.mult,
         )
         quantize_qm1(0, HALF)

@@ -18,10 +18,11 @@ ALU = mybir.AluOpType
 
 P = 128
 PACK = 4
-QM1_TAIL = 128
+QM1_GPSIMD = 192
 HALF = N // 2
 LIST_COLS = N // 16
-RAW_BUFS = 7
+QM0_GPSIMD = 320
+RAW_BUFS = 8
 
 
 def tile_attend_gat_tnh_k_kernel(tc, qT, kT, vT, doT, rw, qm, offs, out):
@@ -105,17 +106,16 @@ def tile_attend_gat_tnh_k_kernel(tc, qT, kT, vT, doT, rw, qm, offs, out):
         k_planes = [load_plane(kT, "k_plane", 0)]
         nc.sync.dma_start(offsets[:], offs)
         k_planes.extend(load_plane(kT, "k_plane", j) for j in range(1, PACK))
-        v_planes = [load_plane(vT, "v_plane", 0)]
         q0_rows = load_rows(qT[0], "q0_rows")
+        v_planes = [load_plane(vT, "v_plane", j) for j in range(2)]
         gate = keep.tile([P, B, PACK], F32, name="gate")
         nc.sync.dma_start(out=gate[:], in_=rw.rearrange("b (p t) o -> p b (t o)", t=PACK))
-        v_planes.append(load_plane(vT, "v_plane", 1))
-        v_last = keep.tile([P, 2 * T], F32, name="v_last")
-        for j in range(2):
-            v_planes.append(v_last[:, j * T : (j + 1) * T])
-            nc.sync.dma_start(out=v_planes[2 + j], in_=vT.rearrange("(p j) t -> p j t", j=PACK)[:, 2 + j, :])
-        values1_tile = keep.tile([P, 7 * N], F32, name="values1_tile", align_bytes=64)
-        do0_rows = values1_tile[:, 3 * N : 7 * N].rearrange("p (j w) -> p j w", j=PACK)
+        v_planes.extend(load_plane(vT, "v_plane", j) for j in range(2, PACK))
+        shared = keep.tile([P, 6 * N], F32, name="shared", align_bytes=64)
+        q0_packed = shared[:, 0 : 2 * N].bitcast(BF16)
+        k1_packed = shared[:, HALF : 2 * N + HALF].bitcast(BF16)
+        do0_tile = shared[:, 2 * N : 6 * N]
+        do0_rows = do0_tile.rearrange("p (j w) -> p j w", j=PACK)
         nc.sync.dma_start(out=do0_rows, in_=doT[0].rearrange("(p j) w -> p j w", j=PACK))
         q1_rows = load_rows(qT[1], "q1_rows")
         qm0_rows = load_rows(qm[0], "qm0_rows")
@@ -128,84 +128,89 @@ def tile_attend_gat_tnh_k_kernel(tc, qT, kT, vT, doT, rw, qm, offs, out):
             nc.gpsimd.memset(tile[:], 0.0)
             placed.append(tile)
 
-        keys = keep.tile([P, PACK, B * N], BF16, name="keys")
-        cast_plane = keep.tile([P, T], BF16, name="cast_plane")
+        key_pairs = [packed_tile("key_pairs%d" % b) for b in range(B)]
+        cast_keys = keep.tile([P, T], BF16, name="cast_keys")
+        cast_values = keep.tile([P, T], BF16, name="cast_values")
+        rows1 = keep.tile([P, 2, N], BF16, name="rows1")
         stage = keep.tile([P, 2, N], F32, name="stage")
         values0 = keep.tile([P, PACK, N], F32, name="values0")[:]
-        values1 = values1_tile[:, 0 : PACK * N].rearrange("p (j n) -> p j n", j=PACK)
-        pairs0 = packed_tile("pairs0")
-        pair_rows = pairs0.rearrange("p (u n e) -> p u e n", u=2, e=2)
+        value_pairs = [packed_tile("value_pairs%d" % b) for b in range(B)]
+
+        def pair_row(pairs, j):
+            return pairs.rearrange("p (u n e) -> p u e n", u=2, e=2)[:, j // 2, j % 2, :]
+
+        def weave(copy, dt, dst, pairs, lo=0, hi=N):
+            runs = slice(lo // PACK, hi // PACK)
+            copy(
+                dst.bitcast(dt).rearrange("p (c i u) -> p c u i", i=PACK, u=2)[:, runs],
+                pairs.bitcast(dt).rearrange("p (u c i) -> p c u i", i=PACK, u=2)[:, runs],
+            )
+
         squares = [keep.tile([P, N * PACK], F32, name="squares%d" % b, align_bytes=64)[:] for b in range(B)]
-        k0_packed, q0_packed, q1_packed, v0_packed, v1_packed, ds0_packed, ds1_packed = (
-            packed_tile(name + "_packed") for name in ("k0", "q0", "q1", "v0", "v1", "ds0", "ds1")
+        k0_packed, q1_packed, v0_packed, ds0_packed, ds1_packed = (
+            packed_tile(name + "_packed") for name in ("k0", "q1", "v0", "ds0", "ds1")
         )
         do0_packed = packed_tile("do0_packed")
         k_mx, q_mx, v_mx, do_mx, qm_mx, ds_mx = (
             [mx_tiles("%s%d" % (name, b)) for b in range(B)] for name in ("k", "q", "v", "do", "qm", "ds")
         )
+        v_mx[1] = v_mx[0]
         banks = [psum.tile([P, N], F32, name="bank%d" % i) for i in range(8)]
         neg_gate = keep.tile([P, B, PACK], F32, name="neg_gate")
-        nc.scalar.activation(neg_gate[:], gate[:], ACT.Copy, scale=-1.0)
 
         for j in range(2):
-            gather(keys[:, j, :], k_planes[j], 0, B)
-        nc.scalar.activation(cast_plane[:], k_planes[2], ACT.Copy)
-        nc.scalar.activation(keys[:, 2, 0:N], cast_plane[:].indirect(lists(0, 1)), ACT.Copy)
-        gather(keys[:, 2, N : 2 * N], k_planes[2], 1, 2)
-        gather(keys[:, 3, 0:N], k_planes[3], 0, 1)
-        gather(keys[:, 3, N : 2 * N], k_planes[3], 1, 2)
-        pack(nc.scalar.copy, k0_packed, keys[:, :, 0:N])
-        k1_packed = packed_tile("k1_packed")
-        pack_gpsimd(k1_packed, keys[:, :, N : 2 * N])
+            nc.scalar.activation(cast_keys[:], k_planes[j], ACT.Copy)
+            nc.scalar.activation(pair_row(key_pairs[0], j), cast_keys[:].indirect(lists(0, 1)), ACT.Copy)
+            gather(pair_row(key_pairs[1], j), k_planes[j], 1, 2)
+        for j in range(2, PACK):
+            for b in range(B):
+                gather(pair_row(key_pairs[b], j), k_planes[j], b, b + 1)
         deal(q0_packed, q0_rows)
-        gather(pair_rows[:, 0, 0, :], v_planes[0], 0, 1)
-        gather(values1[:, 0, :], v_planes[0], 1, 2)
+        weave(nc.vector.tensor_copy, I32, k0_packed, key_pairs[0])
         quantize(k_mx[0], E4M3, k0_packed)
-        quantize(k_mx[1], E4M3, k1_packed)
         quantize(q_mx[0], E4M3, q0_packed)
+        nc.gpsimd.tensor_scalar(
+            k1_packed.rearrange("p (n u e) -> p n u e", u=2, e=2)[:, 0 : 3 * P],
+            key_pairs[1].rearrange("p (u n e) -> p n u e", u=2, e=2)[:, 0 : 3 * P], 1.0, 0.0, ALU.mult, ALU.add,
+        )
+        nc.scalar.activation(cast_values[:], v_planes[0], ACT.Copy)
+        nc.scalar.activation(rows1[:, 0, :], cast_values[:].indirect(lists(1, 2)), ACT.Copy)
+        gather(pair_row(value_pairs[0], 0), v_planes[0], 0, 1)
+        gather(rows1[:, 1, :], v_planes[1], 1, 2)
+        gather(pair_row(value_pairs[0], 1), v_planes[1], 0, 1)
+        nc.gpsimd.tensor_scalar(
+            value_pairs[1][:, 0 : 2 * N].rearrange("p (n e) -> p n e", e=2),
+            rows1[:].rearrange("p e n -> p n e"), 1.0, 0.0, ALU.mult, ALU.add,
+        )
+        nc.scalar.activation(neg_gate[:], gate[:], ACT.Copy, scale=-1.0)
 
-        square0 = [squares[0][:, t * N : (t + 1) * N] for t in range(PACK)]
-        after_q0 = q0_packed.bitcast(F32)
-        after_do0 = do0_packed.bitcast(F32)
-        weight = [after_q0[:, 0:N], after_q0[:, N : 2 * N], do0_rows[:, 2, :], after_do0[:, 0:N]]
-
-        def weigh(t):
-            nc.gpsimd.tensor_scalar(
-                weight[t], square0[t], neg_gate[:, 0, t : t + 1], gate[:, 0, t : t + 1], ALU.mult, ALU.add
-            )
-
+        weight = [squares[0][:, t * N : (t + 1) * N] for t in range(PACK)]
         for t in range(PACK):
             product(banks[t][:], q_mx[0], E4M3, t, k_mx[0], E4M3)
         for t in range(PACK):
-            nc.scalar.activation(square0[t], banks[t][:], ACT.Tanh)
-        for h in range(2):
-            pair = squares[0][:, h * 2 * N : (h + 1) * 2 * N]
-            nc.scalar.activation(pair, pair, ACT.Square)
-        for t in range(2):
-            weigh(t)
-
-        gather(pair_rows[:, 0, 1, :], v_planes[1], 0, 1)
-        gather(values1[:, 1, :], v_planes[1], 1, 2)
-        gather(pair_rows[:, 1, 0, :], v_planes[2], 0, 1)
-        gather(pair_rows[:, 1, 1, :], v_planes[3], 0, 1)
-        for h in range(2):
-            runs = slice(h * HALF // PACK, (h + 1) * HALF // PACK)
-            nc.vector.tensor_copy(
-                v0_packed.bitcast(I32).rearrange("p (c i u) -> p c u i", i=PACK, u=2)[:, runs],
-                pairs0.bitcast(I32).rearrange("p (u c i) -> p c u i", i=PACK, u=2)[:, runs],
+            nc.scalar.activation(weight[t], banks[t][:], ACT.Tanh)
+            nc.scalar.activation(weight[t], weight[t], ACT.Square)
+            nc.gpsimd.tensor_scalar(
+                weight[t], weight[t], neg_gate[:, 0, t : t + 1], gate[:, 0, t : t + 1], ALU.mult, ALU.add
             )
-        gather(values1[:, 2, :], v_last[:], 1, 2)
+
+        for j in range(2, PACK):
+            for b in range(B):
+                gather(pair_row(value_pairs[b], j), v_planes[j], b, b + 1)
+        for h in range(2):
+            weave(nc.vector.tensor_copy, I32, v0_packed, value_pairs[0], h * HALF, (h + 1) * HALF)
         deal(do0_packed, do0_rows)
         quantize(v_mx[0], E4M3, v0_packed, 0, HALF)
         quantize(v_mx[0], E4M3, v0_packed, HALF, N)
         quantize(do_mx[0], E5M2, do0_packed)
         for t in range(PACK):
             product(banks[t][:], do_mx[0], E5M2, t, v_mx[0], E4M3)
-        gather(values1[:, 3, :], v_planes[3], 1, 2)
-        nc.scalar.activation(weight[2], square0[2], ACT.Identity, bias=gate[:, 0, 2:3], scale=neg_gate[:, 0, 2:3])
-        weigh(3)
-        qm0_packed = v0_packed
-        pack_gpsimd(qm0_packed, qm0_rows, 0, 448)
+        weave(nc.scalar.copy, U32, k1_packed, key_pairs[1], 3 * P, N)
+        v1_packed = do0_tile[:, 2 * N : 4 * N].bitcast(BF16)
+        weave(nc.vector.tensor_copy, I32, v1_packed, value_pairs[1], 0, HALF)
+        quantize(k_mx[1], E4M3, k1_packed)
+        qm0_packed = k1_packed
+        pack_gpsimd(qm0_packed, qm0_rows, 0, QM0_GPSIMD)
 
         ds0_rows = k0_packed
         for t in range(PACK):
@@ -217,57 +222,53 @@ def tile_attend_gat_tnh_k_kernel(tc, qT, kT, vT, doT, rw, qm, offs, out):
         quantize(ds_mx[0], E5M2, ds0_packed)
 
         deal(q1_packed, q1_rows)
-        quantize(q_mx[1], E4M3, q1_packed, 0, HALF)
+        quantize(q_mx[1], E4M3, q1_packed)
         quantize(qm_mx[0], E4M3, qm0_packed, 0, HALF)
         key_grad(banks[0], 0, 0)
-        quantize(q_mx[1], E4M3, q1_packed, HALF, N)
-        pack(nc.scalar.copy, v1_packed, values1)
-        nc.scalar.copy(*pack_views("p c j i", qm0_packed, qm0_rows, 448, N))
+        weave(nc.scalar.copy, U32, v1_packed, value_pairs[1], HALF, N)
+        nc.scalar.copy(*pack_views("p c j i", qm0_packed, qm0_rows, QM0_GPSIMD, N))
         quantize(qm_mx[0], E4M3, qm0_packed, HALF, N)
-        late_tile = keep.tile([P, 5 * N], F32, name="late", align_bytes=64)
-        last_factor = late_tile[:, 0:N]
-        late = late_tile[:, N : 5 * N]
+        late = keep.tile([P, 3 * N + HALF], F32, name="late", align_bytes=64)
+        early_words = QM1_GPSIMD * 2
         do1_packed = late[:, 0 : 2 * N].bitcast(BF16)
+        last_factor = late[:, early_words : early_words + N]
+        low_start = early_words + N
+        qm1_halves = [late[:, low_start : low_start + N].bitcast(BF16), late[:, 0:N].bitcast(BF16)]
+        third_stage = late[:, low_start + early_words : low_start + early_words + N]
+        factor = [do0_tile[:, (c + 1) * N : (c + 2) * N] for c in range(3)] + [last_factor]
+
+        def qm1_views(order, h, lo, hi):
+            return pack_views(order, qm1_halves[h], qm1_rows[:, :, h * HALF : (h + 1) * HALF], lo, hi)
+
+        def quantize_qm1(h):
+            codes, scales = qm_mx[1]
+            cols = slice(h * HALF, (h + 1) * HALF)
+            nc.vector.quantize_mx(out=codes[:, cols].bitcast(E4M3), scales=scales[:, cols], in_=qm1_halves[h])
+
         deal(do1_packed, do1_rows)
         for c in range(4):
             for t in range(PACK):
                 product(banks[4 + c][:, t * P : (t + 1) * P], q_mx[1], E4M3, t, k_mx[1], E4M3, c * P, (c + 1) * P)
 
-        def chunk(x, c):
-            return x[:, c * N : (c + 1) * N]
-
-        tanh_pair = do1_rows[:, 0:2, :].rearrange("p a b -> p (a b)")
+        def chunk(x, c, end=None):
+            return x[:, c * N : (c + 1 if end is None else end) * N]
 
         def tanh_slot_major(c):
             nc.scalar.activation(
-                slot_major(chunk(tanh_pair, c % 2)), banks[4 + c][:].rearrange("p (t n) -> p n t", t=PACK), ACT.Tanh
+                slot_major(factor[c]), banks[4 + c][:].rearrange("p (t n) -> p n t", t=PACK), ACT.Tanh
             )
 
-        tanh_slot_major(0)
-        place(0, 0, banks[0], values0[:, 0, :])
-        quantize(v_mx[1], E4M3, v1_packed)
-        quantize(do_mx[1], E5M2, do1_packed)
-        qm1_halves = [late[:, N : 2 * N].bitcast(BF16), late_tile[:, N - P : 2 * N - P].bitcast(BF16)]
+        def place_half(j, h, bank, stage):
+            cols = slice(h * HALF, (h + 1) * HALF)
+            nc.scalar.copy(stage[:, cols], bank[:, cols])
+            half_list = offsets[:, h * LIST_COLS // 2 : (h + 1) * LIST_COLS // 2]
+            nc.vector.tensor_copy(placed[j][:].indirect(half_list), stage[:, cols])
 
-        def qm1_views(order, lo, hi):
-            h = lo // HALF
-            return pack_views(order, qm1_halves[h], qm1_rows[:, :, h * HALF : (h + 1) * HALF], lo - h * HALF, hi - h * HALF)
-
-        for lo, hi in ((0, 96), (320, 512)):
-            nc.gpsimd.tensor_scalar(*qm1_views("p c i j", lo, hi), 1.0, 0.0, ALU.mult, ALU.add)
-
-        def quantize_qm1(lo, hi):
-            h = lo // HALF
-            codes, scales = qm_mx[1]
-            nc.vector.quantize_mx(
-                out=codes[:, lo:hi].bitcast(E4M3), scales=scales[:, lo:hi], in_=qm1_halves[h][:, (lo - h * HALF) * PACK : (hi - h * HALF) * PACK]
-            )
-
-        flat = do0_rows.rearrange("p a b -> p (a b)")
+        flat = squares[1]
         gated = [flat[:, h * 2 * N : (h + 1) * 2 * N].rearrange("p (t n) -> p t n", t=PACK) for h in range(2)]
 
-        def gate_dp(h, first=0, end=PACK):
-            for t in range(first, end):
+        def gate_dp(h):
+            for t in range(PACK):
                 nc.scalar.activation(
                     gated[h][:, t, :],
                     dp1_banks[t][:, h * HALF : (h + 1) * HALF],
@@ -275,60 +276,62 @@ def tile_attend_gat_tnh_k_kernel(tc, qT, kT, vT, doT, rw, qm, offs, out):
                     scale=neg_gate[:, 1, t : t + 1],
                 )
 
-        def multiply_on_gpsimd(c, n):
+        def multiply_on_gpsimd(c):
             nc.gpsimd.tensor_tensor(
-                slot_major(chunk(ds1_packed, c))[:, 0:n],
-                slot_major(chunk(squares[0], c))[:, 0:n],
-                gated[c // 2][:, :, (c % 2) * P : (c % 2) * P + n].rearrange("p t n -> p n t"),
+                slot_major(chunk(ds1_packed, c)),
+                slot_major(factor[c]),
+                gated[c // 2][:, :, (c % 2) * P : (c % 2 + 1) * P].rearrange("p t n -> p n t"),
                 ALU.mult,
             )
 
-        key_grad(banks[4], 0, 1)
+        tanh_slot_major(0)
+        quantize(v_mx[1], E4M3, v1_packed)
+        quantize(do_mx[1], E5M2, do1_packed)
+        place(0, 0, banks[0], values0[:, 0, :])
         tanh_slot_major(1)
-        for c in range(2):
-            nc.scalar.activation(chunk(squares[1], c), chunk(tanh_pair, c), ACT.Square)
-        for c in range(2):
-            nc.gpsimd.tensor_scalar(chunk(squares[0], c), chunk(squares[1], c), 1.0, -1.0, ALU.mult, ALU.add)
+        for h in range(2):
+            nc.gpsimd.tensor_scalar(*qm1_views("p c i j", h, 0, QM1_GPSIMD), 1.0, 0.0, ALU.mult, ALU.add)
+        low = do0_tile[:, N : 3 * N]
+        nc.scalar.activation(low, low, ACT.Square)
+        nc.gpsimd.tensor_scalar(low, low, 1.0, -1.0, ALU.mult, ALU.add)
+        key_grad(banks[4], 0, 1)
         dp1_banks = banks[1:4] + banks[0:1]
         for t in range(PACK):
             product(dp1_banks[t][:], do_mx[1], E5M2, t, v_mx[1], E4M3)
-        gate_dp(0, 0, 1)
+        tanh_slot_major(2)
         place(0, 1, banks[4], stage[:, 0, :])
         key_grad(banks[5], 0, 2)
         key_grad(banks[4], 0, 3)
-        gate_dp(0, 1, PACK)
-        multiply_on_gpsimd(0, P)
-        multiply_on_gpsimd(1, P)
-        tanh_slot_major(2)
-        nc.scalar.activation(chunk(tanh_pair, 1), banks[7][:], ACT.Tanh)
-        place(0, 2, banks[5], stage[:, 1, :])
-        for c in range(2, 4):
-            nc.scalar.activation(chunk(late, c), chunk(tanh_pair, c % 2), ACT.Square)
-        nc.scalar.activation(chunk(squares[0], 2), chunk(late, 2), ACT.Copy, bias=-1.0)
+        gate_dp(0)
+        multiply_on_gpsimd(0)
+        multiply_on_gpsimd(1)
+
+        def square(c):
+            nc.scalar.activation(factor[c], factor[c], ACT.Square)
+
+        def less_one(c):
+            nc.scalar.activation(factor[c], factor[c], ACT.Copy, bias=-1.0)
+
+        tanh_slot_major(3)
+        square(2)
+        place(0, 2, banks[5], third_stage)
         gate_dp(1)
-        first_half = values0[:, 0, 0:HALF]
-        nc.scalar.copy(first_half, banks[4][:, 0:HALF])
-        nc.vector.tensor_copy(placed[3][:].indirect(offsets[:, 0 : LIST_COLS // 2]), first_half)
-        multiply_on_gpsimd(2, P)
-        nc.scalar.activation(last_factor, chunk(late, 3), ACT.Copy, bias=-1.0)
-        nc.scalar.copy(*qm1_views("p c j i", 96, HALF))
-        nc.vector.tensor_tensor(
-            ds1_packed[:, 3 * N : 4 * N].rearrange("p (c i t) -> p c t i", i=8, t=PACK),
-            last_factor.rearrange("p (t c i) -> p c t i", i=8, t=PACK),
-            gated[1][:, :, P : 2 * P].rearrange("p t (c i) -> p c t i", i=8),
-            ALU.mult,
-        )
-        quantize_qm1(0, HALF)
+        less_one(2)
+        multiply_on_gpsimd(2)
+        square(3)
+        place_half(3, 0, banks[4], stage[:, 1, :])
+        less_one(3)
+        multiply_on_gpsimd(3)
+        nc.scalar.copy(*qm1_views("p c j i", 0, QM1_GPSIMD, HALF))
+        quantize_qm1(0)
         quantize(ds_mx[1], E5M2, ds1_packed)
-        nc.scalar.copy(*qm1_views("p c j i", 256, 320))
-        quantize_qm1(HALF, N)
+        nc.scalar.copy(*qm1_views("p c j i", 1, QM1_GPSIMD, HALF))
+        quantize_qm1(1)
 
         dk1_banks = banks[5:8] + banks[0:1]
         for j in range(D // P):
             key_grad(dk1_banks[j], 1, j)
-        second_half = last_factor[:, 0:HALF]
-        nc.scalar.copy(second_half, banks[4][:, HALF:N])
-        nc.vector.tensor_copy(placed[3][:].indirect(offsets[:, LIST_COLS // 2 : LIST_COLS]), second_half)
+        place_half(3, 1, banks[4], factor[3])
         for j in range(D // P):
             place(1, j, dk1_banks[j], values0[:, j, :])
             nc.sync.dma_start(out=out[j * P : (j + 1) * P, :], in_=placed[j][:])

@@ -21,7 +21,8 @@ PACK = 4
 QM1_GPSIMD = 192
 HALF = N // 2
 LIST_COLS = N // 16
-QM0_GPSIMD = 320
+QM0_GPSIMD = 256
+DO0_VECTOR = 48
 RAW_BUFS = 8
 
 
@@ -69,9 +70,10 @@ def tile_attend_gat_tnh_k_kernel(tc, qT, kT, vT, doT, rw, qm, offs, out):
         def pack_gpsimd(dst, src, lo=0, hi=N):
             nc.gpsimd.tensor_scalar(*pack_views("p c i j", dst, src, lo, hi), 1.0, 0.0, ALU.mult, ALU.add)
 
-        def deal(dst, src):
-            nc.scalar.copy(
-                dst.rearrange("p (t m j) -> p m j t", t=PACK, j=PACK), src.rearrange("p j (m t) -> p m j t", t=PACK)
+        def deal(dst, src, copy=nc.scalar.copy, lo=0, hi=P):
+            copy(
+                dst.rearrange("p (t m j) -> p m j t", t=PACK, j=PACK)[:, lo:hi],
+                src.rearrange("p j (m t) -> p m j t", t=PACK)[:, lo:hi],
             )
 
         def quantize(mx, fmt, src, lo=0, hi=N):
@@ -111,10 +113,8 @@ def tile_attend_gat_tnh_k_kernel(tc, qT, kT, vT, doT, rw, qm, offs, out):
         gate = keep.tile([P, B, PACK], F32, name="gate")
         nc.sync.dma_start(out=gate[:], in_=rw.rearrange("b (p t) o -> p b (t o)", t=PACK))
         v_planes.extend(load_plane(vT, "v_plane", j) for j in range(2, PACK))
-        shared = keep.tile([P, 6 * N], F32, name="shared", align_bytes=64)
-        q0_packed = shared[:, 0 : 2 * N].bitcast(BF16)
-        k1_packed = shared[:, HALF : 2 * N + HALF].bitcast(BF16)
-        do0_tile = shared[:, 2 * N : 6 * N]
+        shared = keep.tile([P, 3 * HALF + PACK * N + N], F32, name="shared", align_bytes=64)
+        do0_tile = shared[:, 3 * HALF : 3 * HALF + PACK * N]
         do0_rows = do0_tile.rearrange("p (j w) -> p j w", j=PACK)
         nc.sync.dma_start(out=do0_rows, in_=doT[0].rearrange("(p j) w -> p j w", j=PACK))
         q1_rows = load_rows(qT[1], "q1_rows")
@@ -134,7 +134,7 @@ def tile_attend_gat_tnh_k_kernel(tc, qT, kT, vT, doT, rw, qm, offs, out):
         rows1 = keep.tile([P, 2, N], BF16, name="rows1")
         stage = keep.tile([P, 2, N], F32, name="stage")
         values0 = keep.tile([P, PACK, N], F32, name="values0")[:]
-        value_pairs = [packed_tile("value_pairs%d" % b) for b in range(B)]
+        value_pairs = [packed_tile("value_pairs0"), shared[:, 0 : 2 * N].bitcast(BF16)]
 
         def pair_row(pairs, j):
             return pairs.rearrange("p (u n e) -> p u e n", u=2, e=2)[:, j // 2, j % 2, :]
@@ -147,10 +147,11 @@ def tile_attend_gat_tnh_k_kernel(tc, qT, kT, vT, doT, rw, qm, offs, out):
             )
 
         squares = [keep.tile([P, N * PACK], F32, name="squares%d" % b, align_bytes=64)[:] for b in range(B)]
-        k0_packed, q1_packed, v0_packed, ds0_packed, ds1_packed = (
-            packed_tile(name + "_packed") for name in ("k0", "q1", "v0", "ds0", "ds1")
+        k0_packed, k1_packed, q0_packed, q1_packed, v0_packed, ds0_packed, ds1_packed = (
+            packed_tile(name + "_packed") for name in ("k0", "k1", "q0", "q1", "v0", "ds0", "ds1")
         )
-        do0_packed = packed_tile("do0_packed")
+        reused = keep.tile([P, 3 * N], F32, name="reused", align_bytes=64)
+        do0_packed = reused[:, N : 3 * N].bitcast(BF16)
         k_mx, q_mx, v_mx, do_mx, qm_mx, ds_mx = (
             [mx_tiles("%s%d" % (name, b)) for b in range(B)] for name in ("k", "q", "v", "do", "qm", "ds")
         )
@@ -167,12 +168,10 @@ def tile_attend_gat_tnh_k_kernel(tc, qT, kT, vT, doT, rw, qm, offs, out):
                 gather(pair_row(key_pairs[b], j), k_planes[j], b, b + 1)
         deal(q0_packed, q0_rows)
         weave(nc.vector.tensor_copy, I32, k0_packed, key_pairs[0])
+        weave(nc.vector.tensor_copy, I32, k1_packed, key_pairs[1])
         quantize(k_mx[0], E4M3, k0_packed)
+        quantize(k_mx[1], E4M3, k1_packed)
         quantize(q_mx[0], E4M3, q0_packed)
-        nc.gpsimd.tensor_scalar(
-            k1_packed.rearrange("p (n u e) -> p n u e", u=2, e=2)[:, 0 : 3 * P],
-            key_pairs[1].rearrange("p (u n e) -> p n u e", u=2, e=2)[:, 0 : 3 * P], 1.0, 0.0, ALU.mult, ALU.add,
-        )
         nc.scalar.activation(cast_values[:], v_planes[0], ACT.Copy)
         nc.scalar.activation(rows1[:, 0, :], cast_values[:].indirect(lists(1, 2)), ACT.Copy)
         gather(pair_row(value_pairs[0], 0), v_planes[0], 0, 1)
@@ -190,26 +189,41 @@ def tile_attend_gat_tnh_k_kernel(tc, qT, kT, vT, doT, rw, qm, offs, out):
         for t in range(PACK):
             nc.scalar.activation(weight[t], banks[t][:], ACT.Tanh)
             nc.scalar.activation(weight[t], weight[t], ACT.Square)
+        for t in range(PACK - 1):
             nc.gpsimd.tensor_scalar(
                 weight[t], weight[t], neg_gate[:, 0, t : t + 1], gate[:, 0, t : t + 1], ALU.mult, ALU.add
             )
 
+        def gather_half(j, h):
+            cols = slice(LIST_COLS + h * LIST_COLS // 2, LIST_COLS + (h + 1) * LIST_COLS // 2)
+            nc.vector.tensor_copy(
+                pair_row(value_pairs[1], j)[:, h * HALF : (h + 1) * HALF], v_planes[j].indirect(offsets[:, cols])
+            )
+
         for j in range(2, PACK):
-            for b in range(B):
-                gather(pair_row(value_pairs[b], j), v_planes[j], b, b + 1)
+            gather(pair_row(value_pairs[0], j), v_planes[j], 0, 1)
+            gather_half(j, 0)
         for h in range(2):
             weave(nc.vector.tensor_copy, I32, v0_packed, value_pairs[0], h * HALF, (h + 1) * HALF)
-        deal(do0_packed, do0_rows)
+        deal(do0_packed, do0_rows, nc.scalar.copy, DO0_VECTOR, P)
+        tail = 3 * HALF + 3 * N + HALF
+        last_weight = shared[:, tail : tail + N]
+        nc.scalar.activation(last_weight, weight[3], ACT.Identity, bias=gate[:, 0, 3:4], scale=neg_gate[:, 0, 3:4])
+        weight[3] = last_weight
         quantize(v_mx[0], E4M3, v0_packed, 0, HALF)
         quantize(v_mx[0], E4M3, v0_packed, HALF, N)
+        deal(do0_packed, do0_rows, nc.vector.tensor_copy, 0, DO0_VECTOR)
         quantize(do_mx[0], E5M2, do0_packed)
         for t in range(PACK):
             product(banks[t][:], do_mx[0], E5M2, t, v_mx[0], E4M3)
-        weave(nc.scalar.copy, U32, k1_packed, key_pairs[1], 3 * P, N)
-        v1_packed = do0_tile[:, 2 * N : 4 * N].bitcast(BF16)
-        weave(nc.vector.tensor_copy, I32, v1_packed, value_pairs[1], 0, HALF)
-        quantize(k_mx[1], E4M3, k1_packed)
-        qm0_packed = k1_packed
+        for j in range(2, PACK):
+            gather_half(j, 1)
+        v1_packed = do0_packed
+        nc.gpsimd.tensor_scalar(
+            v1_packed.rearrange("p (n u e) -> p n u e", u=2, e=2)[:, 0:HALF],
+            value_pairs[1].rearrange("p (u n e) -> p n u e", u=2, e=2)[:, 0:HALF], 1.0, 0.0, ALU.mult, ALU.add,
+        )
+        qm0_packed = v0_packed
         pack_gpsimd(qm0_packed, qm0_rows, 0, QM0_GPSIMD)
 
         ds0_rows = k0_packed
@@ -235,7 +249,7 @@ def tile_attend_gat_tnh_k_kernel(tc, qT, kT, vT, doT, rw, qm, offs, out):
         low_start = early_words + N
         qm1_halves = [late[:, low_start : low_start + N].bitcast(BF16), late[:, 0:N].bitcast(BF16)]
         third_stage = late[:, low_start + early_words : low_start + early_words + N]
-        factor = [do0_tile[:, (c + 1) * N : (c + 2) * N] for c in range(3)] + [last_factor]
+        factor = [reused[:, c * N : (c + 1) * N] for c in range(3)] + [last_factor]
 
         def qm1_views(order, h, lo, hi):
             return pack_views(order, qm1_halves[h], qm1_rows[:, :, h * HALF : (h + 1) * HALF], lo, hi)
@@ -291,14 +305,13 @@ def tile_attend_gat_tnh_k_kernel(tc, qT, kT, vT, doT, rw, qm, offs, out):
         tanh_slot_major(1)
         for h in range(2):
             nc.gpsimd.tensor_scalar(*qm1_views("p c i j", h, 0, QM1_GPSIMD), 1.0, 0.0, ALU.mult, ALU.add)
-        low = do0_tile[:, N : 3 * N]
-        nc.scalar.activation(low, low, ACT.Square)
-        nc.gpsimd.tensor_scalar(low, low, 1.0, -1.0, ALU.mult, ALU.add)
         key_grad(banks[4], 0, 1)
         dp1_banks = banks[1:4] + banks[0:1]
         for t in range(PACK):
             product(dp1_banks[t][:], do_mx[1], E5M2, t, v_mx[1], E4M3)
-        tanh_slot_major(2)
+        low = reused[:, 0 : 2 * N]
+        nc.scalar.activation(low, low, ACT.Square)
+        nc.gpsimd.tensor_scalar(low, low, 1.0, -1.0, ALU.mult, ALU.add)
         place(0, 1, banks[4], stage[:, 0, :])
         key_grad(banks[5], 0, 2)
         key_grad(banks[4], 0, 3)
@@ -312,6 +325,7 @@ def tile_attend_gat_tnh_k_kernel(tc, qT, kT, vT, doT, rw, qm, offs, out):
         def less_one(c):
             nc.scalar.activation(factor[c], factor[c], ACT.Copy, bias=-1.0)
 
+        tanh_slot_major(2)
         tanh_slot_major(3)
         square(2)
         place(0, 2, banks[5], third_stage)

@@ -18,7 +18,8 @@ ALU = mybir.AluOpType
 
 P = 128
 PACK = 4
-QM1_GPSIMD = 192
+QM1_GPSIMD = (0, 192)
+LAST_GPSIMD = 128
 HALF = N // 2
 LIST_COLS = N // 16
 QM0_GPSIMD = 256
@@ -242,13 +243,12 @@ def tile_attend_gat_tnh_k_kernel(tc, qT, kT, vT, doT, rw, qm, offs, out):
         weave(nc.scalar.copy, U32, v1_packed, value_pairs[1], HALF, N)
         nc.scalar.copy(*pack_views("p c j i", qm0_packed, qm0_rows, QM0_GPSIMD, N))
         quantize(qm_mx[0], E4M3, qm0_packed, HALF, N)
-        late = keep.tile([P, 3 * N + HALF], F32, name="late", align_bytes=64)
-        early_words = QM1_GPSIMD * 2
+        late = keep.tile([P, 2 * N], F32, name="late", align_bytes=64)
+        early_words = QM1_GPSIMD[1] * 2
         do1_packed = late[:, 0 : 2 * N].bitcast(BF16)
         last_factor = late[:, early_words : early_words + N]
-        low_start = early_words + N
-        qm1_halves = [late[:, low_start : low_start + N].bitcast(BF16), late[:, 0:N].bitcast(BF16)]
-        third_stage = late[:, low_start + early_words : low_start + early_words + N]
+        third_stage = keep.tile([P, N], F32, name="third_stage", align_bytes=64)[:]
+        qm1_halves = [third_stage.bitcast(BF16), late[:, 0:N].bitcast(BF16)]
         factor = [reused[:, c * N : (c + 1) * N] for c in range(3)] + [last_factor]
 
         def qm1_views(order, h, lo, hi):
@@ -290,11 +290,11 @@ def tile_attend_gat_tnh_k_kernel(tc, qT, kT, vT, doT, rw, qm, offs, out):
                     scale=neg_gate[:, 1, t : t + 1],
                 )
 
-        def multiply_on_gpsimd(c):
-            nc.gpsimd.tensor_tensor(
-                slot_major(chunk(ds1_packed, c)),
-                slot_major(factor[c]),
-                gated[c // 2][:, :, (c % 2) * P : (c % 2 + 1) * P].rearrange("p t n -> p n t"),
+        def multiply(engine, c, lo=0, hi=P):
+            engine.tensor_tensor(
+                slot_major(chunk(ds1_packed, c))[:, lo:hi],
+                slot_major(factor[c])[:, lo:hi],
+                gated[c // 2][:, :, (c % 2) * P + lo : (c % 2) * P + hi].rearrange("p t n -> p n t"),
                 ALU.mult,
             )
 
@@ -303,21 +303,19 @@ def tile_attend_gat_tnh_k_kernel(tc, qT, kT, vT, doT, rw, qm, offs, out):
         quantize(do_mx[1], E5M2, do1_packed)
         place(0, 0, banks[0], values0[:, 0, :])
         tanh_slot_major(1)
-        for h in range(2):
-            nc.gpsimd.tensor_scalar(*qm1_views("p c i j", h, 0, QM1_GPSIMD), 1.0, 0.0, ALU.mult, ALU.add)
-        key_grad(banks[4], 0, 1)
+        nc.gpsimd.tensor_scalar(*qm1_views("p c i j", 1, 0, QM1_GPSIMD[1]), 1.0, 0.0, ALU.mult, ALU.add)
         dp1_banks = banks[1:4] + banks[0:1]
         for t in range(PACK):
             product(dp1_banks[t][:], do_mx[1], E5M2, t, v_mx[1], E4M3)
+        key_grad(banks[4], 0, 1)
         low = reused[:, 0 : 2 * N]
         nc.scalar.activation(low, low, ACT.Square)
         nc.gpsimd.tensor_scalar(low, low, 1.0, -1.0, ALU.mult, ALU.add)
         place(0, 1, banks[4], stage[:, 0, :])
         key_grad(banks[5], 0, 2)
-        key_grad(banks[4], 0, 3)
         gate_dp(0)
-        multiply_on_gpsimd(0)
-        multiply_on_gpsimd(1)
+        multiply(nc.gpsimd, 0)
+        multiply(nc.gpsimd, 1)
 
         def square(c):
             nc.scalar.activation(factor[c], factor[c], ACT.Square)
@@ -329,23 +327,24 @@ def tile_attend_gat_tnh_k_kernel(tc, qT, kT, vT, doT, rw, qm, offs, out):
         tanh_slot_major(3)
         square(2)
         place(0, 2, banks[5], third_stage)
+        key_grad(banks[5], 0, 3)
         gate_dp(1)
         less_one(2)
-        multiply_on_gpsimd(2)
+        multiply(nc.gpsimd, 2)
         square(3)
-        place_half(3, 0, banks[4], stage[:, 1, :])
+        place_half(3, 0, banks[5], stage[:, 1, :])
         less_one(3)
-        multiply_on_gpsimd(3)
-        nc.scalar.copy(*qm1_views("p c j i", 0, QM1_GPSIMD, HALF))
+        multiply(nc.gpsimd, 3, 0, LAST_GPSIMD)
+        nc.scalar.copy(*qm1_views("p c j i", 0, QM1_GPSIMD[0], HALF))
         quantize_qm1(0)
         quantize(ds_mx[1], E5M2, ds1_packed)
-        nc.scalar.copy(*qm1_views("p c j i", 1, QM1_GPSIMD, HALF))
+        nc.scalar.copy(*qm1_views("p c j i", 1, QM1_GPSIMD[1], HALF))
         quantize_qm1(1)
 
-        dk1_banks = banks[5:8] + banks[0:1]
+        dk1_banks = [banks[4], banks[6], banks[7], banks[0]]
         for j in range(D // P):
             key_grad(dk1_banks[j], 1, j)
-        place_half(3, 1, banks[4], factor[3])
+        place_half(3, 1, banks[5], factor[3])
         for j in range(D // P):
             place(1, j, dk1_banks[j], values0[:, j, :])
             nc.sync.dma_start(out=out[j * P : (j + 1) * P, :], in_=placed[j][:])

@@ -24,6 +24,7 @@ HALF = N // 2
 LIST_COLS = N // 16
 QM0_GPSIMD = 256
 DO0_VECTOR = 48
+DO1_VECTOR = 32
 RAW_BUFS = 8
 
 
@@ -259,7 +260,8 @@ def tile_attend_gat_tnh_k_kernel(tc, qT, kT, vT, doT, rw, qm, offs, out):
             cols = slice(h * HALF, (h + 1) * HALF)
             nc.vector.quantize_mx(out=codes[:, cols].bitcast(E4M3), scales=scales[:, cols], in_=qm1_halves[h])
 
-        deal(do1_packed, do1_rows)
+        deal(do1_packed, do1_rows, nc.scalar.copy, DO1_VECTOR, P)
+        deal(do1_packed, do1_rows, nc.vector.tensor_copy, 0, DO1_VECTOR)
         for c in range(4):
             for t in range(PACK):
                 product(banks[4 + c][:, t * P : (t + 1) * P], q_mx[1], E4M3, t, k_mx[1], E4M3, c * P, (c + 1) * P)
@@ -304,10 +306,10 @@ def tile_attend_gat_tnh_k_kernel(tc, qT, kT, vT, doT, rw, qm, offs, out):
         place(0, 0, banks[0], values0[:, 0, :])
         tanh_slot_major(1)
         nc.gpsimd.tensor_scalar(*qm1_views("p c i j", 1, 0, QM1_GPSIMD[1]), 1.0, 0.0, ALU.mult, ALU.add)
+        key_grad(banks[4], 0, 1)
         dp1_banks = banks[1:4] + banks[0:1]
         for t in range(PACK):
             product(dp1_banks[t][:], do_mx[1], E5M2, t, v_mx[1], E4M3)
-        key_grad(banks[4], 0, 1)
         low = reused[:, 0 : 2 * N]
         nc.scalar.activation(low, low, ACT.Square)
         nc.gpsimd.tensor_scalar(low, low, 1.0, -1.0, ALU.mult, ALU.add)

@@ -22,9 +22,9 @@ QM1_GPSIMD = (0, 192)
 LAST_GPSIMD = 128
 HALF = N // 2
 LIST_COLS = N // 16
-QM0_GPSIMD = 256
+QM0_GPSIMD = 192
 DO0_VECTOR = 48
-DO1_VECTOR = 32
+DO1_VECTOR = 24
 RAW_BUFS = 8
 
 
@@ -152,8 +152,8 @@ def tile_attend_gat_tnh_k_kernel(tc, qT, kT, vT, doT, rw, qm, offs, out):
         k0_packed, k1_packed, q0_packed, q1_packed, v0_packed, ds0_packed, ds1_packed = (
             packed_tile(name + "_packed") for name in ("k0", "k1", "q0", "q1", "v0", "ds0", "ds1")
         )
-        reused = keep.tile([P, 3 * N], F32, name="reused", align_bytes=64)
-        do0_packed = reused[:, N : 3 * N].bitcast(BF16)
+        reused = keep.tile([P, 2 * N], F32, name="reused", align_bytes=64)
+        do0_packed = reused[:].bitcast(BF16)
         k_mx, q_mx, v_mx, do_mx, qm_mx, ds_mx = (
             [mx_tiles("%s%d" % (name, b)) for b in range(B)] for name in ("k", "q", "v", "do", "qm", "ds")
         )
@@ -238,19 +238,21 @@ def tile_attend_gat_tnh_k_kernel(tc, qT, kT, vT, doT, rw, qm, offs, out):
         quantize(ds_mx[0], E5M2, ds0_packed)
 
         deal(q1_packed, q1_rows)
-        quantize(q_mx[1], E4M3, q1_packed)
-        quantize(qm_mx[0], E4M3, qm0_packed, 0, HALF)
-        key_grad(banks[0], 0, 0)
+        quantize(q_mx[1], E4M3, q1_packed, 0, HALF)
         weave(nc.scalar.copy, U32, v1_packed, value_pairs[1], HALF, N)
         nc.scalar.copy(*pack_views("p c j i", qm0_packed, qm0_rows, QM0_GPSIMD, N))
+        quantize(qm_mx[0], E4M3, qm0_packed, 0, HALF)
+        key_grad(banks[0], 0, 0)
+        quantize(q_mx[1], E4M3, q1_packed, HALF, N)
         quantize(qm_mx[0], E4M3, qm0_packed, HALF, N)
-        late = keep.tile([P, 2 * N], F32, name="late", align_bytes=64)
+        late = keep.tile([P, 3 * N], F32, name="late", align_bytes=64)
         early_words = QM1_GPSIMD[1] * 2
         do1_packed = late[:, 0 : 2 * N].bitcast(BF16)
         last_factor = late[:, early_words : early_words + N]
-        third_stage = keep.tile([P, N], F32, name="third_stage", align_bytes=64)[:]
-        qm1_halves = [third_stage.bitcast(BF16), late[:, 0:N].bitcast(BF16)]
-        factor = [reused[:, c * N : (c + 1) * N] for c in range(3)] + [last_factor]
+        spare = keep.tile([P, 2 * N], F32, name="spare", align_bytes=64)
+        third_stage, last_square = spare[:, 0:N], spare[:, N : 2 * N]
+        qm1_halves = [spare[:, HALF : N + HALF].bitcast(BF16), late[:, 0:N].bitcast(BF16)]
+        factor = [reused[:, 0:N], reused[:, N : 2 * N], late[:, early_words + N : early_words + 2 * N], last_factor]
 
         def qm1_views(order, h, lo, hi):
             return pack_views(order, qm1_halves[h], qm1_rows[:, :, h * HALF : (h + 1) * HALF], lo, hi)
@@ -300,19 +302,19 @@ def tile_attend_gat_tnh_k_kernel(tc, qT, kT, vT, doT, rw, qm, offs, out):
                 ALU.mult,
             )
 
-        tanh_slot_major(0)
         quantize(v_mx[1], E4M3, v1_packed)
         quantize(do_mx[1], E5M2, do1_packed)
         place(0, 0, banks[0], values0[:, 0, :])
+        tanh_slot_major(0)
         tanh_slot_major(1)
         nc.gpsimd.tensor_scalar(*qm1_views("p c i j", 1, 0, QM1_GPSIMD[1]), 1.0, 0.0, ALU.mult, ALU.add)
         key_grad(banks[4], 0, 1)
         dp1_banks = banks[1:4] + banks[0:1]
         for t in range(PACK):
             product(dp1_banks[t][:], do_mx[1], E5M2, t, v_mx[1], E4M3)
-        low = reused[:, 0 : 2 * N]
-        nc.scalar.activation(low, low, ACT.Square)
-        nc.gpsimd.tensor_scalar(low, low, 1.0, -1.0, ALU.mult, ALU.add)
+        for c in range(2):
+            nc.scalar.activation(factor[c], factor[c], ACT.Square)
+            nc.gpsimd.tensor_scalar(factor[c], factor[c], 1.0, -1.0, ALU.mult, ALU.add)
         place(0, 1, banks[4], stage[:, 0, :])
         key_grad(banks[5], 0, 2)
         gate_dp(0)
@@ -326,17 +328,20 @@ def tile_attend_gat_tnh_k_kernel(tc, qT, kT, vT, doT, rw, qm, offs, out):
             nc.scalar.activation(factor[c], factor[c], ACT.Copy, bias=-1.0)
 
         tanh_slot_major(2)
-        tanh_slot_major(3)
-        square(2)
         place(0, 2, banks[5], third_stage)
         key_grad(banks[5], 0, 3)
+        square(2)
         gate_dp(1)
         less_one(2)
         multiply(nc.gpsimd, 2)
-        square(3)
+        tanh_slot_major(3)
         place_half(3, 0, banks[5], stage[:, 1, :])
-        less_one(3)
-        multiply(nc.gpsimd, 3, 0, LAST_GPSIMD)
+        halves = [slice(h * HALF, (h + 1) * HALF) for h in range(2)]
+        for cols in halves:
+            nc.scalar.activation(last_square[:, cols], factor[3][:, cols], ACT.Square)
+        for h, cols in enumerate(halves):
+            nc.scalar.activation(factor[3][:, cols], last_square[:, cols], ACT.Copy, bias=-1.0)
+            multiply(nc.gpsimd, 3, h * P // 2, (h + 1) * P // 2)
         nc.scalar.copy(*qm1_views("p c j i", 0, QM1_GPSIMD[0], HALF))
         quantize_qm1(0)
         quantize(ds_mx[1], E5M2, ds1_packed)

@@ -18,14 +18,14 @@ ALU = mybir.AluOpType
 
 P = 128
 PACK = 4
-QM1_GPSIMD = (0, 192)
-LAST_GPSIMD = 128
 HALF = N // 2
 LIST_COLS = N // 16
-QM0_GPSIMD = 192
-DO0_VECTOR = 48
-DO1_VECTOR = 24
+RUN = 8
 RAW_BUFS = 8
+DO0_VECTOR = 56
+DO1_VECTOR = 24
+QM0_GPSIMD = 192
+QM1_GPSIMD = 192
 
 
 def tile_attend_gat_tnh_k_kernel(tc, qT, kT, vT, doT, rw, qm, offs, out):
@@ -53,11 +53,32 @@ def tile_attend_gat_tnh_k_kernel(tc, qT, kT, vT, doT, rw, qm, offs, out):
             scales = keep.tile([P, N], U8, name=name + "_scales", align_bytes=64)
             return codes, scales
 
-        def lists(first, end):
-            return offsets[:, first * LIST_COLS : end * LIST_COLS]
+        def whole_list(b):
+            return offsets[:, b * LIST_COLS : (b + 1) * LIST_COLS]
 
-        def gather(dst, window, first, end):
-            nc.vector.tensor_copy(dst, window.indirect(lists(first, end)))
+        def half_list(b, h):
+            first = b * LIST_COLS + h * LIST_COLS // 2
+            return offsets[:, first : first + LIST_COLS // 2]
+
+        def gather(dst, window, entries):
+            nc.vector.tensor_copy(dst, window.indirect(entries))
+
+        def gather_on_scalar(dst, cast, plane, entries):
+            nc.scalar.activation(cast[:], plane, ACT.Copy)
+            nc.scalar.activation(dst, cast[:].indirect(entries), ACT.Copy)
+
+        def move_on_gpsimd(dst, src):
+            nc.gpsimd.tensor_scalar(dst, src, 1.0, 0.0, ALU.mult, ALU.add)
+
+        def pair_row(pairs, j):
+            return pairs.rearrange("p (u n e) -> p u e n", u=2, e=2)[:, j // 2, j % 2, :]
+
+        def weave(copy, word, dst, pairs, lo=0, hi=N):
+            runs = slice(lo // PACK, hi // PACK)
+            copy(
+                dst.bitcast(word).rearrange("p (c i u) -> p c u i", i=PACK, u=2)[:, runs],
+                pairs.bitcast(word).rearrange("p (u c i) -> p c u i", i=PACK, u=2)[:, runs],
+            )
 
         def pack_views(order, dst, src, lo, hi):
             cs = slice(lo // PACK, hi // PACK)
@@ -66,23 +87,24 @@ def tile_attend_gat_tnh_k_kernel(tc, qT, kT, vT, doT, rw, qm, offs, out):
                 src.rearrange("p j (c i) -> " + order, i=PACK)[:, cs],
             )
 
-        def pack(copy, dst, src):
-            copy(*pack_views("p c j i", dst, src, 0, N))
+        def pack_on_scalar(dst, src, lo, hi):
+            nc.scalar.copy(*pack_views("p c j i", dst, src, lo, hi))
 
-        def pack_gpsimd(dst, src, lo=0, hi=N):
-            nc.gpsimd.tensor_scalar(*pack_views("p c i j", dst, src, lo, hi), 1.0, 0.0, ALU.mult, ALU.add)
+        def pack_on_gpsimd(dst, src, lo, hi):
+            move_on_gpsimd(*pack_views("p c i j", dst, src, lo, hi))
 
-        def deal(dst, src, copy=nc.scalar.copy, lo=0, hi=P):
+        def deal(copy, dst, src, lo=0, hi=P):
             copy(
                 dst.rearrange("p (t m j) -> p m j t", t=PACK, j=PACK)[:, lo:hi],
                 src.rearrange("p j (m t) -> p m j t", t=PACK)[:, lo:hi],
             )
 
-        def quantize(mx, fmt, src, lo=0, hi=N):
+        def quantize_into(mx, fmt, lo, hi, src):
             codes, scales = mx
-            nc.vector.quantize_mx(
-                out=codes[:, lo:hi].bitcast(fmt), scales=scales[:, lo:hi], in_=src[:, lo * PACK : hi * PACK]
-            )
+            nc.vector.quantize_mx(out=codes[:, lo:hi].bitcast(fmt), scales=scales[:, lo:hi], in_=src)
+
+        def quantize(mx, fmt, packed, lo=0, hi=N):
+            quantize_into(mx, fmt, lo, hi, packed[:, lo * PACK : hi * PACK])
 
         def product(dst, left, left_fmt, block, right, right_fmt, lo=0, hi=N):
             cols = slice(block * P, (block + 1) * P)
@@ -99,9 +121,9 @@ def tile_attend_gat_tnh_k_kernel(tc, qT, kT, vT, doT, rw, qm, offs, out):
         def key_grad(bank, b, j):
             product(bank[:], qm_mx[b], E4M3, j, ds_mx[b], E5M2)
 
-        def place(b, j, bank, stage):
-            nc.scalar.copy(stage, bank[:])
-            nc.vector.tensor_copy(placed[j][:].indirect(lists(b, b + 1)), stage)
+        def place(j, entries, source, stage):
+            nc.scalar.copy(stage, source)
+            nc.vector.tensor_copy(placed[j][:].indirect(entries), stage)
 
         def slot_major(x):
             return x.rearrange("p (n t) -> p n t", t=PACK)
@@ -115,9 +137,11 @@ def tile_attend_gat_tnh_k_kernel(tc, qT, kT, vT, doT, rw, qm, offs, out):
         gate = keep.tile([P, B, PACK], F32, name="gate")
         nc.sync.dma_start(out=gate[:], in_=rw.rearrange("b (p t) o -> p b (t o)", t=PACK))
         v_planes.extend(load_plane(vT, "v_plane", j) for j in range(2, PACK))
-        shared = keep.tile([P, 3 * HALF + PACK * N + N], F32, name="shared", align_bytes=64)
-        do0_tile = shared[:, 3 * HALF : 3 * HALF + PACK * N]
-        do0_rows = do0_tile.rearrange("p (j w) -> p j w", j=PACK)
+        do0_start = 2 * N - HALF
+        do0_end = do0_start + PACK * N
+        around_do0 = keep.tile([P, do0_end + N], F32, name="around_do0", align_bytes=64)
+        do0_rows = around_do0[:, do0_start:do0_end].rearrange("p (j w) -> p j w", j=PACK)
+        last_weight = around_do0[:, do0_end - HALF : do0_end + HALF]
         nc.sync.dma_start(out=do0_rows, in_=doT[0].rearrange("(p j) w -> p j w", j=PACK))
         q1_rows = load_rows(qT[1], "q1_rows")
         qm0_rows = load_rows(qm[0], "qm0_rows")
@@ -133,157 +157,137 @@ def tile_attend_gat_tnh_k_kernel(tc, qT, kT, vT, doT, rw, qm, offs, out):
         key_pairs = [packed_tile("key_pairs%d" % b) for b in range(B)]
         cast_keys = keep.tile([P, T], BF16, name="cast_keys")
         cast_values = keep.tile([P, T], BF16, name="cast_values")
-        rows1 = keep.tile([P, 2, N], BF16, name="rows1")
+        value_rows = keep.tile([P, 2, N], BF16, name="value_rows")
         stage = keep.tile([P, 2, N], F32, name="stage")
-        values0 = keep.tile([P, PACK, N], F32, name="values0")[:]
-        value_pairs = [packed_tile("value_pairs0"), shared[:, 0 : 2 * N].bitcast(BF16)]
-
-        def pair_row(pairs, j):
-            return pairs.rearrange("p (u n e) -> p u e n", u=2, e=2)[:, j // 2, j % 2, :]
-
-        def weave(copy, dt, dst, pairs, lo=0, hi=N):
-            runs = slice(lo // PACK, hi // PACK)
-            copy(
-                dst.bitcast(dt).rearrange("p (c i u) -> p c u i", i=PACK, u=2)[:, runs],
-                pairs.bitcast(dt).rearrange("p (u c i) -> p c u i", i=PACK, u=2)[:, runs],
-            )
-
-        squares = [keep.tile([P, N * PACK], F32, name="squares%d" % b, align_bytes=64)[:] for b in range(B)]
+        final_stage = keep.tile([P, PACK, N], F32, name="final_stage")
+        value_pairs = [packed_tile("value_pairs0"), around_do0[:, 0 : 2 * N].bitcast(BF16)]
+        weights = keep.tile([P, N * PACK], F32, name="weights", align_bytes=64)
+        gated_dp = keep.tile([P, N * PACK], F32, name="gated_dp", align_bytes=64)
         k0_packed, k1_packed, q0_packed, q1_packed, v0_packed, ds0_packed, ds1_packed = (
             packed_tile(name + "_packed") for name in ("k0", "k1", "q0", "q1", "v0", "ds0", "ds1")
         )
         reused = keep.tile([P, 2 * N], F32, name="reused", align_bytes=64)
         do0_packed = reused[:].bitcast(BF16)
-        k_mx, q_mx, v_mx, do_mx, qm_mx, ds_mx = (
-            [mx_tiles("%s%d" % (name, b)) for b in range(B)] for name in ("k", "q", "v", "do", "qm", "ds")
-        )
-        v_mx[1] = v_mx[0]
+        k_mx, q_mx = ([mx_tiles("%s%d" % (name, b)) for b in range(B)] for name in ("k", "q"))
+        v_mx = mx_tiles("v")
+        do_mx, qm_mx, ds_mx = ([mx_tiles("%s%d" % (name, b)) for b in range(B)] for name in ("do", "qm", "ds"))
         banks = [psum.tile([P, N], F32, name="bank%d" % i) for i in range(8)]
         neg_gate = keep.tile([P, B, PACK], F32, name="neg_gate")
 
         for j in range(2):
-            nc.scalar.activation(cast_keys[:], k_planes[j], ACT.Copy)
-            nc.scalar.activation(pair_row(key_pairs[0], j), cast_keys[:].indirect(lists(0, 1)), ACT.Copy)
-            gather(pair_row(key_pairs[1], j), k_planes[j], 1, 2)
+            gather_on_scalar(pair_row(key_pairs[0], j), cast_keys, k_planes[j], whole_list(0))
+            gather(pair_row(key_pairs[1], j), k_planes[j], whole_list(1))
         for j in range(2, PACK):
             for b in range(B):
-                gather(pair_row(key_pairs[b], j), k_planes[j], b, b + 1)
-        deal(q0_packed, q0_rows)
+                gather(pair_row(key_pairs[b], j), k_planes[j], whole_list(b))
+        deal(nc.scalar.copy, q0_packed, q0_rows)
         weave(nc.vector.tensor_copy, I32, k0_packed, key_pairs[0])
         weave(nc.vector.tensor_copy, I32, k1_packed, key_pairs[1])
         quantize(k_mx[0], E4M3, k0_packed)
         quantize(k_mx[1], E4M3, k1_packed)
         quantize(q_mx[0], E4M3, q0_packed)
-        nc.scalar.activation(cast_values[:], v_planes[0], ACT.Copy)
-        nc.scalar.activation(rows1[:, 0, :], cast_values[:].indirect(lists(1, 2)), ACT.Copy)
-        gather(pair_row(value_pairs[0], 0), v_planes[0], 0, 1)
-        gather(rows1[:, 1, :], v_planes[1], 1, 2)
-        gather(pair_row(value_pairs[0], 1), v_planes[1], 0, 1)
-        nc.gpsimd.tensor_scalar(
-            value_pairs[1][:, 0 : 2 * N].rearrange("p (n e) -> p n e", e=2),
-            rows1[:].rearrange("p e n -> p n e"), 1.0, 0.0, ALU.mult, ALU.add,
+
+        gather_on_scalar(value_rows[:, 0, :], cast_values, v_planes[0], whole_list(1))
+        gather(pair_row(value_pairs[0], 0), v_planes[0], whole_list(0))
+        gather(value_rows[:, 1, :], v_planes[1], whole_list(1))
+        gather(pair_row(value_pairs[0], 1), v_planes[1], whole_list(0))
+        move_on_gpsimd(
+            value_pairs[1][:, 0 : 2 * N].rearrange("p (n e) -> p n e", e=2), value_rows[:].rearrange("p e n -> p n e")
         )
         nc.scalar.activation(neg_gate[:], gate[:], ACT.Copy, scale=-1.0)
 
-        weight = [squares[0][:, t * N : (t + 1) * N] for t in range(PACK)]
+        weight = [weights[:, t * N : (t + 1) * N] for t in range(PACK)]
         for t in range(PACK):
             product(banks[t][:], q_mx[0], E4M3, t, k_mx[0], E4M3)
         for t in range(PACK):
             nc.scalar.activation(weight[t], banks[t][:], ACT.Tanh)
             nc.scalar.activation(weight[t], weight[t], ACT.Square)
-        for t in range(PACK - 1):
+        last = PACK - 1
+        for t in range(last):
             nc.gpsimd.tensor_scalar(
                 weight[t], weight[t], neg_gate[:, 0, t : t + 1], gate[:, 0, t : t + 1], ALU.mult, ALU.add
             )
 
-        def gather_half(j, h):
-            cols = slice(LIST_COLS + h * LIST_COLS // 2, LIST_COLS + (h + 1) * LIST_COLS // 2)
-            nc.vector.tensor_copy(
-                pair_row(value_pairs[1], j)[:, h * HALF : (h + 1) * HALF], v_planes[j].indirect(offsets[:, cols])
-            )
+        def gather_value_half(j, h):
+            gather(pair_row(value_pairs[1], j)[:, h * HALF : (h + 1) * HALF], v_planes[j], half_list(1, h))
 
         for j in range(2, PACK):
-            gather(pair_row(value_pairs[0], j), v_planes[j], 0, 1)
-            gather_half(j, 0)
+            gather(pair_row(value_pairs[0], j), v_planes[j], whole_list(0))
+            gather_value_half(j, 0)
         for h in range(2):
             weave(nc.vector.tensor_copy, I32, v0_packed, value_pairs[0], h * HALF, (h + 1) * HALF)
-        deal(do0_packed, do0_rows, nc.scalar.copy, DO0_VECTOR, P)
-        tail = 3 * HALF + 3 * N + HALF
-        last_weight = shared[:, tail : tail + N]
-        nc.scalar.activation(last_weight, weight[3], ACT.Identity, bias=gate[:, 0, 3:4], scale=neg_gate[:, 0, 3:4])
-        weight[3] = last_weight
-        quantize(v_mx[0], E4M3, v0_packed, 0, HALF)
-        quantize(v_mx[0], E4M3, v0_packed, HALF, N)
-        deal(do0_packed, do0_rows, nc.vector.tensor_copy, 0, DO0_VECTOR)
+        deal(nc.scalar.copy, do0_packed, do0_rows, DO0_VECTOR, P)
+        nc.scalar.activation(
+            last_weight, weight[last], ACT.Identity, bias=gate[:, 0, last:PACK], scale=neg_gate[:, 0, last:PACK]
+        )
+        for h in range(2):
+            quantize(v_mx, E4M3, v0_packed, h * HALF, (h + 1) * HALF)
+        deal(nc.vector.tensor_copy, do0_packed, do0_rows, 0, DO0_VECTOR)
         quantize(do_mx[0], E5M2, do0_packed)
         for t in range(PACK):
-            product(banks[t][:], do_mx[0], E5M2, t, v_mx[0], E4M3)
+            product(banks[t][:], do_mx[0], E5M2, t, v_mx, E4M3)
         for j in range(2, PACK):
-            gather_half(j, 1)
+            gather_value_half(j, 1)
         v1_packed = do0_packed
-        nc.gpsimd.tensor_scalar(
+        move_on_gpsimd(
             v1_packed.rearrange("p (n u e) -> p n u e", u=2, e=2)[:, 0:HALF],
-            value_pairs[1].rearrange("p (u n e) -> p n u e", u=2, e=2)[:, 0:HALF], 1.0, 0.0, ALU.mult, ALU.add,
+            value_pairs[1].rearrange("p (u n e) -> p n u e", u=2, e=2)[:, 0:HALF],
         )
         qm0_packed = v0_packed
-        pack_gpsimd(qm0_packed, qm0_rows, 0, QM0_GPSIMD)
+        pack_on_gpsimd(qm0_packed, qm0_rows, 0, QM0_GPSIMD)
 
         ds0_rows = k0_packed
-        for t in range(PACK):
-            nc.vector.tensor_tensor(ds0_rows[:, t * N : (t + 1) * N], banks[t][:], weight[t], ALU.mult)
+        for t, factor_t in enumerate(weight[0:last] + [last_weight]):
+            nc.vector.tensor_tensor(ds0_rows[:, t * N : (t + 1) * N], banks[t][:], factor_t, ALU.mult)
         nc.vector.tensor_copy(
-            ds0_packed.rearrange("p (c i t) -> p c t i", i=8, t=PACK),
-            ds0_rows.rearrange("p (t c i) -> p c t i", i=8, t=PACK),
+            ds0_packed.rearrange("p (c i t) -> p c t i", i=RUN, t=PACK),
+            ds0_rows.rearrange("p (t c i) -> p c t i", i=RUN, t=PACK),
         )
         quantize(ds_mx[0], E5M2, ds0_packed)
 
-        deal(q1_packed, q1_rows)
+        deal(nc.scalar.copy, q1_packed, q1_rows)
         quantize(q_mx[1], E4M3, q1_packed, 0, HALF)
         weave(nc.scalar.copy, U32, v1_packed, value_pairs[1], HALF, N)
-        nc.scalar.copy(*pack_views("p c j i", qm0_packed, qm0_rows, QM0_GPSIMD, N))
+        pack_on_scalar(qm0_packed, qm0_rows, QM0_GPSIMD, N)
         quantize(qm_mx[0], E4M3, qm0_packed, 0, HALF)
-        key_grad(banks[0], 0, 0)
+        for j in range(2):
+            key_grad(banks[j], 0, j)
         quantize(q_mx[1], E4M3, q1_packed, HALF, N)
         quantize(qm_mx[0], E4M3, qm0_packed, HALF, N)
+
         late = keep.tile([P, 3 * N], F32, name="late", align_bytes=64)
-        early_words = QM1_GPSIMD[1] * 2
         do1_packed = late[:, 0 : 2 * N].bitcast(BF16)
-        last_factor = late[:, early_words : early_words + N]
+        last_start = 2 * QM1_GPSIMD
         spare = keep.tile([P, 2 * N], F32, name="spare", align_bytes=64)
         third_stage, last_square = spare[:, 0:N], spare[:, N : 2 * N]
-        qm1_halves = [spare[:, HALF : N + HALF].bitcast(BF16), late[:, 0:N].bitcast(BF16)]
-        factor = [reused[:, 0:N], reused[:, N : 2 * N], late[:, early_words + N : early_words + 2 * N], last_factor]
+        qm1_packed = [spare[:, HALF : N + HALF].bitcast(BF16), late[:, 0:N].bitcast(BF16)]
+        qm1_half_rows = [qm1_rows[:, :, h * HALF : (h + 1) * HALF] for h in range(2)]
+        factor = [
+            reused[:, 0:N],
+            reused[:, N : 2 * N],
+            late[:, last_start + N : last_start + 2 * N],
+            late[:, last_start : last_start + N],
+        ]
 
-        def qm1_views(order, h, lo, hi):
-            return pack_views(order, qm1_halves[h], qm1_rows[:, :, h * HALF : (h + 1) * HALF], lo, hi)
-
-        def quantize_qm1(h):
-            codes, scales = qm_mx[1]
-            cols = slice(h * HALF, (h + 1) * HALF)
-            nc.vector.quantize_mx(out=codes[:, cols].bitcast(E4M3), scales=scales[:, cols], in_=qm1_halves[h])
-
-        deal(do1_packed, do1_rows, nc.scalar.copy, DO1_VECTOR, P)
-        deal(do1_packed, do1_rows, nc.vector.tensor_copy, 0, DO1_VECTOR)
-        for c in range(4):
+        deal(nc.scalar.copy, do1_packed, do1_rows, DO1_VECTOR, P)
+        deal(nc.vector.tensor_copy, do1_packed, do1_rows, 0, DO1_VECTOR)
+        score_banks = banks[PACK : 2 * PACK]
+        for c in range(PACK):
             for t in range(PACK):
-                product(banks[4 + c][:, t * P : (t + 1) * P], q_mx[1], E4M3, t, k_mx[1], E4M3, c * P, (c + 1) * P)
+                product(score_banks[c][:, t * P : (t + 1) * P], q_mx[1], E4M3, t, k_mx[1], E4M3, c * P, (c + 1) * P)
 
-        def chunk(x, c, end=None):
-            return x[:, c * N : (c + 1 if end is None else end) * N]
+        gated = [
+            gated_dp[:, h * 2 * N : (h + 1) * 2 * N].rearrange("p (t n) -> p t n", t=PACK) for h in range(2)
+        ]
 
-        def tanh_slot_major(c):
-            nc.scalar.activation(
-                slot_major(factor[c]), banks[4 + c][:].rearrange("p (t n) -> p n t", t=PACK), ACT.Tanh
-            )
+        def tanh_chunk(c):
+            nc.scalar.activation(slot_major(factor[c]), score_banks[c][:].rearrange("p (t n) -> p n t", t=PACK), ACT.Tanh)
 
-        def place_half(j, h, bank, stage):
-            cols = slice(h * HALF, (h + 1) * HALF)
-            nc.scalar.copy(stage[:, cols], bank[:, cols])
-            half_list = offsets[:, h * LIST_COLS // 2 : (h + 1) * LIST_COLS // 2]
-            nc.vector.tensor_copy(placed[j][:].indirect(half_list), stage[:, cols])
+        def square(dst, src):
+            nc.scalar.activation(dst, src, ACT.Square)
 
-        flat = squares[1]
-        gated = [flat[:, h * 2 * N : (h + 1) * 2 * N].rearrange("p (t n) -> p t n", t=PACK) for h in range(2)]
+        def less_one(dst, src):
+            nc.scalar.activation(dst, src, ACT.Copy, bias=-1.0)
 
         def gate_dp(h):
             for t in range(PACK):
@@ -294,64 +298,56 @@ def tile_attend_gat_tnh_k_kernel(tc, qT, kT, vT, doT, rw, qm, offs, out):
                     scale=neg_gate[:, 1, t : t + 1],
                 )
 
-        def multiply(engine, c, lo=0, hi=P):
-            engine.tensor_tensor(
-                slot_major(chunk(ds1_packed, c))[:, lo:hi],
-                slot_major(factor[c])[:, lo:hi],
-                gated[c // 2][:, :, (c % 2) * P + lo : (c % 2) * P + hi].rearrange("p t n -> p n t"),
+        def multiply_on_gpsimd(factor_part, first, count):
+            nc.gpsimd.tensor_tensor(
+                slot_major(ds1_packed)[:, first : first + count],
+                slot_major(factor_part),
+                gated[first // HALF][:, :, first % HALF : first % HALF + count].rearrange("p t n -> p n t"),
                 ALU.mult,
             )
 
-        quantize(v_mx[1], E4M3, v1_packed)
+        quantize(v_mx, E4M3, v1_packed)
         quantize(do_mx[1], E5M2, do1_packed)
-        place(0, 0, banks[0], values0[:, 0, :])
-        tanh_slot_major(0)
-        tanh_slot_major(1)
-        nc.gpsimd.tensor_scalar(*qm1_views("p c i j", 1, 0, QM1_GPSIMD[1]), 1.0, 0.0, ALU.mult, ALU.add)
-        key_grad(banks[4], 0, 1)
-        dp1_banks = banks[1:4] + banks[0:1]
-        for t in range(PACK):
-            product(dp1_banks[t][:], do_mx[1], E5M2, t, v_mx[1], E4M3)
+        place(0, whole_list(0), banks[0][:], final_stage[:, 0, :])
+        place(1, whole_list(0), banks[1][:], stage[:, 0, :])
         for c in range(2):
-            nc.scalar.activation(factor[c], factor[c], ACT.Square)
+            tanh_chunk(c)
+        pack_on_gpsimd(qm1_packed[1], qm1_half_rows[1], 0, QM1_GPSIMD)
+        dp1_banks = banks[2:PACK] + banks[0:2]
+        for t in range(PACK):
+            product(dp1_banks[t][:], do_mx[1], E5M2, t, v_mx, E4M3)
+        for c in range(2):
+            square(factor[c], factor[c])
             nc.gpsimd.tensor_scalar(factor[c], factor[c], 1.0, -1.0, ALU.mult, ALU.add)
-        place(0, 1, banks[4], stage[:, 0, :])
-        key_grad(banks[5], 0, 2)
+        key_grad(score_banks[1], 0, 2)
         gate_dp(0)
-        multiply(nc.gpsimd, 0)
-        multiply(nc.gpsimd, 1)
-
-        def square(c):
-            nc.scalar.activation(factor[c], factor[c], ACT.Square)
-
-        def less_one(c):
-            nc.scalar.activation(factor[c], factor[c], ACT.Copy, bias=-1.0)
-
-        tanh_slot_major(2)
-        place(0, 2, banks[5], third_stage)
-        key_grad(banks[5], 0, 3)
-        square(2)
+        multiply_on_gpsimd(reused[:], 0, 2 * P)
+        tanh_chunk(2)
+        place(2, whole_list(0), score_banks[1][:], third_stage)
+        key_grad(score_banks[1], 0, last)
+        square(factor[2], factor[2])
         gate_dp(1)
-        less_one(2)
-        multiply(nc.gpsimd, 2)
-        tanh_slot_major(3)
-        place_half(3, 0, banks[5], stage[:, 1, :])
-        halves = [slice(h * HALF, (h + 1) * HALF) for h in range(2)]
-        for cols in halves:
-            nc.scalar.activation(last_square[:, cols], factor[3][:, cols], ACT.Square)
-        for h, cols in enumerate(halves):
-            nc.scalar.activation(factor[3][:, cols], last_square[:, cols], ACT.Copy, bias=-1.0)
-            multiply(nc.gpsimd, 3, h * P // 2, (h + 1) * P // 2)
-        nc.scalar.copy(*qm1_views("p c j i", 0, QM1_GPSIMD[0], HALF))
-        quantize_qm1(0)
-        quantize(ds_mx[1], E5M2, ds1_packed)
-        nc.scalar.copy(*qm1_views("p c j i", 1, QM1_GPSIMD[1], HALF))
-        quantize_qm1(1)
+        less_one(factor[2], factor[2])
+        multiply_on_gpsimd(factor[2], 2 * P, P)
 
-        dk1_banks = [banks[4], banks[6], banks[7], banks[0]]
+        tanh_chunk(last)
+        place(last, half_list(0, 0), score_banks[1][:, 0:HALF], stage[:, 1, 0:HALF])
+        halves = [slice(h * HALF, (h + 1) * HALF) for h in range(2)]
+        for words in halves:
+            square(last_square[:, words], factor[last][:, words])
+        for h, words in enumerate(halves):
+            less_one(factor[last][:, words], last_square[:, words])
+            multiply_on_gpsimd(factor[last][:, words], last * P + h * P // 2, P // 2)
+        pack_on_scalar(qm1_packed[0], qm1_half_rows[0], 0, HALF)
+        quantize_into(qm_mx[1], E4M3, 0, HALF, qm1_packed[0])
+        quantize(ds_mx[1], E5M2, ds1_packed)
+        pack_on_scalar(qm1_packed[1], qm1_half_rows[1], QM1_GPSIMD, HALF)
+        quantize_into(qm_mx[1], E4M3, HALF, N, qm1_packed[1])
+
+        dk1_banks = [score_banks[0], score_banks[2], score_banks[last], banks[0]]
         for j in range(D // P):
             key_grad(dk1_banks[j], 1, j)
-        place_half(3, 1, banks[5], factor[3])
+        place(last, half_list(0, 1), score_banks[1][:, HALF:N], factor[last][:, HALF:N])
         for j in range(D // P):
-            place(1, j, dk1_banks[j], values0[:, j, :])
+            place(j, whole_list(1), dk1_banks[j][:], final_stage[:, j, :])
             nc.sync.dma_start(out=out[j * P : (j + 1) * P, :], in_=placed[j][:])

@@ -20,11 +20,14 @@ P = 128
 PACK = 4
 HALF = N // 2
 LIST_COLS = N // 16
+KEY_ORDER = (0, 2, 1, 3)
 RUN = 8
-RAW_BUFS = 8
-DO0_VECTOR = 56
-DO1_VECTOR = 24
-QM0_GPSIMD = 192
+RAW_BUFS = 7
+Q0_VECTOR = 32
+DO0_VECTOR = 52
+QM0_VECTOR = 48
+DO1_SECOND = 16
+Q1_GPSIMD = 40
 QM1_GPSIMD = 192
 
 
@@ -73,11 +76,17 @@ def tile_attend_gat_tnh_k_kernel(tc, qT, kT, vT, doT, rw, qm, offs, out):
         def pair_row(pairs, j):
             return pairs.rearrange("p (u n e) -> p u e n", u=2, e=2)[:, j // 2, j % 2, :]
 
-        def weave(copy, word, dst, pairs, lo=0, hi=N):
-            runs = slice(lo // PACK, hi // PACK)
+        def weave(copy, word, dst, pairs, h):
+            runs = slice(h * HALF // PACK, (h + 1) * HALF // PACK)
             copy(
-                dst.bitcast(word).rearrange("p (c i u) -> p c u i", i=PACK, u=2)[:, runs],
+                dst.bitcast(word).rearrange("p (c i u) -> p c u i", i=PACK, u=2),
                 pairs.bitcast(word).rearrange("p (u c i) -> p c u i", i=PACK, u=2)[:, runs],
+            )
+
+        def weave_on_gpsimd(dst, pairs, lo, hi):
+            nc.gpsimd.tensor_copy(
+                dst.bitcast(U32).rearrange("p (n u) -> p n u", u=2)[:, lo:hi],
+                pairs.bitcast(U32).rearrange("p (u n) -> p n u", u=2)[:, lo:hi],
             )
 
         def pack_views(order, dst, src, lo, hi):
@@ -97,6 +106,12 @@ def tile_attend_gat_tnh_k_kernel(tc, qT, kT, vT, doT, rw, qm, offs, out):
             copy(
                 dst.rearrange("p (t m j) -> p m j t", t=PACK, j=PACK)[:, lo:hi],
                 src.rearrange("p j (m t) -> p m j t", t=PACK)[:, lo:hi],
+            )
+
+        def deal_on_gpsimd(dst, src, lo, hi):
+            move_on_gpsimd(
+                dst.rearrange("p (t m j) -> p m t j", t=PACK, j=PACK)[:, lo:hi],
+                src.rearrange("p j (m t) -> p m t j", t=PACK)[:, lo:hi],
             )
 
         def quantize_into(mx, fmt, lo, hi, src):
@@ -129,23 +144,24 @@ def tile_attend_gat_tnh_k_kernel(tc, qT, kT, vT, doT, rw, qm, offs, out):
             return x.rearrange("p (n t) -> p n t", t=PACK)
 
         offsets = keep.tile([P, B * LIST_COLS], U16, name="offsets")
-        k_planes = [load_plane(kT, "k_plane", 0)]
+        k_planes = {0: load_plane(kT, "k_plane", 0)}
         nc.sync.dma_start(offsets[:], offs)
-        k_planes.extend(load_plane(kT, "k_plane", j) for j in range(1, PACK))
+        for j in KEY_ORDER[1:]:
+            k_planes[j] = load_plane(kT, "k_plane", j)
         q0_rows = load_rows(qT[0], "q0_rows")
-        v_planes = [load_plane(vT, "v_plane", j) for j in range(2)]
-        gate = keep.tile([P, B, PACK], F32, name="gate")
-        nc.sync.dma_start(out=gate[:], in_=rw.rearrange("b (p t) o -> p b (t o)", t=PACK))
-        v_planes.extend(load_plane(vT, "v_plane", j) for j in range(2, PACK))
+        v_planes = [load_plane(vT, "v_plane", j) for j in range(PACK)]
         do0_start = 2 * N - HALF
         do0_end = do0_start + PACK * N
         around_do0 = keep.tile([P, do0_end + N], F32, name="around_do0", align_bytes=64)
         do0_rows = around_do0[:, do0_start:do0_end].rearrange("p (j w) -> p j w", j=PACK)
-        last_weight = around_do0[:, do0_end - HALF : do0_end + HALF]
         nc.sync.dma_start(out=do0_rows, in_=doT[0].rearrange("(p j) w -> p j w", j=PACK))
+        gate = keep.tile([P, B, PACK], F32, name="gate")
+        nc.sync.dma_start(out=gate[:], in_=rw.rearrange("b (p t) o -> p b (t o)", t=PACK))
         q1_rows = load_rows(qT[1], "q1_rows")
         qm0_rows = load_rows(qm[0], "qm0_rows")
-        do1_rows = load_rows(doT[1], "do1_rows")
+        do1_tile = keep.tile([P, PACK * (N + DO1_SECOND)], F32, name="do1_tile", align_bytes=64)
+        do1_rows = do1_tile[:, 0 : PACK * N].rearrange("p (j w) -> p j w", j=PACK)
+        nc.sync.dma_start(out=do1_rows, in_=doT[1].rearrange("(p j) w -> p j w", j=PACK))
         qm1_rows = load_rows(qm[1], "qm1_rows")
 
         placed = []
@@ -158,102 +174,115 @@ def tile_attend_gat_tnh_k_kernel(tc, qT, kT, vT, doT, rw, qm, offs, out):
         cast_keys = keep.tile([P, T], BF16, name="cast_keys")
         cast_values = keep.tile([P, T], BF16, name="cast_values")
         value_rows = keep.tile([P, 2, N], BF16, name="value_rows")
-        stage = keep.tile([P, 2, N], F32, name="stage")
+        half_stage = keep.tile([P, HALF], F32, name="half_stage")
         final_stage = keep.tile([P, PACK, N], F32, name="final_stage")
         value_pairs = [packed_tile("value_pairs0"), around_do0[:, 0 : 2 * N].bitcast(BF16)]
-        weights = keep.tile([P, N * PACK], F32, name="weights", align_bytes=64)
+        weights = keep.tile([P, N * (PACK - 1)], F32, name="weights", align_bytes=64)
         gated_dp = keep.tile([P, N * PACK], F32, name="gated_dp", align_bytes=64)
-        k0_packed, k1_packed, q0_packed, q1_packed, v0_packed, ds0_packed, ds1_packed = (
-            packed_tile(name + "_packed") for name in ("k0", "k1", "q0", "q1", "v0", "ds0", "ds1")
+        k0_packed, v0_packed, ds0_packed, ds1_packed = (
+            packed_tile(name + "_packed") for name in ("k0", "v0", "ds0", "ds1")
         )
-        reused = keep.tile([P, 2 * N], F32, name="reused", align_bytes=64)
-        do0_packed = reused[:].bitcast(BF16)
+        qm0_packed = v0_packed
+        shared = 32
+        q0_k1 = keep.tile([P, 2 * PACK * N - shared], BF16, name="q0_k1", align_bytes=64)
+        q0_packed, k1_packed = q0_k1[:, 0 : PACK * N], q0_k1[:, PACK * N - shared :]
+        do0_q1 = keep.tile([P, 2 * PACK * N - shared], BF16, name="do0_q1", align_bytes=64)
+        do0_packed, q1_packed = do0_q1[:, 0 : PACK * N], do0_q1[:, PACK * N - shared :]
+        first_weight = keep.tile([P, 3 * N - 16], F32, name="first_weight", align_bytes=64)
+        v1_packed = first_weight[:, N - 16 :].bitcast(BF16)
         k_mx, q_mx = ([mx_tiles("%s%d" % (name, b)) for b in range(B)] for name in ("k", "q"))
         v_mx = mx_tiles("v")
         do_mx, qm_mx, ds_mx = ([mx_tiles("%s%d" % (name, b)) for b in range(B)] for name in ("do", "qm", "ds"))
         banks = [psum.tile([P, N], F32, name="bank%d" % i) for i in range(8)]
-        neg_gate = keep.tile([P, B, PACK], F32, name="neg_gate")
+        neg_gate = keep.tile([P, PACK], F32, name="neg_gate")
+        last = PACK - 1
 
-        for j in range(2):
-            gather_on_scalar(pair_row(key_pairs[0], j), cast_keys, k_planes[j], whole_list(0))
+        for j in KEY_ORDER:
             gather(pair_row(key_pairs[1], j), k_planes[j], whole_list(1))
-        for j in range(2, PACK):
-            for b in range(B):
-                gather(pair_row(key_pairs[b], j), k_planes[j], whole_list(b))
-        deal(nc.scalar.copy, q0_packed, q0_rows)
-        weave(nc.vector.tensor_copy, I32, k0_packed, key_pairs[0])
-        weave(nc.vector.tensor_copy, I32, k1_packed, key_pairs[1])
-        quantize(k_mx[0], E4M3, k0_packed)
-        quantize(k_mx[1], E4M3, k1_packed)
+            if j < 2:
+                gather_on_scalar(pair_row(key_pairs[0], j), cast_keys, k_planes[j], whole_list(0))
+            elif j < last:
+                gather(pair_row(key_pairs[0], j), k_planes[j], whole_list(0))
+            else:
+                for h in range(2):
+                    gather(pair_row(key_pairs[0], j)[:, h * HALF : (h + 1) * HALF], k_planes[j], half_list(0, h))
+        weave_on_gpsimd(k1_packed, key_pairs[1], HALF, N)
+        deal(nc.scalar.copy, q0_packed, q0_rows, Q0_VECTOR, P)
+        for h in range(2):
+            weave(nc.vector.tensor_copy, I32, k0_packed[:, h * 2 * N : (h + 1) * 2 * N], key_pairs[0], h)
+        deal(nc.vector.tensor_copy, q0_packed, q0_rows, 0, Q0_VECTOR)
+        for h in range(2):
+            quantize(k_mx[0], E4M3, k0_packed, h * HALF, (h + 1) * HALF)
         quantize(q_mx[0], E4M3, q0_packed)
+        weave_on_gpsimd(k1_packed, key_pairs[1], 0, HALF)
 
         gather_on_scalar(value_rows[:, 0, :], cast_values, v_planes[0], whole_list(1))
         gather(pair_row(value_pairs[0], 0), v_planes[0], whole_list(0))
+        for h in (1, 0):
+            quantize(k_mx[1], E4M3, k1_packed, h * HALF, (h + 1) * HALF)
         gather(value_rows[:, 1, :], v_planes[1], whole_list(1))
         gather(pair_row(value_pairs[0], 1), v_planes[1], whole_list(0))
         move_on_gpsimd(
             value_pairs[1][:, 0 : 2 * N].rearrange("p (n e) -> p n e", e=2), value_rows[:].rearrange("p e n -> p n e")
         )
-        nc.scalar.activation(neg_gate[:], gate[:], ACT.Copy, scale=-1.0)
 
-        weight = [weights[:, t * N : (t + 1) * N] for t in range(PACK)]
+        weight = [first_weight[:, 0:N]] + [weights[:, t * N : (t + 1) * N] for t in range(last)]
         for t in range(PACK):
             product(banks[t][:], q_mx[0], E4M3, t, k_mx[0], E4M3)
         for t in range(PACK):
             nc.scalar.activation(weight[t], banks[t][:], ACT.Tanh)
             nc.scalar.activation(weight[t], weight[t], ACT.Square)
-        last = PACK - 1
-        for t in range(last):
-            nc.gpsimd.tensor_scalar(
-                weight[t], weight[t], neg_gate[:, 0, t : t + 1], gate[:, 0, t : t + 1], ALU.mult, ALU.add
-            )
+        for t in range(2):
+            nc.gpsimd.tensor_scalar(weight[t], weight[t], -1.0, 1.0, ALU.mult, ALU.add)
 
-        def gather_value_half(j, h):
-            gather(pair_row(value_pairs[1], j)[:, h * HALF : (h + 1) * HALF], v_planes[j], half_list(1, h))
+        def gather_value_half(b, j, h):
+            gather(pair_row(value_pairs[b], j)[:, h * HALF : (h + 1) * HALF], v_planes[j], half_list(b, h))
 
-        for j in range(2, PACK):
-            gather(pair_row(value_pairs[0], j), v_planes[j], whole_list(0))
-            gather_value_half(j, 0)
+        gather(pair_row(value_pairs[0], 2), v_planes[2], whole_list(0))
+        gather_value_half(1, 2, 0)
+        gather(pair_row(value_pairs[0], last), v_planes[last], whole_list(0))
+        gather_value_half(1, last, 0)
         for h in range(2):
-            weave(nc.vector.tensor_copy, I32, v0_packed, value_pairs[0], h * HALF, (h + 1) * HALF)
-        deal(nc.scalar.copy, do0_packed, do0_rows, DO0_VECTOR, P)
-        nc.scalar.activation(
-            last_weight, weight[last], ACT.Identity, bias=gate[:, 0, last:PACK], scale=neg_gate[:, 0, last:PACK]
-        )
+            weave(nc.vector.tensor_copy, I32, v0_packed[:, h * 2 * N : (h + 1) * 2 * N], value_pairs[0], h)
         for h in range(2):
             quantize(v_mx, E4M3, v0_packed, h * HALF, (h + 1) * HALF)
+        deal(nc.scalar.copy, do0_packed, do0_rows, DO0_VECTOR, P)
         deal(nc.vector.tensor_copy, do0_packed, do0_rows, 0, DO0_VECTOR)
+        late_weight = [around_do0[:, do0_end - HALF + (t - last) * N : do0_end + HALF + (t - last) * N] for t in range(2, PACK)]
+        for t in range(2, PACK):
+            nc.scalar.activation(late_weight[t - 2], weight[t], ACT.Copy, bias=1.0, scale=-1.0)
         quantize(do_mx[0], E5M2, do0_packed)
         for t in range(PACK):
             product(banks[t][:], do_mx[0], E5M2, t, v_mx, E4M3)
         for j in range(2, PACK):
-            gather_value_half(j, 1)
-        v1_packed = do0_packed
-        move_on_gpsimd(
-            v1_packed.rearrange("p (n u e) -> p n u e", u=2, e=2)[:, 0:HALF],
-            value_pairs[1].rearrange("p (u n e) -> p n u e", u=2, e=2)[:, 0:HALF],
-        )
-        qm0_packed = v0_packed
-        pack_on_gpsimd(qm0_packed, qm0_rows, 0, QM0_GPSIMD)
+            gather_value_half(1, j, 1)
+        deal_on_gpsimd(q1_packed, q1_rows, 0, Q1_GPSIMD)
 
         ds0_rows = k0_packed
-        for t, factor_t in enumerate(weight[0:last] + [last_weight]):
-            nc.vector.tensor_tensor(ds0_rows[:, t * N : (t + 1) * N], banks[t][:], factor_t, ALU.mult)
-        nc.vector.tensor_copy(
-            ds0_packed.rearrange("p (c i t) -> p c t i", i=RUN, t=PACK),
-            ds0_rows.rearrange("p (t c i) -> p c t i", i=RUN, t=PACK),
-        )
-        quantize(ds_mx[0], E5M2, ds0_packed)
-
-        deal(nc.scalar.copy, q1_packed, q1_rows)
+        for t, factor_t in enumerate(weight[0:2] + late_weight):
+            nc.vector.scalar_tensor_tensor(
+                ds0_rows[:, t * N : (t + 1) * N], banks[t][:], gate[:, 0, t : t + 1], factor_t, ALU.mult, ALU.mult
+            )
+        weave_on_gpsimd(v1_packed, value_pairs[1], 0, N)
+        deal(nc.scalar.copy, q1_packed, q1_rows, Q1_GPSIMD, P)
         quantize(q_mx[1], E4M3, q1_packed, 0, HALF)
-        weave(nc.scalar.copy, U32, v1_packed, value_pairs[1], HALF, N)
-        pack_on_scalar(qm0_packed, qm0_rows, QM0_GPSIMD, N)
+        pack_on_scalar(qm0_packed, qm0_rows, 0, HALF)
+        pack_on_scalar(qm0_packed, qm0_rows, HALF, N - QM0_VECTOR)
         quantize(qm_mx[0], E4M3, qm0_packed, 0, HALF)
+        for h in range(2):
+            runs = slice(h * HALF // RUN, (h + 1) * HALF // RUN)
+            nc.vector.tensor_copy(
+                ds0_packed.rearrange("p (c i t) -> p c t i", i=RUN, t=PACK)[:, runs],
+                ds0_rows.rearrange("p (t c i) -> p c t i", i=RUN, t=PACK)[:, runs],
+            )
+        for h in range(2):
+            quantize(ds_mx[0], E5M2, ds0_packed, h * HALF, (h + 1) * HALF)
         for j in range(2):
             key_grad(banks[j], 0, j)
+        nc.vector.tensor_copy(*pack_views("p c j i", qm0_packed, qm0_rows, N - QM0_VECTOR, N))
         quantize(q_mx[1], E4M3, q1_packed, HALF, N)
         quantize(qm_mx[0], E4M3, qm0_packed, HALF, N)
+        nc.scalar.activation(neg_gate[:], gate[:, 1, :], ACT.Copy, scale=-1.0)
 
         late = keep.tile([P, 3 * N], F32, name="late", align_bytes=64)
         do1_packed = late[:, 0 : 2 * N].bitcast(BF16)
@@ -262,15 +291,16 @@ def tile_attend_gat_tnh_k_kernel(tc, qT, kT, vT, doT, rw, qm, offs, out):
         third_stage, last_square = spare[:, 0:N], spare[:, N : 2 * N]
         qm1_packed = [spare[:, HALF : N + HALF].bitcast(BF16), late[:, 0:N].bitcast(BF16)]
         qm1_half_rows = [qm1_rows[:, :, h * HALF : (h + 1) * HALF] for h in range(2)]
+        first_factors = do1_tile[:, 0 : 2 * N]
         factor = [
-            reused[:, 0:N],
-            reused[:, N : 2 * N],
+            first_factors[:, 0:N],
+            first_factors[:, N : 2 * N],
             late[:, last_start + N : last_start + 2 * N],
             late[:, last_start : last_start + N],
         ]
 
-        deal(nc.scalar.copy, do1_packed, do1_rows, DO1_VECTOR, P)
-        deal(nc.vector.tensor_copy, do1_packed, do1_rows, 0, DO1_VECTOR)
+        deal(nc.scalar.copy, do1_packed, do1_rows, DO1_SECOND, P)
+        deal(nc.scalar.copy, do1_packed, do1_rows, 0, DO1_SECOND)
         score_banks = banks[PACK : 2 * PACK]
         for c in range(PACK):
             for t in range(PACK):
@@ -295,7 +325,7 @@ def tile_attend_gat_tnh_k_kernel(tc, qT, kT, vT, doT, rw, qm, offs, out):
                     gated[h][:, t, :],
                     dp1_banks[t][:, h * HALF : (h + 1) * HALF],
                     ACT.Copy,
-                    scale=neg_gate[:, 1, t : t + 1],
+                    scale=neg_gate[:, t : t + 1],
                 )
 
         def multiply_on_gpsimd(factor_part, first, count):
@@ -308,8 +338,8 @@ def tile_attend_gat_tnh_k_kernel(tc, qT, kT, vT, doT, rw, qm, offs, out):
 
         quantize(v_mx, E4M3, v1_packed)
         quantize(do_mx[1], E5M2, do1_packed)
-        place(0, whole_list(0), banks[0][:], final_stage[:, 0, :])
-        place(1, whole_list(0), banks[1][:], stage[:, 0, :])
+        place(0, whole_list(0), banks[0][:], do1_tile[:, last * N + PACK * DO1_SECOND :])
+        place(1, whole_list(0), banks[1][:], do1_rows[:, 2, :])
         for c in range(2):
             tanh_chunk(c)
         pack_on_gpsimd(qm1_packed[1], qm1_half_rows[1], 0, QM1_GPSIMD)
@@ -321,7 +351,7 @@ def tile_attend_gat_tnh_k_kernel(tc, qT, kT, vT, doT, rw, qm, offs, out):
             nc.gpsimd.tensor_scalar(factor[c], factor[c], 1.0, -1.0, ALU.mult, ALU.add)
         key_grad(score_banks[1], 0, 2)
         gate_dp(0)
-        multiply_on_gpsimd(reused[:], 0, 2 * P)
+        multiply_on_gpsimd(first_factors, 0, 2 * P)
         tanh_chunk(2)
         place(2, whole_list(0), score_banks[1][:], third_stage)
         key_grad(score_banks[1], 0, last)
@@ -331,7 +361,7 @@ def tile_attend_gat_tnh_k_kernel(tc, qT, kT, vT, doT, rw, qm, offs, out):
         multiply_on_gpsimd(factor[2], 2 * P, P)
 
         tanh_chunk(last)
-        place(last, half_list(0, 0), score_banks[1][:, 0:HALF], stage[:, 1, 0:HALF])
+        place(last, half_list(0, 0), score_banks[1][:, 0:HALF], half_stage[:])
         halves = [slice(h * HALF, (h + 1) * HALF) for h in range(2)]
         for words in halves:
             square(last_square[:, words], factor[last][:, words])

@@ -22,13 +22,13 @@ HALF = N // 2
 LIST_COLS = N // 16
 KEY_ORDER = (0, 2, 1, 3)
 RUN = 8
-RAW_BUFS = 7
+RAW_BUFS = 6
 Q0_VECTOR = 32
 DO0_VECTOR = 52
-QM0_VECTOR = 48
-DO1_SECOND = 16
 Q1_GPSIMD = 40
-QM1_GPSIMD = 192
+DO1_EARLY = 24
+QM1_SCALAR = 64
+TAIL = 64
 
 
 def tile_attend_gat_tnh_k_kernel(tc, qT, kT, vT, doT, rw, qm, offs, out):
@@ -51,9 +51,9 @@ def tile_attend_gat_tnh_k_kernel(tc, qT, kT, vT, doT, rw, qm, offs, out):
         def packed_tile(name):
             return keep.tile([P, N * PACK], BF16, name=name, align_bytes=64)[:]
 
-        def mx_tiles(name):
-            codes = keep.tile([P, N], U32, name=name + "_codes", align_bytes=64)
-            scales = keep.tile([P, N], U8, name=name + "_scales", align_bytes=64)
+        def mx_tiles(name, width=N):
+            codes = keep.tile([P, width], U32, name=name + "_codes", align_bytes=64)
+            scales = keep.tile([P, width], U8, name=name + "_scales", align_bytes=64)
             return codes, scales
 
         def whole_list(b):
@@ -133,12 +133,8 @@ def tile_attend_gat_tnh_k_kernel(tc, qT, kT, vT, doT, rw, qm, offs, out):
                 stop=True,
             )
 
-        def key_grad(bank, b, j):
-            product(bank[:], qm_mx[b], E4M3, j, ds_mx[b], E5M2)
-
-        def place(j, entries, source, stage):
-            nc.scalar.copy(stage, source)
-            nc.vector.tensor_copy(placed[j][:].indirect(entries), stage)
+        def key_grad(bank, b, j, first):
+            product(bank[:], qm_mx[b], E4M3, j, grad_mx, E5M2, first, first + N)
 
         def slot_major(x):
             return x.rearrange("p (n t) -> p n t", t=PACK)
@@ -157,11 +153,15 @@ def tile_attend_gat_tnh_k_kernel(tc, qT, kT, vT, doT, rw, qm, offs, out):
         nc.sync.dma_start(out=do0_rows, in_=doT[0].rearrange("(p j) w -> p j w", j=PACK))
         gate = keep.tile([P, B, PACK], F32, name="gate")
         nc.sync.dma_start(out=gate[:], in_=rw.rearrange("b (p t) o -> p b (t o)", t=PACK))
-        q1_rows = load_rows(qT[1], "q1_rows")
-        qm0_rows = load_rows(qm[0], "qm0_rows")
-        do1_tile = keep.tile([P, PACK * (N + DO1_SECOND)], F32, name="do1_tile", align_bytes=64)
-        do1_rows = do1_tile[:, 0 : PACK * N].rearrange("p (j w) -> p j w", j=PACK)
-        nc.sync.dma_start(out=do1_rows, in_=doT[1].rearrange("(p j) w -> p j w", j=PACK))
+        v1_q1 = keep.tile([P, 2 * N - 16 + PACK * N], F32, name="v1_q1", align_bytes=64)
+        v1_packed = v1_q1[:, 0 : 2 * N].bitcast(BF16)
+        q1_rows = v1_q1[:, 2 * N - 16 :].rearrange("p (j w) -> p j w", j=PACK)
+        nc.sync.dma_start(out=q1_rows, in_=qT[1].rearrange("(p j) w -> p j w", j=PACK))
+        ds0_qm0 = keep.tile([P, 2 * N - 16 + PACK * N], F32, name="ds0_qm0", align_bytes=64)
+        ds0_packed = ds0_qm0[:, 0 : 2 * N].bitcast(BF16)
+        qm0_rows = ds0_qm0[:, 2 * N - 16 :].rearrange("p (j w) -> p j w", j=PACK)
+        nc.sync.dma_start(out=qm0_rows, in_=qm[0].rearrange("(p j) w -> p j w", j=PACK))
+        do1_rows = load_rows(doT[1], "do1_rows")
         qm1_rows = load_rows(qm[1], "qm1_rows")
 
         placed = []
@@ -174,25 +174,25 @@ def tile_attend_gat_tnh_k_kernel(tc, qT, kT, vT, doT, rw, qm, offs, out):
         cast_keys = keep.tile([P, T], BF16, name="cast_keys")
         cast_values = keep.tile([P, T], BF16, name="cast_values")
         value_rows = keep.tile([P, 2, N], BF16, name="value_rows")
-        half_stage = keep.tile([P, HALF], F32, name="half_stage")
-        final_stage = keep.tile([P, PACK, N], F32, name="final_stage")
         value_pairs = [packed_tile("value_pairs0"), around_do0[:, 0 : 2 * N].bitcast(BF16)]
-        weights = keep.tile([P, N * (PACK - 1)], F32, name="weights", align_bytes=64)
+        weights = keep.tile([P, N * PACK], F32, name="weights", align_bytes=64)
         gated_dp = keep.tile([P, N * PACK], F32, name="gated_dp", align_bytes=64)
-        k0_packed, v0_packed, ds0_packed, ds1_packed = (
-            packed_tile(name + "_packed") for name in ("k0", "v0", "ds0", "ds1")
-        )
-        qm0_packed = v0_packed
+        k0_packed, do1_packed = (packed_tile(name + "_packed") for name in ("k0", "do1"))
         shared = 32
         q0_k1 = keep.tile([P, 2 * PACK * N - shared], BF16, name="q0_k1", align_bytes=64)
         q0_packed, k1_packed = q0_k1[:, 0 : PACK * N], q0_k1[:, PACK * N - shared :]
         do0_q1 = keep.tile([P, 2 * PACK * N - shared], BF16, name="do0_q1", align_bytes=64)
         do0_packed, q1_packed = do0_q1[:, 0 : PACK * N], do0_q1[:, PACK * N - shared :]
-        first_weight = keep.tile([P, 3 * N - 16], F32, name="first_weight", align_bytes=64)
-        v1_packed = first_weight[:, N - 16 :].bitcast(BF16)
+        v0_qm1 = keep.tile([P, 2 * PACK * N - shared], BF16, name="v0_qm1", align_bytes=64)
+        v0_packed, qm1_packed = v0_qm1[:, 0 : PACK * N], v0_qm1[:, PACK * N - shared :]
+        qm0_packed = v0_packed
+        ds1_halves = keep.tile([P, PACK * N - shared], BF16, name="ds1_halves", align_bytes=64)
+        ds1_packed = [ds1_halves[:, 0 : 2 * N], ds1_halves[:, 2 * N - shared :]]
         k_mx, q_mx = ([mx_tiles("%s%d" % (name, b)) for b in range(B)] for name in ("k", "q"))
         v_mx = mx_tiles("v")
-        do_mx, qm_mx, ds_mx = ([mx_tiles("%s%d" % (name, b)) for b in range(B)] for name in ("do", "qm", "ds"))
+        qm_mx = [mx_tiles("qm%d" % b) for b in range(B)]
+        grad_mx = mx_tiles("grad", 3 * N)
+        do_mx = [grad_mx, mx_tiles("do1")]
         banks = [psum.tile([P, N], F32, name="bank%d" % i) for i in range(8)]
         neg_gate = keep.tile([P, PACK], F32, name="neg_gate")
         last = PACK - 1
@@ -226,7 +226,7 @@ def tile_attend_gat_tnh_k_kernel(tc, qT, kT, vT, doT, rw, qm, offs, out):
             value_pairs[1][:, 0 : 2 * N].rearrange("p (n e) -> p n e", e=2), value_rows[:].rearrange("p e n -> p n e")
         )
 
-        weight = [first_weight[:, 0:N]] + [weights[:, t * N : (t + 1) * N] for t in range(last)]
+        weight = [weights[:, t * N : (t + 1) * N] for t in range(PACK)]
         for t in range(PACK):
             product(banks[t][:], q_mx[0], E4M3, t, k_mx[0], E4M3)
         for t in range(PACK):
@@ -266,41 +266,46 @@ def tile_attend_gat_tnh_k_kernel(tc, qT, kT, vT, doT, rw, qm, offs, out):
         weave_on_gpsimd(v1_packed, value_pairs[1], 0, N)
         deal(nc.scalar.copy, q1_packed, q1_rows, Q1_GPSIMD, P)
         quantize(q_mx[1], E4M3, q1_packed, 0, HALF)
-        pack_on_scalar(qm0_packed, qm0_rows, 0, HALF)
-        pack_on_scalar(qm0_packed, qm0_rows, HALF, N - QM0_VECTOR)
-        quantize(qm_mx[0], E4M3, qm0_packed, 0, HALF)
-        for h in range(2):
+
+        def pack_ds0(copy, h):
             runs = slice(h * HALF // RUN, (h + 1) * HALF // RUN)
-            nc.vector.tensor_copy(
+            copy(
                 ds0_packed.rearrange("p (c i t) -> p c t i", i=RUN, t=PACK)[:, runs],
                 ds0_rows.rearrange("p (t c i) -> p c t i", i=RUN, t=PACK)[:, runs],
             )
-        for h in range(2):
-            quantize(ds_mx[0], E5M2, ds0_packed, h * HALF, (h + 1) * HALF)
-        for j in range(2):
-            key_grad(banks[j], 0, j)
-        nc.vector.tensor_copy(*pack_views("p c j i", qm0_packed, qm0_rows, N - QM0_VECTOR, N))
+
+        pack_on_scalar(qm0_packed, qm0_rows, 0, P)
+        pack_on_scalar(qm0_packed, qm0_rows, HALF, N)
+        pack_ds0(nc.vector.tensor_copy, 0)
+        pack_ds0(nc.scalar.copy, 1)
+        nc.vector.tensor_copy(*pack_views("p c j i", qm0_packed, qm0_rows, P, HALF))
+        quantize_into(grad_mx, E5M2, N, N + HALF, ds0_packed[:, 0 : 2 * N])
+        quantize(qm_mx[0], E4M3, qm0_packed, P, HALF)
+        key_grad(banks[PACK], 0, 1, HALF)
+        quantize(qm_mx[0], E4M3, qm0_packed, 0, P)
+        key_grad(banks[PACK + 1], 0, 0, HALF)
         quantize(q_mx[1], E4M3, q1_packed, HALF, N)
+        quantize_into(grad_mx, E5M2, N + HALF, 2 * N, ds0_packed[:, 2 * N :])
+        for j in range(2):
+            key_grad(banks[j], 0, 1 - j, N)
+        quantize(v_mx, E4M3, v1_packed)
         quantize(qm_mx[0], E4M3, qm0_packed, HALF, N)
         nc.scalar.activation(neg_gate[:], gate[:, 1, :], ACT.Copy, scale=-1.0)
 
-        late = keep.tile([P, 3 * N], F32, name="late", align_bytes=64)
-        do1_packed = late[:, 0 : 2 * N].bitcast(BF16)
-        last_start = 2 * QM1_GPSIMD
-        spare = keep.tile([P, 2 * N], F32, name="spare", align_bytes=64)
-        third_stage, last_square = spare[:, 0:N], spare[:, N : 2 * N]
-        qm1_packed = [spare[:, HALF : N + HALF].bitcast(BF16), late[:, 0:N].bitcast(BF16)]
-        qm1_half_rows = [qm1_rows[:, :, h * HALF : (h + 1) * HALF] for h in range(2)]
-        first_factors = do1_tile[:, 0 : 2 * N]
-        factor = [
-            first_factors[:, 0:N],
-            first_factors[:, N : 2 * N],
-            late[:, last_start + N : last_start + 2 * N],
-            late[:, last_start : last_start + N],
-        ]
+        factor = weight
+        stages = keep.tile([P, 4, N], F32, name="stages")
 
-        deal(nc.scalar.copy, do1_packed, do1_rows, DO1_SECOND, P)
-        deal(nc.scalar.copy, do1_packed, do1_rows, 0, DO1_SECOND)
+        def copy_out(stage, source):
+            nc.scalar.copy(stage, source)
+
+        def scatter(j, entries, stage):
+            nc.vector.tensor_copy(placed[j][:].indirect(entries), stage)
+
+        first, second = slice(0, HALF), slice(HALF, N)
+        deal(nc.scalar.copy, do1_packed, do1_rows, 0, DO1_EARLY)
+        for j in range(2):
+            copy_out(stages[:, j, first], banks[PACK + j][:, second])
+            scatter(1 - j, half_list(0, 0), stages[:, j, first])
         score_banks = banks[PACK : 2 * PACK]
         for c in range(PACK):
             for t in range(PACK):
@@ -328,56 +333,62 @@ def tile_attend_gat_tnh_k_kernel(tc, qT, kT, vT, doT, rw, qm, offs, out):
                     scale=neg_gate[:, t : t + 1],
                 )
 
-        def multiply_on_gpsimd(factor_part, first, count):
-            nc.gpsimd.tensor_tensor(
-                slot_major(ds1_packed)[:, first : first + count],
-                slot_major(factor_part),
-                gated[first // HALF][:, :, first % HALF : first % HALF + count].rearrange("p t n -> p n t"),
-                ALU.mult,
-            )
+        def multiply_on_gpsimd(h, factors, parts):
+            for slots in parts:
+                nc.gpsimd.tensor_tensor(
+                    slot_major(ds1_packed[h])[:, slots],
+                    slot_major(factors)[:, slots],
+                    gated[h].rearrange("p t n -> p n t")[:, slots],
+                    ALU.mult,
+                )
 
-        quantize(v_mx, E4M3, v1_packed)
+        deal(nc.scalar.copy, do1_packed, do1_rows, DO1_EARLY, P)
         quantize(do_mx[1], E5M2, do1_packed)
-        place(0, whole_list(0), banks[0][:], do1_tile[:, last * N + PACK * DO1_SECOND :])
-        place(1, whole_list(0), banks[1][:], do1_rows[:, 2, :])
-        for c in range(2):
+        copy_out(stages[:, 0, second], banks[0][:, second])
+        scatter(1, half_list(0, 1), stages[:, 0, second])
+        pack_on_gpsimd(qm1_packed, qm1_rows, 0, N - QM1_SCALAR)
+        pack_on_scalar(qm1_packed, qm1_rows, N - QM1_SCALAR, N)
+        quantize(qm_mx[1], E4M3, qm1_packed)
+        for c in (0, 1, last):
             tanh_chunk(c)
-        pack_on_gpsimd(qm1_packed[1], qm1_half_rows[1], 0, QM1_GPSIMD)
+        copy_out(qm1_rows[:, 0, first], banks[1][:, second])
+        scatter(0, half_list(0, 1), qm1_rows[:, 0, first])
+        key_grad(score_banks[0], 0, 2, N)
+        key_grad(score_banks[1], 0, last, N)
         dp1_banks = banks[2:PACK] + banks[0:2]
         for t in range(PACK):
             product(dp1_banks[t][:], do_mx[1], E5M2, t, v_mx, E4M3)
-        for c in range(2):
-            square(factor[c], factor[c])
-            nc.gpsimd.tensor_scalar(factor[c], factor[c], 1.0, -1.0, ALU.mult, ALU.add)
-        key_grad(score_banks[1], 0, 2)
+        first_factors, second_factors = qm1_packed.bitcast(F32), weights[:, 2 * N :]
+        square(weights[:, 0 : 2 * N], weights[:, 0 : 2 * N])
+        nc.gpsimd.tensor_scalar(first_factors, weights[:, 0 : 2 * N], 1.0, -1.0, ALU.mult, ALU.add)
+        copy_out(stages[:, 2, :], score_banks[0][:])
+        scatter(2, whole_list(0), stages[:, 2, :])
         gate_dp(0)
-        multiply_on_gpsimd(first_factors, 0, 2 * P)
+        copy_out(stages[:, last, first], score_banks[1][:, first])
+        scatter(last, half_list(0, 0), stages[:, last, first])
+        multiply_on_gpsimd(0, first_factors, [first])
+        square(factor[last], factor[last])
         tanh_chunk(2)
-        place(2, whole_list(0), score_banks[1][:], third_stage)
-        key_grad(score_banks[1], 0, last)
-        square(factor[2], factor[2])
+        less_one(factor[last], factor[last])
         gate_dp(1)
+        multiply_on_gpsimd(1, second_factors, [slice(HALF - TAIL, HALF)])
+        quantize_into(grad_mx, E5M2, 2 * N, 2 * N + HALF, ds1_packed[0])
+        square(factor[2], factor[2])
+        copy_out(first_factors[:, first], score_banks[1][:, second])
+        scatter(last, half_list(0, 1), first_factors[:, first])
         less_one(factor[2], factor[2])
-        multiply_on_gpsimd(factor[2], 2 * P, P)
-
-        tanh_chunk(last)
-        place(last, half_list(0, 0), score_banks[1][:, 0:HALF], half_stage[:])
-        halves = [slice(h * HALF, (h + 1) * HALF) for h in range(2)]
-        for words in halves:
-            square(last_square[:, words], factor[last][:, words])
-        for h, words in enumerate(halves):
-            less_one(factor[last][:, words], last_square[:, words])
-            multiply_on_gpsimd(factor[last][:, words], last * P + h * P // 2, P // 2)
-        pack_on_scalar(qm1_packed[0], qm1_half_rows[0], 0, HALF)
-        quantize_into(qm_mx[1], E4M3, 0, HALF, qm1_packed[0])
-        quantize(ds_mx[1], E5M2, ds1_packed)
-        pack_on_scalar(qm1_packed[1], qm1_half_rows[1], QM1_GPSIMD, HALF)
-        quantize_into(qm_mx[1], E4M3, HALF, N, qm1_packed[1])
-
-        dk1_banks = [score_banks[0], score_banks[2], score_banks[last], banks[0]]
-        for j in range(D // P):
-            key_grad(dk1_banks[j], 1, j)
-        place(last, half_list(0, 1), score_banks[1][:, HALF:N], factor[last][:, HALF:N])
-        for j in range(D // P):
-            place(j, whole_list(1), dk1_banks[j][:], final_stage[:, j, :])
+        for j in range(2):
+            key_grad(score_banks[2 + j], 1, j, N + HALF)
+        copy_out(stages[:, 0, first], score_banks[2][:, second])
+        scatter(0, half_list(1, 0), stages[:, 0, first])
+        multiply_on_gpsimd(1, second_factors, [slice(0, HALF - TAIL)])
+        quantize_into(grad_mx, E5M2, 2 * N + HALF, 3 * N, ds1_packed[1])
+        copy_out(second_factors[:, first], score_banks[last][:, second])
+        scatter(1, half_list(1, 0), second_factors[:, first])
+        for j in range(PACK):
+            key_grad(banks[j], 1, j, 2 * N)
+        for j in range(PACK):
+            slots = second if j < 2 else slice(0, N)
+            copy_out(stages[:, j, slots], banks[j][:, slots])
+            scatter(j, half_list(1, 1) if j < 2 else whole_list(1), stages[:, j, slots])
             nc.sync.dma_start(out=out[j * P : (j + 1) * P, :], in_=placed[j][:])

@@ -20,15 +20,7 @@ P = 128
 PACK = 4
 HALF = N // 2
 LIST_COLS = N // 16
-KEY_ORDER = (0, 2, 1, 3)
-RUN = 8
-RAW_BUFS = 6
-Q0_VECTOR = 32
-DO0_VECTOR = 52
-Q1_GPSIMD = 40
-DO1_EARLY = 24
-QM1_SCALAR = 64
-TAIL = 64
+RAW_BUFS = 10
 
 
 def tile_attend_gat_tnh_k_kernel(tc, qT, kT, vT, doT, rw, qm, offs, out):
@@ -48,45 +40,39 @@ def tile_attend_gat_tnh_k_kernel(tc, qT, kT, vT, doT, rw, qm, offs, out):
             nc.sync.dma_start(out=rows[:], in_=src.rearrange("(p j) w -> p j w", j=PACK))
             return rows[:]
 
-        def packed_tile(name):
-            return keep.tile([P, N * PACK], BF16, name=name, align_bytes=64)[:]
+        def packed_tile(name, tag=None):
+            return keep.tile([P, N * PACK], BF16, name=name, tag=tag or name, align_bytes=64)[:]
 
-        def mx_tiles(name, width=N):
-            codes = keep.tile([P, width], U32, name=name + "_codes", align_bytes=64)
-            scales = keep.tile([P, width], U8, name=name + "_scales", align_bytes=64)
+        def mx_tiles(name, tag=None):
+            codes = keep.tile([P, N], U32, name=name + "_codes", tag=tag or name + "_codes", align_bytes=64)
+            scales = keep.tile([P, N], U8, name=name + "_scales", align_bytes=64)
             return codes, scales
 
-        def whole_list(b):
-            return offsets[:, b * LIST_COLS : (b + 1) * LIST_COLS]
+        def entries(b, lo=0, hi=N):
+            return offsets[:, b * LIST_COLS + lo // 16 : b * LIST_COLS + hi // 16]
 
-        def half_list(b, h):
-            first = b * LIST_COLS + h * LIST_COLS // 2
-            return offsets[:, first : first + LIST_COLS // 2]
+        def gather(dst, window, b):
+            nc.vector.tensor_copy(dst, window.indirect(entries(b)))
 
-        def gather(dst, window, entries):
-            nc.vector.tensor_copy(dst, window.indirect(entries))
-
-        def gather_on_scalar(dst, cast, plane, entries):
-            nc.scalar.activation(cast[:], plane, ACT.Copy)
-            nc.scalar.activation(dst, cast[:].indirect(entries), ACT.Copy)
-
-        def move_on_gpsimd(dst, src):
-            nc.gpsimd.tensor_scalar(dst, src, 1.0, 0.0, ALU.mult, ALU.add)
+        def gather_on_scalar(dst, window, b):
+            nc.scalar.activation(dst, window.indirect(entries(b)), ACT.Copy)
 
         def pair_row(pairs, j):
             return pairs.rearrange("p (u n e) -> p u e n", u=2, e=2)[:, j // 2, j % 2, :]
 
-        def weave(copy, word, dst, pairs, h):
-            runs = slice(h * HALF // PACK, (h + 1) * HALF // PACK)
-            copy(
-                dst.bitcast(word).rearrange("p (c i u) -> p c u i", i=PACK, u=2),
-                pairs.bitcast(word).rearrange("p (u c i) -> p c u i", i=PACK, u=2)[:, runs],
+        def row(rows, j):
+            return rows[:, j * N : (j + 1) * N]
+
+        def weave(dst, pairs):
+            nc.vector.tensor_copy(
+                dst.bitcast(I32).rearrange("p (c i u) -> p c u i", i=PACK, u=2),
+                pairs.bitcast(I32).rearrange("p (u c i) -> p c u i", i=PACK, u=2),
             )
 
-        def weave_on_gpsimd(dst, pairs, lo, hi):
-            nc.gpsimd.tensor_copy(
-                dst.bitcast(U32).rearrange("p (n u) -> p n u", u=2)[:, lo:hi],
-                pairs.bitcast(U32).rearrange("p (u n) -> p n u", u=2)[:, lo:hi],
+        def interleave(dst, rows):
+            nc.scalar.copy(
+                dst.rearrange("p (c i j) -> p c j i", i=PACK, j=PACK),
+                rows.rearrange("p (j c i) -> p c j i", i=PACK, j=PACK),
             )
 
         def pack_views(order, dst, src, lo, hi):
@@ -96,30 +82,17 @@ def tile_attend_gat_tnh_k_kernel(tc, qT, kT, vT, doT, rw, qm, offs, out):
                 src.rearrange("p j (c i) -> " + order, i=PACK)[:, cs],
             )
 
-        def pack_on_scalar(dst, src, lo, hi):
-            nc.scalar.copy(*pack_views("p c j i", dst, src, lo, hi))
-
-        def pack_on_gpsimd(dst, src, lo, hi):
-            move_on_gpsimd(*pack_views("p c i j", dst, src, lo, hi))
-
-        def deal(copy, dst, src, lo=0, hi=P):
+        def deal(copy, dst, src):
             copy(
-                dst.rearrange("p (t m j) -> p m j t", t=PACK, j=PACK)[:, lo:hi],
-                src.rearrange("p j (m t) -> p m j t", t=PACK)[:, lo:hi],
+                dst.rearrange("p (t m j) -> p m j t", t=PACK, j=PACK),
+                src.rearrange("p j (m t) -> p m j t", t=PACK),
             )
-
-        def deal_on_gpsimd(dst, src, lo, hi):
-            move_on_gpsimd(
-                dst.rearrange("p (t m j) -> p m t j", t=PACK, j=PACK)[:, lo:hi],
-                src.rearrange("p j (m t) -> p m t j", t=PACK)[:, lo:hi],
-            )
-
-        def quantize_into(mx, fmt, lo, hi, src):
-            codes, scales = mx
-            nc.vector.quantize_mx(out=codes[:, lo:hi].bitcast(fmt), scales=scales[:, lo:hi], in_=src)
 
         def quantize(mx, fmt, packed, lo=0, hi=N):
-            quantize_into(mx, fmt, lo, hi, packed[:, lo * PACK : hi * PACK])
+            codes, scales = mx
+            nc.vector.quantize_mx(
+                out=codes[:, lo:hi].bitcast(fmt), scales=scales[:, lo:hi], in_=packed[:, lo * PACK : hi * PACK]
+            )
 
         def product(dst, left, left_fmt, block, right, right_fmt, lo=0, hi=N):
             cols = slice(block * P, (block + 1) * P)
@@ -133,34 +106,18 @@ def tile_attend_gat_tnh_k_kernel(tc, qT, kT, vT, doT, rw, qm, offs, out):
                 stop=True,
             )
 
-        def key_grad(bank, b, j, first):
-            product(bank[:], qm_mx[b], E4M3, j, grad_mx, E5M2, first, first + N)
-
-        def slot_major(x):
-            return x.rearrange("p (n t) -> p n t", t=PACK)
-
         offsets = keep.tile([P, B * LIST_COLS], U16, name="offsets")
-        k_planes = {0: load_plane(kT, "k_plane", 0)}
+        k_planes = [load_plane(kT, "k_plane", 0)]
         nc.sync.dma_start(offsets[:], offs)
-        for j in KEY_ORDER[1:]:
-            k_planes[j] = load_plane(kT, "k_plane", j)
-        q0_rows = load_rows(qT[0], "q0_rows")
+        k_planes.extend([load_plane(kT, "k_plane", j) for j in range(1, PACK)])
+        q_rows = [load_rows(qT[b], "q_rows%d" % b) for b in range(B)]
+        gate = keep.tile([P, B * PACK], F32, name="gate")
+        nc.sync.dma_start(
+            out=gate[:].rearrange("p (b t) -> p b t", b=B), in_=rw.rearrange("b (p t) o -> p b (t o)", t=PACK)
+        )
         v_planes = [load_plane(vT, "v_plane", j) for j in range(PACK)]
-        do0_start = 2 * N - HALF
-        do0_end = do0_start + PACK * N
-        around_do0 = keep.tile([P, do0_end + N], F32, name="around_do0", align_bytes=64)
-        do0_rows = around_do0[:, do0_start:do0_end].rearrange("p (j w) -> p j w", j=PACK)
-        nc.sync.dma_start(out=do0_rows, in_=doT[0].rearrange("(p j) w -> p j w", j=PACK))
-        gate = keep.tile([P, B, PACK], F32, name="gate")
-        nc.sync.dma_start(out=gate[:], in_=rw.rearrange("b (p t) o -> p b (t o)", t=PACK))
-        v1_q1 = keep.tile([P, 2 * N - 16 + PACK * N], F32, name="v1_q1", align_bytes=64)
-        v1_packed = v1_q1[:, 0 : 2 * N].bitcast(BF16)
-        q1_rows = v1_q1[:, 2 * N - 16 :].rearrange("p (j w) -> p j w", j=PACK)
-        nc.sync.dma_start(out=q1_rows, in_=qT[1].rearrange("(p j) w -> p j w", j=PACK))
-        ds0_qm0 = keep.tile([P, 2 * N - 16 + PACK * N], F32, name="ds0_qm0", align_bytes=64)
-        ds0_packed = ds0_qm0[:, 0 : 2 * N].bitcast(BF16)
-        qm0_rows = ds0_qm0[:, 2 * N - 16 :].rearrange("p (j w) -> p j w", j=PACK)
-        nc.sync.dma_start(out=qm0_rows, in_=qm[0].rearrange("(p j) w -> p j w", j=PACK))
+        do0_rows = load_rows(doT[0], "do0_rows")
+        qm0_rows = load_rows(qm[0], "qm0_rows")
         do1_rows = load_rows(doT[1], "do1_rows")
         qm1_rows = load_rows(qm[1], "qm1_rows")
 
@@ -169,226 +126,153 @@ def tile_attend_gat_tnh_k_kernel(tc, qT, kT, vT, doT, rw, qm, offs, out):
             tile = keep.tile([P, T], F32, name="placed%d" % j)
             nc.gpsimd.memset(tile[:], 0.0)
             placed.append(tile)
+        neg_gate = keep.tile([P, B * PACK], F32, name="neg_gate")
+        nc.gpsimd.tensor_scalar(neg_gate[:], gate[:], -1.0, 0.0, ALU.mult, ALU.add)
 
-        key_pairs = [packed_tile("key_pairs%d" % b) for b in range(B)]
-        cast_keys = keep.tile([P, T], BF16, name="cast_keys")
-        cast_values = keep.tile([P, T], BF16, name="cast_values")
-        value_rows = keep.tile([P, 2, N], BF16, name="value_rows")
-        value_pairs = [packed_tile("value_pairs0"), around_do0[:, 0 : 2 * N].bitcast(BF16)]
-        weights = keep.tile([P, N * PACK], F32, name="weights", align_bytes=64)
-        gated_dp = keep.tile([P, N * PACK], F32, name="gated_dp", align_bytes=64)
-        k0_packed, do1_packed = (packed_tile(name + "_packed") for name in ("k0", "do1"))
-        shared = 32
-        q0_k1 = keep.tile([P, 2 * PACK * N - shared], BF16, name="q0_k1", align_bytes=64)
-        q0_packed, k1_packed = q0_k1[:, 0 : PACK * N], q0_k1[:, PACK * N - shared :]
-        do0_q1 = keep.tile([P, 2 * PACK * N - shared], BF16, name="do0_q1", align_bytes=64)
-        do0_packed, q1_packed = do0_q1[:, 0 : PACK * N], do0_q1[:, PACK * N - shared :]
-        v0_qm1 = keep.tile([P, 2 * PACK * N - shared], BF16, name="v0_qm1", align_bytes=64)
-        v0_packed, qm1_packed = v0_qm1[:, 0 : PACK * N], v0_qm1[:, PACK * N - shared :]
-        qm0_packed = v0_packed
-        ds1_halves = keep.tile([P, PACK * N - shared], BF16, name="ds1_halves", align_bytes=64)
-        ds1_packed = [ds1_halves[:, 0 : 2 * N], ds1_halves[:, 2 * N - shared :]]
-        k_mx, q_mx = ([mx_tiles("%s%d" % (name, b)) for b in range(B)] for name in ("k", "q"))
-        v_mx = mx_tiles("v")
-        qm_mx = [mx_tiles("qm%d" % b) for b in range(B)]
-        grad_mx = mx_tiles("grad", 3 * N)
-        do_mx = [grad_mx, mx_tiles("do1")]
         banks = [psum.tile([P, N], F32, name="bank%d" % i) for i in range(8)]
-        neg_gate = keep.tile([P, PACK], F32, name="neg_gate")
-        last = PACK - 1
+        weights = [keep.tile([P, N * PACK], F32, name="weights%d" % b, align_bytes=64) for b in range(B)]
 
-        for j in KEY_ORDER:
-            gather(pair_row(key_pairs[1], j), k_planes[j], whole_list(1))
-            if j < 2:
-                gather_on_scalar(pair_row(key_pairs[0], j), cast_keys, k_planes[j], whole_list(0))
-            elif j < last:
-                gather(pair_row(key_pairs[0], j), k_planes[j], whole_list(0))
+        key_pairs = packed_tile("key_pairs", "pairs")
+        key_rows = packed_tile("key_rows", "rows")
+        for j in range(PACK):
+            gather(pair_row(key_pairs, j), k_planes[j], 0)
+            gather_on_scalar(row(key_rows, j), k_planes[j], 1)
+        k0_packed = packed_tile("k0_packed", "packed0")
+        k1_packed = packed_tile("k1_packed", "packed1")
+        weave(k0_packed, key_pairs)
+        interleave(k1_packed, key_rows)
+        k0_mx = mx_tiles("k0")
+        quantize(k0_mx, E4M3, k0_packed)
+        q_packed = [packed_tile("q%d_packed" % b) for b in range(B)]
+        q_mx = [mx_tiles("q%d" % b) for b in range(B)]
+        deal(nc.vector.tensor_copy, q_packed[0], q_rows[0])
+        quantize(q_mx[0], E4M3, q_packed[0])
+        k_mx = [k0_mx, mx_tiles("k1", "q0_packed")]
+        quantize(k_mx[1], E4M3, k1_packed)
+        deal(nc.vector.tensor_copy, q_packed[1], q_rows[1])
+        quantize(q_mx[1], E4M3, q_packed[1])
+
+        for b in range(B):
+            for t in range(PACK):
+                product(banks[b * PACK + t][:], q_mx[b], E4M3, t, k_mx[b], E4M3)
+            for t in range(PACK):
+                factor = row(weights[b][:], t)
+                col = slice(b * PACK + t, b * PACK + t + 1)
+                nc.scalar.activation(factor, banks[b * PACK + t][:], ACT.Tanh)
+                nc.scalar.activation(factor, factor, ACT.Square)
+                nc.gpsimd.tensor_scalar(factor, factor, neg_gate[:, col], gate[:, col], ALU.mult, ALU.add)
+
+        value_pairs = packed_tile("value_pairs", "pairs")
+        value_rows = packed_tile("value_rows", "rows")
+        for j in range(PACK):
+            gather(pair_row(value_pairs, j), v_planes[j], 0)
+            if j < PACK - 1:
+                gather(row(value_rows, j), v_planes[j], 1)
             else:
-                for h in range(2):
-                    gather(pair_row(key_pairs[0], j)[:, h * HALF : (h + 1) * HALF], k_planes[j], half_list(0, h))
-        weave_on_gpsimd(k1_packed, key_pairs[1], HALF, N)
-        deal(nc.scalar.copy, q0_packed, q0_rows, Q0_VECTOR, P)
-        for h in range(2):
-            weave(nc.vector.tensor_copy, I32, k0_packed[:, h * 2 * N : (h + 1) * 2 * N], key_pairs[0], h)
-        deal(nc.vector.tensor_copy, q0_packed, q0_rows, 0, Q0_VECTOR)
-        for h in range(2):
-            quantize(k_mx[0], E4M3, k0_packed, h * HALF, (h + 1) * HALF)
-        quantize(q_mx[0], E4M3, q0_packed)
-        weave_on_gpsimd(k1_packed, key_pairs[1], 0, HALF)
+                gather_on_scalar(row(value_rows, j), v_planes[j], 1)
+        v0_packed = packed_tile("v0_packed", "packed0")
+        v1_packed = packed_tile("v1_packed", "packed1")
+        weave(v0_packed, value_pairs)
+        interleave(v1_packed, value_rows)
+        v0_mx = mx_tiles("v0")
+        quantize(v0_mx, E4M3, v0_packed)
+        do_packed = [packed_tile("do%d_packed" % b) for b in range(B)]
+        do_mx = [mx_tiles("do%d" % b) for b in range(B)]
+        deal(nc.vector.tensor_copy, do_packed[0], do0_rows)
+        quantize(do_mx[0], E5M2, do_packed[0])
+        v_mx = [v0_mx, mx_tiles("v1", "do0_packed")]
+        quantize(v_mx[1], E4M3, v1_packed)
 
-        gather_on_scalar(value_rows[:, 0, :], cast_values, v_planes[0], whole_list(1))
-        gather(pair_row(value_pairs[0], 0), v_planes[0], whole_list(0))
-        for h in (1, 0):
-            quantize(k_mx[1], E4M3, k1_packed, h * HALF, (h + 1) * HALF)
-        gather(value_rows[:, 1, :], v_planes[1], whole_list(1))
-        gather(pair_row(value_pairs[0], 1), v_planes[1], whole_list(0))
-        move_on_gpsimd(
-            value_pairs[1][:, 0 : 2 * N].rearrange("p (n e) -> p n e", e=2), value_rows[:].rearrange("p e n -> p n e")
-        )
+        qm_packed = [packed_tile("qm%d_packed" % b) for b in range(B)]
+        qm_mx = [mx_tiles("qm%d" % b) for b in range(B)]
+        ds_packed = [packed_tile("ds%d_packed" % b) for b in range(B)]
+        ds_mx = [mx_tiles("ds%d" % b) for b in range(B)]
 
-        weight = [weights[:, t * N : (t + 1) * N] for t in range(PACK)]
-        for t in range(PACK):
-            product(banks[t][:], q_mx[0], E4M3, t, k_mx[0], E4M3)
-        for t in range(PACK):
-            nc.scalar.activation(weight[t], banks[t][:], ACT.Tanh)
-            nc.scalar.activation(weight[t], weight[t], ACT.Square)
-        for t in range(2):
-            nc.gpsimd.tensor_scalar(weight[t], weight[t], -1.0, 1.0, ALU.mult, ALU.add)
+        def value_products(b):
+            for c in range(PACK):
+                for t in range(PACK):
+                    product(banks[c][:, t * P : (t + 1) * P], do_mx[b], E5M2, t, v_mx[b], E4M3, c * P, (c + 1) * P)
 
-        def gather_value_half(b, j, h):
-            gather(pair_row(value_pairs[b], j)[:, h * HALF : (h + 1) * HALF], v_planes[j], half_list(b, h))
-
-        gather(pair_row(value_pairs[0], 2), v_planes[2], whole_list(0))
-        gather_value_half(1, 2, 0)
-        gather(pair_row(value_pairs[0], last), v_planes[last], whole_list(0))
-        gather_value_half(1, last, 0)
-        for h in range(2):
-            weave(nc.vector.tensor_copy, I32, v0_packed[:, h * 2 * N : (h + 1) * 2 * N], value_pairs[0], h)
-        for h in range(2):
-            quantize(v_mx, E4M3, v0_packed, h * HALF, (h + 1) * HALF)
-        deal(nc.scalar.copy, do0_packed, do0_rows, DO0_VECTOR, P)
-        deal(nc.vector.tensor_copy, do0_packed, do0_rows, 0, DO0_VECTOR)
-        late_weight = [around_do0[:, do0_end - HALF + (t - last) * N : do0_end + HALF + (t - last) * N] for t in range(2, PACK)]
-        for t in range(2, PACK):
-            nc.scalar.activation(late_weight[t - 2], weight[t], ACT.Copy, bias=1.0, scale=-1.0)
-        quantize(do_mx[0], E5M2, do0_packed)
-        for t in range(PACK):
-            product(banks[t][:], do_mx[0], E5M2, t, v_mx, E4M3)
-        for j in range(2, PACK):
-            gather_value_half(1, j, 1)
-        deal_on_gpsimd(q1_packed, q1_rows, 0, Q1_GPSIMD)
-
-        ds0_rows = k0_packed
-        for t, factor_t in enumerate(weight[0:2] + late_weight):
-            nc.vector.scalar_tensor_tensor(
-                ds0_rows[:, t * N : (t + 1) * N], banks[t][:], gate[:, 0, t : t + 1], factor_t, ALU.mult, ALU.mult
-            )
-        weave_on_gpsimd(v1_packed, value_pairs[1], 0, N)
-        deal(nc.scalar.copy, q1_packed, q1_rows, Q1_GPSIMD, P)
-        quantize(q_mx[1], E4M3, q1_packed, 0, HALF)
-
-        def pack_ds0(copy, h):
-            runs = slice(h * HALF // RUN, (h + 1) * HALF // RUN)
-            copy(
-                ds0_packed.rearrange("p (c i t) -> p c t i", i=RUN, t=PACK)[:, runs],
-                ds0_rows.rearrange("p (t c i) -> p c t i", i=RUN, t=PACK)[:, runs],
+        def score_grad(b, c):
+            runs = slice(c * P // PACK, (c + 1) * P // PACK)
+            nc.vector.tensor_tensor(
+                ds_packed[b].rearrange("p (c i t) -> p c t i", i=PACK, t=PACK)[:, runs],
+                banks[c][:].rearrange("p (t c i) -> p c t i", i=PACK, t=PACK),
+                weights[b][:].rearrange("p (t c i) -> p c t i", i=PACK, t=PACK)[:, runs],
+                ALU.mult,
             )
 
-        pack_on_scalar(qm0_packed, qm0_rows, 0, P)
-        pack_on_scalar(qm0_packed, qm0_rows, HALF, N)
-        pack_ds0(nc.vector.tensor_copy, 0)
-        pack_ds0(nc.scalar.copy, 1)
-        nc.vector.tensor_copy(*pack_views("p c j i", qm0_packed, qm0_rows, P, HALF))
-        quantize_into(grad_mx, E5M2, N, N + HALF, ds0_packed[:, 0 : 2 * N])
-        quantize(qm_mx[0], E4M3, qm0_packed, P, HALF)
-        key_grad(banks[PACK], 0, 1, HALF)
-        quantize(qm_mx[0], E4M3, qm0_packed, 0, P)
-        key_grad(banks[PACK + 1], 0, 0, HALF)
-        quantize(q_mx[1], E4M3, q1_packed, HALF, N)
-        quantize_into(grad_mx, E5M2, N + HALF, 2 * N, ds0_packed[:, 2 * N :])
-        for j in range(2):
-            key_grad(banks[j], 0, 1 - j, N)
-        quantize(v_mx, E4M3, v1_packed)
-        quantize(qm_mx[0], E4M3, qm0_packed, HALF, N)
-        nc.scalar.activation(neg_gate[:], gate[:, 1, :], ACT.Copy, scale=-1.0)
+        def key_grad(bank, b, j, lo, hi):
+            product(bank[:, 0 : hi - lo], qm_mx[b], E4M3, j, ds_mx[b], E5M2, lo, hi)
 
-        factor = weight
-        stages = keep.tile([P, 4, N], F32, name="stages")
+        def stage_tile(name, width, tag=None):
+            return keep.tile([P, width], F32, name=name, tag=tag or name, align_bytes=64)[:]
 
-        def copy_out(stage, source):
-            nc.scalar.copy(stage, source)
+        def place_on_vector(j, b, lo, hi, bank, stage):
+            nc.vector.tensor_copy(stage, bank[:, 0 : hi - lo])
+            nc.vector.tensor_copy(placed[j][:].indirect(entries(b, lo, hi)), stage)
 
-        def scatter(j, entries, stage):
-            nc.vector.tensor_copy(placed[j][:].indirect(entries), stage)
-
-        first, second = slice(0, HALF), slice(HALF, N)
-        deal(nc.scalar.copy, do1_packed, do1_rows, 0, DO1_EARLY)
-        for j in range(2):
-            copy_out(stages[:, j, first], banks[PACK + j][:, second])
-            scatter(1 - j, half_list(0, 0), stages[:, j, first])
-        score_banks = banks[PACK : 2 * PACK]
-        for c in range(PACK):
-            for t in range(PACK):
-                product(score_banks[c][:, t * P : (t + 1) * P], q_mx[1], E4M3, t, k_mx[1], E4M3, c * P, (c + 1) * P)
-
-        gated = [
-            gated_dp[:, h * 2 * N : (h + 1) * 2 * N].rearrange("p (t n) -> p t n", t=PACK) for h in range(2)
-        ]
-
-        def tanh_chunk(c):
-            nc.scalar.activation(slot_major(factor[c]), score_banks[c][:].rearrange("p (t n) -> p n t", t=PACK), ACT.Tanh)
-
-        def square(dst, src):
-            nc.scalar.activation(dst, src, ACT.Square)
-
-        def less_one(dst, src):
-            nc.scalar.activation(dst, src, ACT.Copy, bias=-1.0)
-
-        def gate_dp(h):
-            for t in range(PACK):
+        def place_on_scalar(j, b, lo, hi, bank, stage):
+            nc.scalar.copy(stage, bank[:, 0 : hi - lo])
+            for first in range(lo, hi, HALF):
                 nc.scalar.activation(
-                    gated[h][:, t, :],
-                    dp1_banks[t][:, h * HALF : (h + 1) * HALF],
+                    placed[j][:].indirect(entries(b, first, first + HALF)),
+                    stage[:, first - lo : first - lo + HALF],
                     ACT.Copy,
-                    scale=neg_gate[:, t : t + 1],
                 )
 
-        def multiply_on_gpsimd(h, factors, parts):
-            for slots in parts:
-                nc.gpsimd.tensor_tensor(
-                    slot_major(ds1_packed[h])[:, slots],
-                    slot_major(factors)[:, slots],
-                    gated[h].rearrange("p t n -> p n t")[:, slots],
-                    ALU.mult,
-                )
+        def store(queue, j):
+            queue.dma_start(out=out[j * P : (j + 1) * P, :], in_=placed[j][:])
 
-        deal(nc.scalar.copy, do1_packed, do1_rows, DO1_EARLY, P)
-        quantize(do_mx[1], E5M2, do1_packed)
-        copy_out(stages[:, 0, second], banks[0][:, second])
-        scatter(1, half_list(0, 1), stages[:, 0, second])
-        pack_on_gpsimd(qm1_packed, qm1_rows, 0, N - QM1_SCALAR)
-        pack_on_scalar(qm1_packed, qm1_rows, N - QM1_SCALAR, N)
-        quantize(qm_mx[1], E4M3, qm1_packed)
-        for c in (0, 1, last):
-            tanh_chunk(c)
-        copy_out(qm1_rows[:, 0, first], banks[1][:, second])
-        scatter(0, half_list(0, 1), qm1_rows[:, 0, first])
-        key_grad(score_banks[0], 0, 2, N)
-        key_grad(score_banks[1], 0, last, N)
-        dp1_banks = banks[2:PACK] + banks[0:2]
-        for t in range(PACK):
-            product(dp1_banks[t][:], do_mx[1], E5M2, t, v_mx, E4M3)
-        first_factors, second_factors = qm1_packed.bitcast(F32), weights[:, 2 * N :]
-        square(weights[:, 0 : 2 * N], weights[:, 0 : 2 * N])
-        nc.gpsimd.tensor_scalar(first_factors, weights[:, 0 : 2 * N], 1.0, -1.0, ALU.mult, ALU.add)
-        copy_out(stages[:, 2, :], score_banks[0][:])
-        scatter(2, whole_list(0), stages[:, 2, :])
-        gate_dp(0)
-        copy_out(stages[:, last, first], score_banks[1][:, first])
-        scatter(last, half_list(0, 0), stages[:, last, first])
-        multiply_on_gpsimd(0, first_factors, [first])
-        square(factor[last], factor[last])
-        tanh_chunk(2)
-        less_one(factor[last], factor[last])
-        gate_dp(1)
-        multiply_on_gpsimd(1, second_factors, [slice(HALF - TAIL, HALF)])
-        quantize_into(grad_mx, E5M2, 2 * N, 2 * N + HALF, ds1_packed[0])
-        square(factor[2], factor[2])
-        copy_out(first_factors[:, first], score_banks[1][:, second])
-        scatter(last, half_list(0, 1), first_factors[:, first])
-        less_one(factor[2], factor[2])
-        for j in range(2):
-            key_grad(score_banks[2 + j], 1, j, N + HALF)
-        copy_out(stages[:, 0, first], score_banks[2][:, second])
-        scatter(0, half_list(1, 0), stages[:, 0, first])
-        multiply_on_gpsimd(1, second_factors, [slice(0, HALF - TAIL)])
-        quantize_into(grad_mx, E5M2, 2 * N + HALF, 3 * N, ds1_packed[1])
-        copy_out(second_factors[:, first], score_banks[last][:, second])
-        scatter(1, half_list(1, 0), second_factors[:, first])
-        for j in range(PACK):
-            key_grad(banks[j], 1, j, 2 * N)
-        for j in range(PACK):
-            slots = second if j < 2 else slice(0, N)
-            copy_out(stages[:, j, slots], banks[j][:, slots])
-            scatter(j, half_list(1, 1) if j < 2 else whole_list(1), stages[:, j, slots])
-            nc.sync.dma_start(out=out[j * P : (j + 1) * P, :], in_=placed[j][:])
+        value_products(0)
+        for h in range(2):
+            nc.scalar.copy(*pack_views("p c j i", qm_packed[0], qm0_rows, h * HALF, (h + 1) * HALF))
+        deal(nc.scalar.copy, do_packed[1], do1_rows)
+        nc.gpsimd.tensor_scalar(*pack_views("p c i j", qm_packed[1], qm1_rows, 0, N), 1.0, 0.0, ALU.mult, ALU.add)
+        score_grad(0, 0)
+        score_grad(0, 1)
+        quantize(qm_mx[0], E4M3, qm_packed[0], 0, HALF)
+        quantize(ds_mx[0], E5M2, ds_packed[0], 0, HALF)
+        key_grad(banks[4], 0, 0, 0, HALF)
+        key_grad(banks[5], 0, 1, 0, HALF)
+        score_grad(0, 2)
+        score_grad(0, 3)
+        quantize(ds_mx[0], E5M2, ds_packed[0], HALF, N)
+        key_grad(banks[6], 0, 0, HALF, N)
+        key_grad(banks[7], 0, 1, HALF, N)
+        place_on_vector(0, 0, 0, HALF, banks[4], stage_tile("stage_a0a", HALF))
+        place_on_scalar(1, 0, 0, HALF, banks[5], do1_rows[:, 0, 0:HALF])
+        quantize(do_mx[1], E5M2, do_packed[1])
+        quantize(qm_mx[0], E4M3, qm_packed[0], HALF, N)
+        value_products(1)
+        key_grad(banks[5], 0, 3, 0, N)
+        place_on_vector(0, 0, HALF, N, banks[6], stage_tile("stage_a0b", HALF, "do1_packed"))
+        place_on_scalar(1, 0, HALF, N, banks[7], do1_rows[:, 0, HALF:N])
+        key_grad(banks[7], 0, 2, 0, HALF)
+        place_on_scalar(3, 0, 0, N, banks[5], do1_rows[:, 1, :])
+        score_grad(1, 0)
+        score_grad(1, 1)
+        quantize(qm_mx[1], E4M3, qm_packed[1])
+        quantize(ds_mx[1], E5M2, ds_packed[1], 0, HALF)
+        key_grad(banks[4], 1, 0, 0, HALF)
+        key_grad(banks[5], 1, 1, 0, HALF)
+        score_grad(1, 2)
+        score_grad(1, 3)
+        quantize(ds_mx[1], E5M2, ds_packed[1], HALF, N)
+        place_on_scalar(2, 0, 0, HALF, banks[7], do1_rows[:, 2, 0:HALF])
+        key_grad(banks[6], 1, 0, HALF, N)
+        key_grad(banks[7], 1, 1, HALF, N)
+        key_grad(banks[3], 0, 2, HALF, N)
+        place_on_vector(0, 1, 0, HALF, banks[4], stage_tile("stage_a1a", HALF))
+        place_on_scalar(1, 1, 0, HALF, banks[5], do1_rows[:, 2, HALF:N])
+        key_grad(banks[4], 1, 2, 0, N)
+        key_grad(banks[5], 1, 3, 0, N)
+        place_on_vector(0, 1, HALF, N, banks[6], stage_tile("stage_a1b", HALF))
+        store(nc.sync, 0)
+        place_on_scalar(1, 1, HALF, N, banks[7], do1_rows[:, 3, 0:HALF])
+        store(nc.scalar, 1)
+        place_on_vector(2, 0, HALF, N, banks[3], stage_tile("stage_c0b", HALF))
+        place_on_scalar(3, 1, 0, N, banks[5], stage_tile("stage_d1", N))
+        store(nc.scalar, 3)
+        place_on_vector(2, 1, 0, N, banks[4], stage_tile("stage_c1", N))
+        store(nc.sync, 2)

@@ -21,6 +21,11 @@ PACK = 4
 HALF = N // 2
 LIST_COLS = N // 16
 RAW_BUFS = 10
+RUN = 8
+LINK = 32
+Q1_VECTOR = 40
+DO1_GPSIMD = 40
+SQUARES_GPSIMD = 2
 
 
 def tile_attend_gat_tnh_k_kernel(tc, qT, kT, vT, doT, rw, qm, offs, out):
@@ -51,8 +56,8 @@ def tile_attend_gat_tnh_k_kernel(tc, qT, kT, vT, doT, rw, qm, offs, out):
         def entries(b, lo=0, hi=N):
             return offsets[:, b * LIST_COLS + lo // 16 : b * LIST_COLS + hi // 16]
 
-        def gather(dst, window, b):
-            nc.vector.tensor_copy(dst, window.indirect(entries(b)))
+        def gather(dst, window, b, lo=0, hi=N):
+            nc.vector.tensor_copy(dst[:, lo:hi], window.indirect(entries(b, lo, hi)))
 
         def gather_on_scalar(dst, window, b):
             nc.scalar.activation(dst, window.indirect(entries(b)), ACT.Copy)
@@ -63,10 +68,17 @@ def tile_attend_gat_tnh_k_kernel(tc, qT, kT, vT, doT, rw, qm, offs, out):
         def row(rows, j):
             return rows[:, j * N : (j + 1) * N]
 
-        def weave(dst, pairs):
-            nc.vector.tensor_copy(
-                dst.bitcast(I32).rearrange("p (c i u) -> p c u i", i=PACK, u=2),
-                pairs.bitcast(I32).rearrange("p (u c i) -> p c u i", i=PACK, u=2),
+        def weave(dst, pairs, lo=0, hi=N, copy=nc.vector.tensor_copy, word=I32):
+            runs = slice(lo // PACK, hi // PACK)
+            copy(
+                dst.bitcast(word).rearrange("p (c i u) -> p c u i", i=PACK, u=2)[:, runs],
+                pairs.bitcast(word).rearrange("p (u c i) -> p c u i", i=PACK, u=2)[:, runs],
+            )
+
+        def weave_on_gpsimd(dst, pairs, lo, hi):
+            nc.gpsimd.tensor_copy(
+                dst.bitcast(U32).rearrange("p (n u) -> p n u", u=2),
+                pairs.bitcast(U32).rearrange("p (u n) -> p n u", u=2)[:, lo:hi],
             )
 
         def interleave(dst, rows):
@@ -78,21 +90,31 @@ def tile_attend_gat_tnh_k_kernel(tc, qT, kT, vT, doT, rw, qm, offs, out):
         def pack_views(order, dst, src, lo, hi):
             cs = slice(lo // PACK, hi // PACK)
             return (
-                dst.rearrange("p (c i j) -> " + order, i=PACK, j=PACK)[:, cs],
+                dst.rearrange("p (c i j) -> " + order, i=PACK, j=PACK),
                 src.rearrange("p j (c i) -> " + order, i=PACK)[:, cs],
             )
 
-        def deal(copy, dst, src):
+        def deal(copy, dst, src, lo=0, hi=P):
             copy(
-                dst.rearrange("p (t m j) -> p m j t", t=PACK, j=PACK),
-                src.rearrange("p j (m t) -> p m j t", t=PACK),
+                dst.rearrange("p (t m j) -> p m j t", t=PACK, j=PACK)[:, lo:hi],
+                src.rearrange("p j (m t) -> p m j t", t=PACK)[:, lo:hi],
             )
 
-        def quantize(mx, fmt, packed, lo=0, hi=N):
-            codes, scales = mx
-            nc.vector.quantize_mx(
-                out=codes[:, lo:hi].bitcast(fmt), scales=scales[:, lo:hi], in_=packed[:, lo * PACK : hi * PACK]
+        def move_on_gpsimd(dst, src):
+            nc.gpsimd.tensor_scalar(dst, src, 1.0, 0.0, ALU.mult, ALU.add)
+
+        def deal_on_gpsimd(dst, src, lo, hi):
+            move_on_gpsimd(
+                dst.rearrange("p (t m j) -> p m t j", t=PACK, j=PACK)[:, lo:hi],
+                src.rearrange("p j (m t) -> p m t j", t=PACK)[:, lo:hi],
             )
+
+        def quantize_into(mx, fmt, lo, hi, src):
+            codes, scales = mx
+            nc.vector.quantize_mx(out=codes[:, lo:hi].bitcast(fmt), scales=scales[:, lo:hi], in_=src)
+
+        def quantize(mx, fmt, packed, lo=0, hi=N):
+            quantize_into(mx, fmt, lo, hi, packed[:, lo * PACK : hi * PACK])
 
         def product(dst, left, left_fmt, block, right, right_fmt, lo=0, hi=N):
             cols = slice(block * P, (block + 1) * P)
@@ -115,9 +137,15 @@ def tile_attend_gat_tnh_k_kernel(tc, qT, kT, vT, doT, rw, qm, offs, out):
         nc.sync.dma_start(
             out=gate[:].rearrange("p (b t) -> p b t", b=B), in_=rw.rearrange("b (p t) o -> p b (t o)", t=PACK)
         )
-        v_planes = [load_plane(vT, "v_plane", j) for j in range(PACK)]
         do0_rows = load_rows(doT[0], "do0_rows")
-        qm0_rows = load_rows(qm[0], "qm0_rows")
+        v_planes = [load_plane(vT, "v_plane", j) for j in range(PACK)]
+        words = PACK * N
+        link = LINK // 2
+        ds0_start = words - link
+        factor_start = ds0_start + N - link
+        behind_qm0 = keep.tile([P, factor_start + words], F32, name="behind_qm0", align_bytes=64)
+        qm0_rows = behind_qm0[:, 0:words].rearrange("p (j w) -> p j w", j=PACK)
+        nc.sync.dma_start(out=qm0_rows, in_=qm[0].rearrange("(p j) w -> p j w", j=PACK))
         do1_rows = load_rows(doT[1], "do1_rows")
         qm1_rows = load_rows(qm[1], "qm1_rows")
 
@@ -130,7 +158,10 @@ def tile_attend_gat_tnh_k_kernel(tc, qT, kT, vT, doT, rw, qm, offs, out):
         nc.gpsimd.tensor_scalar(neg_gate[:], gate[:], -1.0, 0.0, ALU.mult, ALU.add)
 
         banks = [psum.tile([P, N], F32, name="bank%d" % i) for i in range(8)]
-        weights = [keep.tile([P, N * PACK], F32, name="weights%d" % b, align_bytes=64) for b in range(B)]
+        weights1 = keep.tile([P, N * PACK], F32, name="weights1", align_bytes=64)
+        weights = [behind_qm0[:, factor_start:], weights1[:]]
+        late_qm1 = keep.tile([P, 2 * N - link + 2 * N], F32, name="late_qm1", align_bytes=64)
+        late_squares = late_qm1[:, 0 : 2 * N]
 
         key_pairs = packed_tile("key_pairs", "pairs")
         key_rows = packed_tile("key_rows", "rows")
@@ -145,47 +176,70 @@ def tile_attend_gat_tnh_k_kernel(tc, qT, kT, vT, doT, rw, qm, offs, out):
         quantize(k0_mx, E4M3, k0_packed)
         q_packed = [packed_tile("q%d_packed" % b) for b in range(B)]
         q_mx = [mx_tiles("q%d" % b) for b in range(B)]
+        k_mx = [k0_mx, mx_tiles("k1")]
         deal(nc.vector.tensor_copy, q_packed[0], q_rows[0])
-        quantize(q_mx[0], E4M3, q_packed[0])
-        k_mx = [k0_mx, mx_tiles("k1", "q0_packed")]
         quantize(k_mx[1], E4M3, k1_packed)
-        deal(nc.vector.tensor_copy, q_packed[1], q_rows[1])
+        quantize(q_mx[0], E4M3, q_packed[0])
+        deal(nc.scalar.copy, q_packed[1], q_rows[1], Q1_VECTOR, P)
+        deal(nc.vector.tensor_copy, q_packed[1], q_rows[1], 0, Q1_VECTOR)
         quantize(q_mx[1], E4M3, q_packed[1])
-
-        for b in range(B):
-            for t in range(PACK):
-                product(banks[b * PACK + t][:], q_mx[b], E4M3, t, k_mx[b], E4M3)
-            for t in range(PACK):
-                factor = row(weights[b][:], t)
-                col = slice(b * PACK + t, b * PACK + t + 1)
-                nc.scalar.activation(factor, banks[b * PACK + t][:], ACT.Tanh)
-                nc.scalar.activation(factor, factor, ACT.Square)
-                nc.gpsimd.tensor_scalar(factor, factor, neg_gate[:, col], gate[:, col], ALU.mult, ALU.add)
-
-        value_pairs = packed_tile("value_pairs", "pairs")
-        value_rows = packed_tile("value_rows", "rows")
-        for j in range(PACK):
-            gather(pair_row(value_pairs, j), v_planes[j], 0)
-            if j < PACK - 1:
-                gather(row(value_rows, j), v_planes[j], 1)
-            else:
-                gather_on_scalar(row(value_rows, j), v_planes[j], 1)
-        v0_packed = packed_tile("v0_packed", "packed0")
-        v1_packed = packed_tile("v1_packed", "packed1")
-        weave(v0_packed, value_pairs)
-        interleave(v1_packed, value_rows)
-        v0_mx = mx_tiles("v0")
-        quantize(v0_mx, E4M3, v0_packed)
-        do_packed = [packed_tile("do%d_packed" % b) for b in range(B)]
+        do0_packed = packed_tile("do0_packed")
         do_mx = [mx_tiles("do%d" % b) for b in range(B)]
-        deal(nc.vector.tensor_copy, do_packed[0], do0_rows)
-        quantize(do_mx[0], E5M2, do_packed[0])
-        v_mx = [v0_mx, mx_tiles("v1", "do0_packed")]
-        quantize(v_mx[1], E4M3, v1_packed)
+        deal(nc.vector.tensor_copy, do0_packed, do0_rows)
+        quantize(do_mx[0], E5M2, do0_packed)
 
-        qm_packed = [packed_tile("qm%d_packed" % b) for b in range(B)]
+        def gate_factor(b, t, square):
+            col = slice(b * PACK + t, b * PACK + t + 1)
+            nc.gpsimd.tensor_scalar(row(weights[b], t), square, neg_gate[:, col], gate[:, col], ALU.mult, ALU.add)
+
+        for t in range(PACK):
+            product(banks[t][:], q_mx[0], E4M3, t, k_mx[0], E4M3)
+        for t in range(PACK):
+            factor = row(weights[0], t)
+            nc.scalar.activation(factor, banks[t][:], ACT.Tanh)
+            if t < SQUARES_GPSIMD:
+                square = row(do0_packed.bitcast(F32), t)
+                nc.gpsimd.tensor_tensor(square, factor, factor, ALU.mult)
+            else:
+                square = factor
+                nc.scalar.activation(square, factor, ACT.Square)
+            gate_factor(0, t, square)
+        for t in (2, 3, 0, 1):
+            product(banks[PACK + t][:], q_mx[1], E4M3, t, k_mx[1], E4M3)
+            square = row(late_squares if t < 2 else weights[1], t)
+            nc.scalar.activation(square, banks[PACK + t][:], ACT.Tanh)
+            nc.scalar.activation(square, square, ACT.Square)
+            if t >= 2:
+                gate_factor(1, t, square)
+
+        ds0_first = behind_qm0[:, ds0_start : ds0_start + N].bitcast(BF16)
+        qm0_early = keep.tile([P, 2 * N], BF16, name="qm0_early", align_bytes=64)[:]
+        qm1_early = late_qm1[:, 2 * N - link : 3 * N - link].bitcast(BF16)
+        do1_packed = weights[1][:, 0 : 2 * N].bitcast(BF16)
+        ds1_first = keep.tile([P, 2 * N], BF16, name="ds1_first", align_bytes=64)[:]
+        ds_halves = [[ds0_first, qm0_early], [ds1_first, qm1_early]]
+
+        value_pairs = [packed_tile("value_pairs0", "pairs"), packed_tile("value_pairs1", "rows")]
+        value_rows = keep.tile([P, 2 * N], BF16, name="value_rows")[:]
+        for j in range(PACK - 1):
+            gather(pair_row(value_pairs[0], j), v_planes[j], 0)
+            if j < 2:
+                gather(pair_row(value_pairs[1], j), v_planes[j], 1)
+        v0_packed = packed_tile("v0_packed", "packed0")
+        v_mx = [mx_tiles("v0"), mx_tiles("v1")]
+        for lo in (0, HALF):
+            gather(pair_row(value_pairs[0], PACK - 1), v_planes[PACK - 1], 0, lo, lo + HALF)
+            weave(v0_packed, value_pairs[0], lo, lo + HALF)
+            quantize(v_mx[0], E4M3, v0_packed, lo, lo + HALF)
+        for j in range(2, PACK):
+            gather_on_scalar(row(value_rows, j - 2), v_planes[j], 1)
+        nc.scalar.copy(
+            value_pairs[1][:, 2 * N :].rearrange("p (c i e) -> p c e i", i=RUN, e=2),
+            value_rows.rearrange("p (e c i) -> p c e i", i=RUN, e=2),
+        )
+
         qm_mx = [mx_tiles("qm%d" % b) for b in range(B)]
-        ds_packed = [packed_tile("ds%d_packed" % b) for b in range(B)]
+        qm0_late = keep.tile([P, 2 * N], BF16, name="qm0_late", align_bytes=64)[:]
         ds_mx = [mx_tiles("ds%d" % b) for b in range(B)]
 
         def value_products(b):
@@ -196,83 +250,109 @@ def tile_attend_gat_tnh_k_kernel(tc, qT, kT, vT, doT, rw, qm, offs, out):
         def score_grad(b, c):
             runs = slice(c * P // PACK, (c + 1) * P // PACK)
             nc.vector.tensor_tensor(
-                ds_packed[b].rearrange("p (c i t) -> p c t i", i=PACK, t=PACK)[:, runs],
+                ds_halves[b][c // 2][:, (c % 2) * N : (c % 2 + 1) * N].rearrange("p (c i t) -> p c t i", i=PACK, t=PACK),
                 banks[c][:].rearrange("p (t c i) -> p c t i", i=PACK, t=PACK),
-                weights[b][:].rearrange("p (t c i) -> p c t i", i=PACK, t=PACK)[:, runs],
+                weights[b].rearrange("p (t c i) -> p c t i", i=PACK, t=PACK)[:, runs],
                 ALU.mult,
             )
 
-        def key_grad(bank, b, j, lo, hi):
-            product(bank[:, 0 : hi - lo], qm_mx[b], E4M3, j, ds_mx[b], E5M2, lo, hi)
+        def key_grad(bank, b, j, lo, hi, at=0):
+            product(bank[:, at : at + hi - lo], qm_mx[b], E4M3, j, ds_mx[b], E5M2, lo, hi)
 
         def stage_tile(name, width, tag=None):
             return keep.tile([P, width], F32, name=name, tag=tag or name, align_bytes=64)[:]
 
-        def place_on_vector(j, b, lo, hi, bank, stage):
-            nc.vector.tensor_copy(stage, bank[:, 0 : hi - lo])
+        def scatter_on_vector(j, b, lo, hi, stage):
             nc.vector.tensor_copy(placed[j][:].indirect(entries(b, lo, hi)), stage)
 
-        def place_on_scalar(j, b, lo, hi, bank, stage):
-            nc.scalar.copy(stage, bank[:, 0 : hi - lo])
-            for first in range(lo, hi, HALF):
-                nc.scalar.activation(
-                    placed[j][:].indirect(entries(b, first, first + HALF)),
-                    stage[:, first - lo : first - lo + HALF],
-                    ACT.Copy,
-                )
+        def scatter_on_scalar(j, b, lo, stage):
+            nc.scalar.activation(placed[j][:].indirect(entries(b, lo, lo + HALF)), stage, ACT.Copy)
 
         def store(queue, j):
             queue.dma_start(out=out[j * P : (j + 1) * P, :], in_=placed[j][:])
 
+        def quantize_ds(b, h):
+            quantize_into(ds_mx[b], E5M2, h * HALF, (h + 1) * HALF, ds_halves[b][h])
+
         value_products(0)
-        for h in range(2):
-            nc.scalar.copy(*pack_views("p c j i", qm_packed[0], qm0_rows, h * HALF, (h + 1) * HALF))
-        deal(nc.scalar.copy, do_packed[1], do1_rows)
-        nc.gpsimd.tensor_scalar(*pack_views("p c i j", qm_packed[1], qm1_rows, 0, N), 1.0, 0.0, ALU.mult, ALU.add)
+        nc.vector.tensor_copy(*pack_views("p c j i", qm0_early, qm0_rows, HALF, N))
+        nc.scalar.copy(*pack_views("p c j i", qm0_late, qm0_rows, 0, HALF))
+        deal(nc.scalar.copy, do1_packed, do1_rows)
         score_grad(0, 0)
         score_grad(0, 1)
-        quantize(qm_mx[0], E4M3, qm_packed[0], 0, HALF)
-        quantize(ds_mx[0], E5M2, ds_packed[0], 0, HALF)
-        key_grad(banks[4], 0, 0, 0, HALF)
-        key_grad(banks[5], 0, 1, 0, HALF)
+        quantize_into(qm_mx[0], E4M3, HALF, N, qm0_early)
+        quantize_into(qm_mx[0], E4M3, 0, HALF, qm0_late)
+        quantize_ds(0, 0)
+        weave_on_gpsimd(qm0_late, value_pairs[1], 0, HALF)
+        weave_on_gpsimd(ds0_first, value_pairs[1], HALF, N)
+        key_grad(banks[4], 0, 2, 0, HALF)
+        key_grad(banks[4], 0, 3, 0, HALF, HALF)
+        key_grad(banks[6], 0, 1, 0, HALF)
         score_grad(0, 2)
         score_grad(0, 3)
-        quantize(ds_mx[0], E5M2, ds_packed[0], HALF, N)
-        key_grad(banks[6], 0, 0, HALF, N)
-        key_grad(banks[7], 0, 1, HALF, N)
-        place_on_vector(0, 0, 0, HALF, banks[4], stage_tile("stage_a0a", HALF))
-        place_on_scalar(1, 0, 0, HALF, banks[5], do1_rows[:, 0, 0:HALF])
-        quantize(do_mx[1], E5M2, do_packed[1])
-        quantize(qm_mx[0], E4M3, qm_packed[0], HALF, N)
+        quantize_into(v_mx[1], E4M3, 0, HALF, qm0_late)
+        quantize_ds(0, 1)
+        key_grad(banks[5], 0, 2, HALF, N)
+        key_grad(banks[5], 0, 1, HALF, N, HALF)
+        quantize(do_mx[1], E5M2, do1_packed)
+        quantize_into(v_mx[1], E4M3, HALF, N, ds0_first)
+        for t in range(2):
+            gate_factor(1, t, row(late_squares, t))
+        move_on_gpsimd(*pack_views("p c i j", qm1_early, qm1_rows, P, P + HALF))
+
+        stage = [do1_rows[:, j, h * HALF : (h + 1) * HALF] for j in range(PACK) for h in range(2)]
+        nc.scalar.copy(stage[0], banks[4][:, 0:HALF])
+        nc.scalar.copy(stage[1], banks[4][:, HALF:N])
+        first = stage_tile("stage_first", HALF)
+        nc.vector.tensor_copy(first, banks[6][:, 0:HALF])
         value_products(1)
-        key_grad(banks[5], 0, 3, 0, N)
-        place_on_vector(0, 0, HALF, N, banks[6], stage_tile("stage_a0b", HALF, "do1_packed"))
-        place_on_scalar(1, 0, HALF, N, banks[7], do1_rows[:, 0, HALF:N])
-        key_grad(banks[7], 0, 2, 0, HALF)
-        place_on_scalar(3, 0, 0, N, banks[5], do1_rows[:, 1, :])
+        scatter_on_vector(1, 0, 0, HALF, first)
+        scatter_on_scalar(2, 0, 0, stage[0])
+        scatter_on_scalar(3, 0, 0, stage[1])
+        nc.scalar.copy(stage[0], banks[5][:, 0:HALF])
+        nc.scalar.copy(stage[2], banks[5][:, HALF:N])
+        scatter_on_scalar(2, 0, HALF, stage[0])
+        scatter_on_scalar(1, 0, HALF, stage[2])
         score_grad(1, 0)
         score_grad(1, 1)
-        quantize(qm_mx[1], E4M3, qm_packed[1])
-        quantize(ds_mx[1], E5M2, ds_packed[1], 0, HALF)
-        key_grad(banks[4], 1, 0, 0, HALF)
-        key_grad(banks[5], 1, 1, 0, HALF)
+        quantize_into(qm_mx[1], E4M3, P, P + HALF, qm1_early)
+        quantize_ds(1, 0)
+        key_grad(banks[7], 1, 2, 0, HALF)
+        key_grad(banks[6], 1, 1, 0, HALF)
         score_grad(1, 2)
         score_grad(1, 3)
-        quantize(ds_mx[1], E5M2, ds_packed[1], HALF, N)
-        place_on_scalar(2, 0, 0, HALF, banks[7], do1_rows[:, 2, 0:HALF])
-        key_grad(banks[6], 1, 0, HALF, N)
-        key_grad(banks[7], 1, 1, HALF, N)
-        key_grad(banks[3], 0, 2, HALF, N)
-        place_on_vector(0, 1, 0, HALF, banks[4], stage_tile("stage_a1a", HALF))
-        place_on_scalar(1, 1, 0, HALF, banks[5], do1_rows[:, 2, HALF:N])
-        key_grad(banks[4], 1, 2, 0, N)
-        key_grad(banks[5], 1, 3, 0, N)
-        place_on_vector(0, 1, HALF, N, banks[6], stage_tile("stage_a1b", HALF))
-        store(nc.sync, 0)
-        place_on_scalar(1, 1, HALF, N, banks[7], do1_rows[:, 3, 0:HALF])
-        store(nc.scalar, 1)
-        place_on_vector(2, 0, HALF, N, banks[3], stage_tile("stage_c0b", HALF))
-        place_on_scalar(3, 1, 0, N, banks[5], stage_tile("stage_d1", N))
-        store(nc.scalar, 3)
-        place_on_vector(2, 1, 0, N, banks[4], stage_tile("stage_c1", N))
+        nc.vector.tensor_copy(first, banks[6][:, 0:HALF])
+        quantize_ds(1, 1)
+        qm1_late = ds_halves[1][1]
+        for i, j in enumerate((0, 3)):
+            move_on_gpsimd(*pack_views("p c i j", qm1_late[:, i * N : (i + 1) * N], qm1_rows, j * P, (j + 1) * P))
+        key_grad(banks[1], 1, 1, HALF, N)
+        key_grad(banks[0], 1, 2, HALF, N)
+        key_grad(banks[0], 0, 3, HALF, N, HALF)
+        key_grad(banks[2], 0, 0, 0, N)
+        scatter_on_vector(1, 1, 0, HALF, first)
+        second = stage_tile("stage_second", HALF)
+        nc.vector.tensor_copy(second, banks[1][:, 0:HALF])
+        scatter_on_vector(1, 1, HALF, N, second)
+        for i, j in enumerate((0, 3)):
+            quantize_into(qm_mx[1], E4M3, j * P, (j + 1) * P, qm1_late[:, i * N : (i + 1) * N])
+        key_grad(banks[3], 1, 0, 0, N)
+        key_grad(banks[4], 1, 3, 0, N)
+        nc.scalar.copy(stage[3], banks[7][:, 0:HALF])
+        scatter_on_scalar(2, 1, 0, stage[3])
+        nc.scalar.copy(stage[4], banks[0][:, 0:HALF])
+        nc.scalar.copy(stage[5], banks[0][:, HALF:N])
+        scatter_on_scalar(2, 1, HALF, stage[4])
         store(nc.sync, 2)
+        store(nc.sync, 1)
+        scatter_on_scalar(3, 0, HALF, stage[5])
+        nc.scalar.copy(stage[6], banks[4][:, 0:HALF])
+        nc.scalar.copy(stage[7], banks[4][:, HALF:N])
+        scatter_on_scalar(3, 1, 0, stage[6])
+        scatter_on_scalar(3, 1, HALF, stage[7])
+        store(nc.sync, 3)
+        rest = late_qm1[:, 2 * N - link :]
+        nc.vector.tensor_copy(rest[:, 0:N], banks[2][:])
+        nc.vector.tensor_copy(rest[:, N:], banks[3][:])
+        scatter_on_vector(0, 0, 0, 2 * N, rest)
+        store(nc.sync, 0)

@@ -23,9 +23,9 @@ LIST_COLS = N // 16
 RAW_BUFS = 10
 RUN = 8
 LINK = 32
-Q1_VECTOR = 40
-DO1_GPSIMD = 40
-SQUARES_GPSIMD = 2
+Q1_VECTOR = 56
+DO1_VECTOR = 24
+SQUARES_GPSIMD = 0
 
 
 def tile_attend_gat_tnh_k_kernel(tc, qT, kT, vT, doT, rw, qm, offs, out):
@@ -79,6 +79,12 @@ def tile_attend_gat_tnh_k_kernel(tc, qT, kT, vT, doT, rw, qm, offs, out):
             nc.gpsimd.tensor_copy(
                 dst.bitcast(U32).rearrange("p (n u) -> p n u", u=2),
                 pairs.bitcast(U32).rearrange("p (u n) -> p n u", u=2)[:, lo:hi],
+            )
+
+        def weave_part(dst, pairs, lo, hi):
+            nc.vector.tensor_copy(
+                dst.bitcast(I32).rearrange("p (c i u) -> p c u i", i=PACK, u=2),
+                pairs.bitcast(I32).rearrange("p (u c i) -> p c u i", i=PACK, u=2)[:, lo // PACK : hi // PACK],
             )
 
         def interleave(dst, rows):
@@ -154,32 +160,27 @@ def tile_attend_gat_tnh_k_kernel(tc, qT, kT, vT, doT, rw, qm, offs, out):
             tile = keep.tile([P, T], F32, name="placed%d" % j)
             nc.gpsimd.memset(tile[:], 0.0)
             placed.append(tile)
-        neg_gate = keep.tile([P, B * PACK], F32, name="neg_gate")
-        nc.gpsimd.tensor_scalar(neg_gate[:], gate[:], -1.0, 0.0, ALU.mult, ALU.add)
 
         banks = [psum.tile([P, N], F32, name="bank%d" % i) for i in range(8)]
         weights1 = keep.tile([P, N * PACK], F32, name="weights1", align_bytes=64)
         weights = [behind_qm0[:, factor_start:], weights1[:]]
         late_qm1 = keep.tile([P, 2 * N - link + 2 * N], F32, name="late_qm1", align_bytes=64)
-        late_squares = late_qm1[:, 0 : 2 * N]
 
-        key_pairs = packed_tile("key_pairs", "pairs")
+        k0_packed = packed_tile("k0_packed", "packed0")
         key_rows = packed_tile("key_rows", "rows")
         for j in range(PACK):
-            gather(pair_row(key_pairs, j), k_planes[j], 0)
+            gather(k0_packed.rearrange("p (n j) -> p j n", j=PACK)[:, j, :], k_planes[j], 0)
             gather_on_scalar(row(key_rows, j), k_planes[j], 1)
-        k0_packed = packed_tile("k0_packed", "packed0")
         k1_packed = packed_tile("k1_packed", "packed1")
-        weave(k0_packed, key_pairs)
         interleave(k1_packed, key_rows)
         k0_mx = mx_tiles("k0")
         quantize(k0_mx, E4M3, k0_packed)
         q_packed = [packed_tile("q%d_packed" % b) for b in range(B)]
         q_mx = [mx_tiles("q%d" % b) for b in range(B)]
-        k_mx = [k0_mx, mx_tiles("k1")]
+        k_mx = [k0_mx, mx_tiles("k1", "q0_packed")]
         deal(nc.vector.tensor_copy, q_packed[0], q_rows[0])
-        quantize(k_mx[1], E4M3, k1_packed)
         quantize(q_mx[0], E4M3, q_packed[0])
+        quantize(k_mx[1], E4M3, k1_packed)
         deal(nc.scalar.copy, q_packed[1], q_rows[1], Q1_VECTOR, P)
         deal(nc.vector.tensor_copy, q_packed[1], q_rows[1], 0, Q1_VECTOR)
         quantize(q_mx[1], E4M3, q_packed[1])
@@ -187,6 +188,9 @@ def tile_attend_gat_tnh_k_kernel(tc, qT, kT, vT, doT, rw, qm, offs, out):
         do_mx = [mx_tiles("do%d" % b) for b in range(B)]
         deal(nc.vector.tensor_copy, do0_packed, do0_rows)
         quantize(do_mx[0], E5M2, do0_packed)
+
+        neg_gate = row(do0_packed.bitcast(F32), 1)[:, 0 : B * PACK]
+        nc.gpsimd.tensor_scalar(neg_gate, gate[:], -1.0, 0.0, ALU.mult, ALU.add)
 
         def gate_factor(b, t, square):
             col = slice(b * PACK + t, b * PACK + t + 1)
@@ -204,18 +208,17 @@ def tile_attend_gat_tnh_k_kernel(tc, qT, kT, vT, doT, rw, qm, offs, out):
                 square = factor
                 nc.scalar.activation(square, factor, ACT.Square)
             gate_factor(0, t, square)
-        for t in (2, 3, 0, 1):
+        for t in range(PACK):
             product(banks[PACK + t][:], q_mx[1], E4M3, t, k_mx[1], E4M3)
-            square = row(late_squares if t < 2 else weights[1], t)
+            square = row(weights[1], t)
             nc.scalar.activation(square, banks[PACK + t][:], ACT.Tanh)
             nc.scalar.activation(square, square, ACT.Square)
-            if t >= 2:
-                gate_factor(1, t, square)
+            gate_factor(1, t, square)
 
         ds0_first = behind_qm0[:, ds0_start : ds0_start + N].bitcast(BF16)
         qm0_early = keep.tile([P, 2 * N], BF16, name="qm0_early", align_bytes=64)[:]
         qm1_early = late_qm1[:, 2 * N - link : 3 * N - link].bitcast(BF16)
-        do1_packed = weights[1][:, 0 : 2 * N].bitcast(BF16)
+        do1_packed = late_qm1[:, 0 : 2 * N].bitcast(BF16)
         ds1_first = keep.tile([P, 2 * N], BF16, name="ds1_first", align_bytes=64)[:]
         ds_halves = [[ds0_first, qm0_early], [ds1_first, qm1_early]]
 
@@ -277,34 +280,35 @@ def tile_attend_gat_tnh_k_kernel(tc, qT, kT, vT, doT, rw, qm, offs, out):
         value_products(0)
         nc.vector.tensor_copy(*pack_views("p c j i", qm0_early, qm0_rows, HALF, N))
         nc.scalar.copy(*pack_views("p c j i", qm0_late, qm0_rows, 0, HALF))
-        deal(nc.scalar.copy, do1_packed, do1_rows)
+        deal(nc.scalar.copy, do1_packed, do1_rows, DO1_VECTOR, P)
         score_grad(0, 0)
         score_grad(0, 1)
         quantize_into(qm_mx[0], E4M3, HALF, N, qm0_early)
         quantize_into(qm_mx[0], E4M3, 0, HALF, qm0_late)
         quantize_ds(0, 0)
-        weave_on_gpsimd(qm0_late, value_pairs[1], 0, HALF)
+        weave_part(qm0_late, value_pairs[1], 0, HALF)
         weave_on_gpsimd(ds0_first, value_pairs[1], HALF, N)
         key_grad(banks[4], 0, 2, 0, HALF)
         key_grad(banks[4], 0, 3, 0, HALF, HALF)
         key_grad(banks[6], 0, 1, 0, HALF)
         score_grad(0, 2)
         score_grad(0, 3)
+        deal(nc.vector.tensor_copy, do1_packed, do1_rows, 0, DO1_VECTOR)
         quantize_into(v_mx[1], E4M3, 0, HALF, qm0_late)
         quantize_ds(0, 1)
         key_grad(banks[5], 0, 2, HALF, N)
         key_grad(banks[5], 0, 1, HALF, N, HALF)
-        quantize(do_mx[1], E5M2, do1_packed)
         quantize_into(v_mx[1], E4M3, HALF, N, ds0_first)
-        for t in range(2):
-            gate_factor(1, t, row(late_squares, t))
+        first = stage_tile("stage_first", HALF)
+        nc.vector.tensor_copy(first, banks[6][:, 0:HALF])
+        quantize(do_mx[1], E5M2, do1_packed)
         move_on_gpsimd(*pack_views("p c i j", qm1_early, qm1_rows, P, P + HALF))
 
         stage = [do1_rows[:, j, h * HALF : (h + 1) * HALF] for j in range(PACK) for h in range(2)]
+        opening = stage_tile("stage_opening", N)
+        stage = [opening[:, 0:HALF], opening[:, HALF:N]] + stage[2:]
         nc.scalar.copy(stage[0], banks[4][:, 0:HALF])
         nc.scalar.copy(stage[1], banks[4][:, HALF:N])
-        first = stage_tile("stage_first", HALF)
-        nc.vector.tensor_copy(first, banks[6][:, 0:HALF])
         value_products(1)
         scatter_on_vector(1, 0, 0, HALF, first)
         scatter_on_scalar(2, 0, 0, stage[0])
@@ -351,7 +355,7 @@ def tile_attend_gat_tnh_k_kernel(tc, qT, kT, vT, doT, rw, qm, offs, out):
         scatter_on_scalar(3, 1, 0, stage[6])
         scatter_on_scalar(3, 1, HALF, stage[7])
         store(nc.sync, 3)
-        rest = late_qm1[:, 2 * N - link :]
+        rest = weights[1][:, 2 * N :]
         nc.vector.tensor_copy(rest[:, 0:N], banks[2][:])
         nc.vector.tensor_copy(rest[:, N:], banks[3][:])
         scatter_on_vector(0, 0, 0, 2 * N, rest)

@@ -19,13 +19,13 @@ ALU = mybir.AluOpType
 P = 128
 PACK = 4
 HALF = N // 2
+ROWS = PACK * N
 LIST_COLS = N // 16
-RAW_BUFS = 10
 RUN = 8
-LINK = 32
+LINK = 16
+RAW_BUFS = 10
 Q1_VECTOR = 56
-DO1_VECTOR = 24
-SQUARES_GPSIMD = 0
+DO1_VECTOR = 48
 
 
 def tile_attend_gat_tnh_k_kernel(tc, qT, kT, vT, doT, rw, qm, offs, out):
@@ -40,13 +40,21 @@ def tile_attend_gat_tnh_k_kernel(tc, qT, kT, vT, doT, rw, qm, offs, out):
             nc.sync.dma_start(out=plane[:], in_=pool_ap.rearrange("(p j) t -> p j t", j=PACK)[:, j, :])
             return plane[:]
 
+        def load_rows_into(words, src):
+            rows = words.rearrange("p (j w) -> p j w", j=PACK)
+            nc.sync.dma_start(out=rows, in_=src.rearrange("(p j) w -> p j w", j=PACK))
+            return rows
+
         def load_rows(src, label):
             rows = ring.tile([P, PACK, N], F32, name=label, tag="raw", bufs=RAW_BUFS, align_bytes=64)
             nc.sync.dma_start(out=rows[:], in_=src.rearrange("(p j) w -> p j w", j=PACK))
             return rows[:]
 
-        def packed_tile(name, tag=None):
-            return keep.tile([P, N * PACK], BF16, name=name, tag=tag or name, align_bytes=64)[:]
+        def packed_tile(name, tag=None, columns=N):
+            return keep.tile([P, columns * PACK], BF16, name=name, tag=tag or name, align_bytes=64)[:]
+
+        def stage_tile(name, width):
+            return keep.tile([P, width], F32, name=name, align_bytes=64)[:]
 
         def mx_tiles(name, tag=None):
             codes = keep.tile([P, N], U32, name=name + "_codes", tag=tag or name + "_codes", align_bytes=64)
@@ -56,49 +64,35 @@ def tile_attend_gat_tnh_k_kernel(tc, qT, kT, vT, doT, rw, qm, offs, out):
         def entries(b, lo=0, hi=N):
             return offsets[:, b * LIST_COLS + lo // 16 : b * LIST_COLS + hi // 16]
 
+        def row(rows, j):
+            return rows[:, j * N : (j + 1) * N]
+
+        def pair_row(pairs, j):
+            return pairs.rearrange("p (u n e) -> p u e n", u=2, e=2)[:, j // 2, j % 2, :]
+
         def gather(dst, window, b, lo=0, hi=N):
             nc.vector.tensor_copy(dst[:, lo:hi], window.indirect(entries(b, lo, hi)))
 
         def gather_on_scalar(dst, window, b):
             nc.scalar.activation(dst, window.indirect(entries(b)), ACT.Copy)
 
-        def pair_row(pairs, j):
-            return pairs.rearrange("p (u n e) -> p u e n", u=2, e=2)[:, j // 2, j % 2, :]
-
-        def row(rows, j):
-            return rows[:, j * N : (j + 1) * N]
-
-        def weave(dst, pairs, lo=0, hi=N, copy=nc.vector.tensor_copy, word=I32):
-            runs = slice(lo // PACK, hi // PACK)
-            copy(
-                dst.bitcast(word).rearrange("p (c i u) -> p c u i", i=PACK, u=2)[:, runs],
-                pairs.bitcast(word).rearrange("p (u c i) -> p c u i", i=PACK, u=2)[:, runs],
-            )
-
-        def weave_on_gpsimd(dst, pairs, lo, hi):
-            nc.gpsimd.tensor_copy(
-                dst.bitcast(U32).rearrange("p (n u) -> p n u", u=2),
-                pairs.bitcast(U32).rearrange("p (u n) -> p n u", u=2)[:, lo:hi],
-            )
-
-        def weave_part(dst, pairs, lo, hi):
+        def weave(dst, pairs, lo):
             nc.vector.tensor_copy(
                 dst.bitcast(I32).rearrange("p (c i u) -> p c u i", i=PACK, u=2),
-                pairs.bitcast(I32).rearrange("p (u c i) -> p c u i", i=PACK, u=2)[:, lo // PACK : hi // PACK],
-            )
-
-        def interleave(dst, rows):
-            nc.scalar.copy(
-                dst.rearrange("p (c i j) -> p c j i", i=PACK, j=PACK),
-                rows.rearrange("p (j c i) -> p c j i", i=PACK, j=PACK),
+                pairs.bitcast(I32).rearrange("p (u c i) -> p c u i", i=PACK, u=2)[:, lo // PACK : (lo + HALF) // PACK],
             )
 
         def pack_views(order, dst, src, lo, hi):
-            cs = slice(lo // PACK, hi // PACK)
             return (
                 dst.rearrange("p (c i j) -> " + order, i=PACK, j=PACK),
-                src.rearrange("p j (c i) -> " + order, i=PACK)[:, cs],
+                src.rearrange("p j (c i) -> " + order, i=PACK)[:, lo // PACK : hi // PACK],
             )
+
+        def pack(copy, dst, src, lo, hi):
+            copy(*pack_views("p c j i", dst, src, lo, hi))
+
+        def pack_on_gpsimd(dst, src, lo, hi):
+            nc.gpsimd.tensor_scalar(*pack_views("p c i j", dst, src, lo, hi), 1.0, 0.0, ALU.mult, ALU.add)
 
         def deal(copy, dst, src, lo=0, hi=P):
             copy(
@@ -106,21 +100,9 @@ def tile_attend_gat_tnh_k_kernel(tc, qT, kT, vT, doT, rw, qm, offs, out):
                 src.rearrange("p j (m t) -> p m j t", t=PACK)[:, lo:hi],
             )
 
-        def move_on_gpsimd(dst, src):
-            nc.gpsimd.tensor_scalar(dst, src, 1.0, 0.0, ALU.mult, ALU.add)
-
-        def deal_on_gpsimd(dst, src, lo, hi):
-            move_on_gpsimd(
-                dst.rearrange("p (t m j) -> p m t j", t=PACK, j=PACK)[:, lo:hi],
-                src.rearrange("p j (m t) -> p m t j", t=PACK)[:, lo:hi],
-            )
-
-        def quantize_into(mx, fmt, lo, hi, src):
-            codes, scales = mx
-            nc.vector.quantize_mx(out=codes[:, lo:hi].bitcast(fmt), scales=scales[:, lo:hi], in_=src)
-
         def quantize(mx, fmt, packed, lo=0, hi=N):
-            quantize_into(mx, fmt, lo, hi, packed[:, lo * PACK : hi * PACK])
+            codes, scales = mx
+            nc.vector.quantize_mx(out=codes[:, lo:hi].bitcast(fmt), scales=scales[:, lo:hi], in_=packed)
 
         def product(dst, left, left_fmt, block, right, right_fmt, lo=0, hi=N):
             cols = slice(block * P, (block + 1) * P)
@@ -138,20 +120,18 @@ def tile_attend_gat_tnh_k_kernel(tc, qT, kT, vT, doT, rw, qm, offs, out):
         k_planes = [load_plane(kT, "k_plane", 0)]
         nc.sync.dma_start(offsets[:], offs)
         k_planes.extend([load_plane(kT, "k_plane", j) for j in range(1, PACK)])
-        q_rows = [load_rows(qT[b], "q_rows%d" % b) for b in range(B)]
+        qm0_start = N
+        ds0_start = qm0_start + ROWS - LINK
+        factor0_start = ds0_start + N - LINK
+        around_qm0 = keep.tile([P, factor0_start + ROWS], F32, name="around_qm0", align_bytes=64)
+        q_rows = [load_rows(qT[0], "q0_rows"), load_rows_into(around_qm0[:, factor0_start:], qT[1])]
         gate = keep.tile([P, B * PACK], F32, name="gate")
         nc.sync.dma_start(
             out=gate[:].rearrange("p (b t) -> p b t", b=B), in_=rw.rearrange("b (p t) o -> p b (t o)", t=PACK)
         )
         do0_rows = load_rows(doT[0], "do0_rows")
         v_planes = [load_plane(vT, "v_plane", j) for j in range(PACK)]
-        words = PACK * N
-        link = LINK // 2
-        ds0_start = words - link
-        factor_start = ds0_start + N - link
-        behind_qm0 = keep.tile([P, factor_start + words], F32, name="behind_qm0", align_bytes=64)
-        qm0_rows = behind_qm0[:, 0:words].rearrange("p (j w) -> p j w", j=PACK)
-        nc.sync.dma_start(out=qm0_rows, in_=qm[0].rearrange("(p j) w -> p j w", j=PACK))
+        qm0_rows = load_rows_into(around_qm0[:, qm0_start : qm0_start + ROWS], qm[0])
         do1_rows = load_rows(doT[1], "do1_rows")
         qm1_rows = load_rows(qm[1], "qm1_rows")
 
@@ -162,17 +142,18 @@ def tile_attend_gat_tnh_k_kernel(tc, qT, kT, vT, doT, rw, qm, offs, out):
             placed.append(tile)
 
         banks = [psum.tile([P, N], F32, name="bank%d" % i) for i in range(8)]
-        weights1 = keep.tile([P, N * PACK], F32, name="weights1", align_bytes=64)
-        weights = [behind_qm0[:, factor_start:], weights1[:]]
-        late_qm1 = keep.tile([P, 2 * N - link + 2 * N], F32, name="late_qm1", align_bytes=64)
+        factor1 = keep.tile([P, ROWS], F32, name="factor1", align_bytes=64)
+        factors = [around_qm0[:, factor0_start:], factor1[:]]
+        do1_qm1 = keep.tile([P, 3 * N - LINK], F32, name="do1_qm1", align_bytes=64)
+        last = PACK - 1
 
         k0_packed = packed_tile("k0_packed", "packed0")
-        key_rows = packed_tile("key_rows", "rows")
+        key_rows = packed_tile("key_rows")
         for j in range(PACK):
             gather(k0_packed.rearrange("p (n j) -> p j n", j=PACK)[:, j, :], k_planes[j], 0)
             gather_on_scalar(row(key_rows, j), k_planes[j], 1)
-        k1_packed = packed_tile("k1_packed", "packed1")
-        interleave(k1_packed, key_rows)
+        k1_packed = packed_tile("k1_packed")
+        pack(nc.scalar.copy, k1_packed, key_rows.rearrange("p (j n) -> p j n", j=PACK), 0, N)
         k0_mx = mx_tiles("k0")
         quantize(k0_mx, E4M3, k0_packed)
         q_packed = [packed_tile("q%d_packed" % b) for b in range(B)]
@@ -192,57 +173,50 @@ def tile_attend_gat_tnh_k_kernel(tc, qT, kT, vT, doT, rw, qm, offs, out):
         neg_gate = row(do0_packed.bitcast(F32), 1)[:, 0 : B * PACK]
         nc.gpsimd.tensor_scalar(neg_gate, gate[:], -1.0, 0.0, ALU.mult, ALU.add)
 
-        def gate_factor(b, t, square):
+        def scores(b, t):
+            product(banks[b * PACK + t][:], q_mx[b], E4M3, t, k_mx[b], E4M3)
+
+        def make_factor(b, t):
+            factor = row(factors[b], t)
             col = slice(b * PACK + t, b * PACK + t + 1)
-            nc.gpsimd.tensor_scalar(row(weights[b], t), square, neg_gate[:, col], gate[:, col], ALU.mult, ALU.add)
+            nc.scalar.activation(factor, banks[b * PACK + t][:], ACT.Tanh)
+            nc.scalar.activation(factor, factor, ACT.Square)
+            nc.gpsimd.tensor_scalar(factor, factor, neg_gate[:, col], gate[:, col], ALU.mult, ALU.add)
 
         for t in range(PACK):
-            product(banks[t][:], q_mx[0], E4M3, t, k_mx[0], E4M3)
+            scores(0, t)
         for t in range(PACK):
-            factor = row(weights[0], t)
-            nc.scalar.activation(factor, banks[t][:], ACT.Tanh)
-            if t < SQUARES_GPSIMD:
-                square = row(do0_packed.bitcast(F32), t)
-                nc.gpsimd.tensor_tensor(square, factor, factor, ALU.mult)
-            else:
-                square = factor
-                nc.scalar.activation(square, factor, ACT.Square)
-            gate_factor(0, t, square)
+            make_factor(0, t)
         for t in range(PACK):
-            product(banks[PACK + t][:], q_mx[1], E4M3, t, k_mx[1], E4M3)
-            square = row(weights[1], t)
-            nc.scalar.activation(square, banks[PACK + t][:], ACT.Tanh)
-            nc.scalar.activation(square, square, ACT.Square)
-            gate_factor(1, t, square)
+            scores(1, t)
+            make_factor(1, t)
 
-        ds0_first = behind_qm0[:, ds0_start : ds0_start + N].bitcast(BF16)
-        qm0_early = keep.tile([P, 2 * N], BF16, name="qm0_early", align_bytes=64)[:]
-        qm1_early = late_qm1[:, 2 * N - link : 3 * N - link].bitcast(BF16)
-        do1_packed = late_qm1[:, 0 : 2 * N].bitcast(BF16)
-        ds1_first = keep.tile([P, 2 * N], BF16, name="ds1_first", align_bytes=64)[:]
-        ds_halves = [[ds0_first, qm0_early], [ds1_first, qm1_early]]
+        qm0_early = packed_tile("qm0_early", columns=HALF)
+        do1_packed = do1_qm1[:, 0 : 2 * N].bitcast(BF16)
+        qm1_early = do1_qm1[:, 2 * N - LINK :].bitcast(BF16)
+        ds_halves = [
+            [around_qm0[:, ds0_start : ds0_start + N].bitcast(BF16), qm0_early],
+            [packed_tile("ds1_first", columns=HALF), qm1_early],
+        ]
 
-        value_pairs = [packed_tile("value_pairs0", "pairs"), packed_tile("value_pairs1", "rows")]
+        value_pairs = [packed_tile("value_pairs0"), around_qm0[:, 0 : 2 * N].bitcast(BF16)]
         value_rows = keep.tile([P, 2 * N], BF16, name="value_rows")[:]
-        for j in range(PACK - 1):
+        for j in range(last):
             gather(pair_row(value_pairs[0], j), v_planes[j], 0)
             if j < 2:
                 gather(pair_row(value_pairs[1], j), v_planes[j], 1)
         v0_packed = packed_tile("v0_packed", "packed0")
-        v_mx = [mx_tiles("v0"), mx_tiles("v1")]
+        v_mx = [mx_tiles("v%d" % b) for b in range(B)]
         for lo in (0, HALF):
-            gather(pair_row(value_pairs[0], PACK - 1), v_planes[PACK - 1], 0, lo, lo + HALF)
-            weave(v0_packed, value_pairs[0], lo, lo + HALF)
-            quantize(v_mx[0], E4M3, v0_packed, lo, lo + HALF)
+            half_packed = v0_packed[:, lo * PACK : (lo + HALF) * PACK]
+            gather(pair_row(value_pairs[0], last), v_planes[last], 0, lo, lo + HALF)
+            weave(half_packed, value_pairs[0], lo)
+            quantize(v_mx[0], E4M3, half_packed, lo, lo + HALF)
         for j in range(2, PACK):
             gather_on_scalar(row(value_rows, j - 2), v_planes[j], 1)
-        nc.scalar.copy(
-            value_pairs[1][:, 2 * N :].rearrange("p (c i e) -> p c e i", i=RUN, e=2),
-            value_rows.rearrange("p (e c i) -> p c e i", i=RUN, e=2),
-        )
 
         qm_mx = [mx_tiles("qm%d" % b) for b in range(B)]
-        qm0_late = keep.tile([P, 2 * N], BF16, name="qm0_late", align_bytes=64)[:]
+        qm0_late = packed_tile("qm0_late", columns=HALF)
         ds_mx = [mx_tiles("ds%d" % b) for b in range(B)]
 
         def value_products(b):
@@ -251,19 +225,24 @@ def tile_attend_gat_tnh_k_kernel(tc, qT, kT, vT, doT, rw, qm, offs, out):
                     product(banks[c][:, t * P : (t + 1) * P], do_mx[b], E5M2, t, v_mx[b], E4M3, c * P, (c + 1) * P)
 
         def score_grad(b, c):
-            runs = slice(c * P // PACK, (c + 1) * P // PACK)
             nc.vector.tensor_tensor(
-                ds_halves[b][c // 2][:, (c % 2) * N : (c % 2 + 1) * N].rearrange("p (c i t) -> p c t i", i=PACK, t=PACK),
+                row(ds_halves[b][c // 2], c % 2).rearrange("p (c i t) -> p c t i", i=PACK, t=PACK),
                 banks[c][:].rearrange("p (t c i) -> p c t i", i=PACK, t=PACK),
-                weights[b].rearrange("p (t c i) -> p c t i", i=PACK, t=PACK)[:, runs],
+                factors[b].rearrange("p (t c i) -> p c t i", i=PACK, t=PACK)[:, c * P // PACK : (c + 1) * P // PACK],
                 ALU.mult,
             )
 
-        def key_grad(bank, b, j, lo, hi, at=0):
-            product(bank[:, at : at + hi - lo], qm_mx[b], E4M3, j, ds_mx[b], E5M2, lo, hi)
+        def quantize_ds(b, h):
+            quantize(ds_mx[b], E5M2, ds_halves[b][h], h * HALF, (h + 1) * HALF)
 
-        def stage_tile(name, width, tag=None):
-            return keep.tile([P, width], F32, name=name, tag=tag or name, align_bytes=64)[:]
+        def key_grad(dst, b, j, lo, hi):
+            product(dst, qm_mx[b], E4M3, j, ds_mx[b], E5M2, lo, hi)
+
+        def left(i):
+            return banks[i][:, 0:HALF]
+
+        def right(i):
+            return banks[i][:, HALF:N]
 
         def scatter_on_vector(j, b, lo, hi, stage):
             nc.vector.tensor_copy(placed[j][:].indirect(entries(b, lo, hi)), stage)
@@ -271,92 +250,97 @@ def tile_attend_gat_tnh_k_kernel(tc, qT, kT, vT, doT, rw, qm, offs, out):
         def scatter_on_scalar(j, b, lo, stage):
             nc.scalar.activation(placed[j][:].indirect(entries(b, lo, lo + HALF)), stage, ACT.Copy)
 
-        def store(queue, j):
-            queue.dma_start(out=out[j * P : (j + 1) * P, :], in_=placed[j][:])
-
-        def quantize_ds(b, h):
-            quantize_into(ds_mx[b], E5M2, h * HALF, (h + 1) * HALF, ds_halves[b][h])
+        def store(j):
+            nc.sync.dma_start(out=out[j * P : (j + 1) * P, :], in_=placed[j][:])
 
         value_products(0)
-        nc.vector.tensor_copy(*pack_views("p c j i", qm0_early, qm0_rows, HALF, N))
-        nc.scalar.copy(*pack_views("p c j i", qm0_late, qm0_rows, 0, HALF))
+        pack(nc.vector.tensor_copy, qm0_early, qm0_rows, HALF, N)
+        pack(nc.scalar.copy, qm0_late, qm0_rows, 0, HALF)
+        nc.scalar.copy(
+            value_pairs[1][:, 2 * N :].rearrange("p (c i e) -> p c e i", i=RUN, e=2),
+            value_rows.rearrange("p (e c i) -> p c e i", i=RUN, e=2),
+        )
         deal(nc.scalar.copy, do1_packed, do1_rows, DO1_VECTOR, P)
         score_grad(0, 0)
         score_grad(0, 1)
-        quantize_into(qm_mx[0], E4M3, HALF, N, qm0_early)
-        quantize_into(qm_mx[0], E4M3, 0, HALF, qm0_late)
+        quantize(qm_mx[0], E4M3, qm0_early, HALF, N)
+        quantize(qm_mx[0], E4M3, qm0_late, 0, HALF)
         quantize_ds(0, 0)
-        weave_part(qm0_late, value_pairs[1], 0, HALF)
-        weave_on_gpsimd(ds0_first, value_pairs[1], HALF, N)
-        key_grad(banks[4], 0, 2, 0, HALF)
-        key_grad(banks[4], 0, 3, 0, HALF, HALF)
-        key_grad(banks[6], 0, 1, 0, HALF)
+        v1_halves = [qm0_late, ds_halves[0][0]]
+        weave(v1_halves[0], value_pairs[1], 0)
+        nc.gpsimd.tensor_copy(
+            v1_halves[1].bitcast(U32).rearrange("p (n u) -> p n u", u=2),
+            value_pairs[1].bitcast(U32).rearrange("p (u n) -> p n u", u=2)[:, HALF:N],
+        )
+        key_grad(left(4), 0, 2, 0, HALF)
+        key_grad(right(4), 0, 3, 0, HALF)
+        key_grad(left(6), 0, 1, 0, HALF)
         score_grad(0, 2)
         score_grad(0, 3)
         deal(nc.vector.tensor_copy, do1_packed, do1_rows, 0, DO1_VECTOR)
-        quantize_into(v_mx[1], E4M3, 0, HALF, qm0_late)
+        quantize(v_mx[1], E4M3, v1_halves[0], 0, HALF)
         quantize_ds(0, 1)
-        key_grad(banks[5], 0, 2, HALF, N)
-        key_grad(banks[5], 0, 1, HALF, N, HALF)
-        quantize_into(v_mx[1], E4M3, HALF, N, ds0_first)
-        first = stage_tile("stage_first", HALF)
-        nc.vector.tensor_copy(first, banks[6][:, 0:HALF])
+        key_grad(left(5), 0, 2, HALF, N)
+        key_grad(right(5), 0, 1, HALF, N)
+        quantize(v_mx[1], E4M3, v1_halves[1], HALF, N)
+        vector_first = stage_tile("vector_first", HALF)
+        nc.vector.tensor_copy(vector_first, left(6))
         quantize(do_mx[1], E5M2, do1_packed)
-        move_on_gpsimd(*pack_views("p c i j", qm1_early, qm1_rows, P, P + HALF))
+        pack_on_gpsimd(qm1_early, qm1_rows, P, P + HALF)
 
-        stage = [do1_rows[:, j, h * HALF : (h + 1) * HALF] for j in range(PACK) for h in range(2)]
-        opening = stage_tile("stage_opening", N)
-        stage = [opening[:, 0:HALF], opening[:, HALF:N]] + stage[2:]
-        nc.scalar.copy(stage[0], banks[4][:, 0:HALF])
-        nc.scalar.copy(stage[1], banks[4][:, HALF:N])
+        opening = stage_tile("scalar_opening", N)
+        later = [do1_rows[:, j, h * HALF : (h + 1) * HALF] for j in range(1, PACK) for h in range(2)]
+        nc.scalar.copy(opening[:, 0:HALF], left(4))
+        nc.scalar.copy(opening[:, HALF:N], right(4))
         value_products(1)
-        scatter_on_vector(1, 0, 0, HALF, first)
-        scatter_on_scalar(2, 0, 0, stage[0])
-        scatter_on_scalar(3, 0, 0, stage[1])
-        nc.scalar.copy(stage[0], banks[5][:, 0:HALF])
-        nc.scalar.copy(stage[2], banks[5][:, HALF:N])
-        scatter_on_scalar(2, 0, HALF, stage[0])
-        scatter_on_scalar(1, 0, HALF, stage[2])
+        scatter_on_vector(1, 0, 0, HALF, vector_first)
+        scatter_on_scalar(2, 0, 0, opening[:, 0:HALF])
+        scatter_on_scalar(3, 0, 0, opening[:, HALF:N])
+        nc.scalar.copy(opening[:, 0:HALF], left(5))
+        nc.scalar.copy(later[0], right(5))
+        scatter_on_scalar(2, 0, HALF, opening[:, 0:HALF])
+        scatter_on_scalar(1, 0, HALF, later[0])
+
         score_grad(1, 0)
         score_grad(1, 1)
-        quantize_into(qm_mx[1], E4M3, P, P + HALF, qm1_early)
+        quantize(qm_mx[1], E4M3, qm1_early, P, P + HALF)
         quantize_ds(1, 0)
-        key_grad(banks[7], 1, 2, 0, HALF)
-        key_grad(banks[6], 1, 1, 0, HALF)
+        key_grad(left(7), 1, 2, 0, HALF)
+        key_grad(left(6), 1, 1, 0, HALF)
         score_grad(1, 2)
         score_grad(1, 3)
-        nc.vector.tensor_copy(first, banks[6][:, 0:HALF])
+        nc.vector.tensor_copy(vector_first, left(6))
         quantize_ds(1, 1)
-        qm1_late = ds_halves[1][1]
-        for i, j in enumerate((0, 3)):
-            move_on_gpsimd(*pack_views("p c i j", qm1_late[:, i * N : (i + 1) * N], qm1_rows, j * P, (j + 1) * P))
-        key_grad(banks[1], 1, 1, HALF, N)
-        key_grad(banks[0], 1, 2, HALF, N)
-        key_grad(banks[0], 0, 3, HALF, N, HALF)
-        key_grad(banks[2], 0, 0, 0, N)
-        scatter_on_vector(1, 1, 0, HALF, first)
-        second = stage_tile("stage_second", HALF)
-        nc.vector.tensor_copy(second, banks[1][:, 0:HALF])
-        scatter_on_vector(1, 1, HALF, N, second)
-        for i, j in enumerate((0, 3)):
-            quantize_into(qm_mx[1], E4M3, j * P, (j + 1) * P, qm1_late[:, i * N : (i + 1) * N])
-        key_grad(banks[3], 1, 0, 0, N)
-        key_grad(banks[4], 1, 3, 0, N)
-        nc.scalar.copy(stage[3], banks[7][:, 0:HALF])
-        scatter_on_scalar(2, 1, 0, stage[3])
-        nc.scalar.copy(stage[4], banks[0][:, 0:HALF])
-        nc.scalar.copy(stage[5], banks[0][:, HALF:N])
-        scatter_on_scalar(2, 1, HALF, stage[4])
-        store(nc.sync, 2)
-        store(nc.sync, 1)
-        scatter_on_scalar(3, 0, HALF, stage[5])
-        nc.scalar.copy(stage[6], banks[4][:, 0:HALF])
-        nc.scalar.copy(stage[7], banks[4][:, HALF:N])
-        scatter_on_scalar(3, 1, 0, stage[6])
-        scatter_on_scalar(3, 1, HALF, stage[7])
-        store(nc.sync, 3)
-        rest = weights[1][:, 2 * N :]
-        nc.vector.tensor_copy(rest[:, 0:N], banks[2][:])
-        nc.vector.tensor_copy(rest[:, N:], banks[3][:])
-        scatter_on_vector(0, 0, 0, 2 * N, rest)
-        store(nc.sync, 0)
+        qm1_late = {0: row(ds_halves[1][1], 0), last: row(ds_halves[1][1], 1)}
+        for j in (0, last):
+            pack_on_gpsimd(qm1_late[j], qm1_rows, j * P, (j + 1) * P)
+        key_grad(left(1), 1, 1, HALF, N)
+        key_grad(left(0), 1, 2, HALF, N)
+        key_grad(right(0), 0, 3, HALF, N)
+        key_grad(banks[2][:], 0, 0, 0, N)
+        scatter_on_vector(1, 1, 0, HALF, vector_first)
+        vector_second = stage_tile("vector_second", HALF)
+        nc.vector.tensor_copy(vector_second, left(1))
+        scatter_on_vector(1, 1, HALF, N, vector_second)
+        for j in (0, last):
+            quantize(qm_mx[1], E4M3, qm1_late[j], j * P, (j + 1) * P)
+        key_grad(banks[3][:], 1, 0, 0, N)
+        key_grad(banks[4][:], 1, 3, 0, N)
+        nc.scalar.copy(later[1], left(7))
+        scatter_on_scalar(2, 1, 0, later[1])
+        nc.scalar.copy(later[2], left(0))
+        nc.scalar.copy(later[3], right(0))
+        scatter_on_scalar(2, 1, HALF, later[2])
+        store(2)
+        store(1)
+        scatter_on_scalar(3, 0, HALF, later[3])
+        nc.scalar.copy(later[4], left(4))
+        nc.scalar.copy(later[5], right(4))
+        scatter_on_scalar(3, 1, 0, later[4])
+        scatter_on_scalar(3, 1, HALF, later[5])
+        store(3)
+        both = factors[1][:, 2 * N :]
+        nc.vector.tensor_copy(row(both, 0), banks[2][:])
+        nc.vector.tensor_copy(row(both, 1), banks[3][:])
+        scatter_on_vector(0, 0, 0, 2 * N, both)
+        store(0)

from contextlib import ExitStack

import concourse.mybir as mybir

B, N, T, D, R = 2, 512, 2048, 512, 512
FLOPS = 3 * 2 * B * N * D * R

F32 = mybir.dt.float32
BF16 = mybir.dt.bfloat16
U32 = mybir.dt.uint32
I32 = mybir.dt.int32
U16 = mybir.dt.uint16
U8 = mybir.dt.uint8
E4M3 = mybir.dt.float8_e4m3fn_x4
E5M2 = mybir.dt.float8_e5m2_x4
ACT = mybir.ActivationFunctionType
ALU = mybir.AluOpType

P = 128
PACK = 4
HALF = N // 2
ROWS = PACK * N
LIST_COLS = N // 16
RUN = 8
LINK = 16
RAW_BUFS = 10
Q1_VECTOR = 56
DO1_VECTOR = 48


def tile_attend_gat_tnh_k_kernel(tc, qT, kT, vT, doT, rw, qm, offs, out):
    nc = tc.nc
    with ExitStack() as ctx:
        keep = ctx.enter_context(tc.tile_pool(name="keep", bufs=1))
        ring = ctx.enter_context(tc.tile_pool(name="ring", bufs=1))
        psum = ctx.enter_context(tc.psum_pool(name="psum", bufs=1))

        def load_plane(pool_ap, label, j):
            plane = ring.tile([P, T], F32, name="%s%d" % (label, j), tag="raw", bufs=RAW_BUFS, align_bytes=64)
            nc.sync.dma_start(out=plane[:], in_=pool_ap.rearrange("(p j) t -> p j t", j=PACK)[:, j, :])
            return plane[:]

        def load_rows_into(words, src):
            rows = words.rearrange("p (j w) -> p j w", j=PACK)
            nc.sync.dma_start(out=rows, in_=src.rearrange("(p j) w -> p j w", j=PACK))
            return rows

        def load_rows(src, label):
            rows = ring.tile([P, PACK, N], F32, name=label, tag="raw", bufs=RAW_BUFS, align_bytes=64)
            nc.sync.dma_start(out=rows[:], in_=src.rearrange("(p j) w -> p j w", j=PACK))
            return rows[:]

        def packed_tile(name, tag=None, columns=N):
            return keep.tile([P, columns * PACK], BF16, name=name, tag=tag or name, align_bytes=64)[:]

        def stage_tile(name, width):
            return keep.tile([P, width], F32, name=name, align_bytes=64)[:]

        def mx_tiles(name, tag=None):
            codes = keep.tile([P, N], U32, name=name + "_codes", tag=tag or name + "_codes", align_bytes=64)
            scales = keep.tile([P, N], U8, name=name + "_scales", align_bytes=64)
            return codes, scales

        def entries(b, lo=0, hi=N):
            return offsets[:, b * LIST_COLS + lo // 16 : b * LIST_COLS + hi // 16]

        def row(rows, j):
            return rows[:, j * N : (j + 1) * N]

        def pair_row(pairs, j):
            return pairs.rearrange("p (u n e) -> p u e n", u=2, e=2)[:, j // 2, j % 2, :]

        def gather(dst, window, b, lo=0, hi=N):
            nc.vector.tensor_copy(dst[:, lo:hi], window.indirect(entries(b, lo, hi)))

        def gather_on_scalar(dst, window, b):
            nc.scalar.activation(dst, window.indirect(entries(b)), ACT.Copy)

        def weave(dst, pairs, lo):
            nc.vector.tensor_copy(
                dst.bitcast(I32).rearrange("p (c i u) -> p c u i", i=PACK, u=2),
                pairs.bitcast(I32).rearrange("p (u c i) -> p c u i", i=PACK, u=2)[:, lo // PACK : (lo + HALF) // PACK],
            )

        def pack_views(order, dst, src, lo, hi):
            return (
                dst.rearrange("p (c i j) -> " + order, i=PACK, j=PACK),
                src.rearrange("p j (c i) -> " + order, i=PACK)[:, lo // PACK : hi // PACK],
            )

        def pack(copy, dst, src, lo, hi):
            copy(*pack_views("p c j i", dst, src, lo, hi))

        def pack_on_gpsimd(dst, src, lo, hi):
            nc.gpsimd.tensor_scalar(*pack_views("p c i j", dst, src, lo, hi), 1.0, 0.0, ALU.mult, ALU.add)

        def deal(copy, dst, src, lo=0, hi=P):
            copy(
                dst.rearrange("p (t m j) -> p m j t", t=PACK, j=PACK)[:, lo:hi],
                src.rearrange("p j (m t) -> p m j t", t=PACK)[:, lo:hi],
            )

        def quantize(mx, fmt, packed, lo=0, hi=N):
            codes, scales = mx
            nc.vector.quantize_mx(out=codes[:, lo:hi].bitcast(fmt), scales=scales[:, lo:hi], in_=packed)

        def product(dst, left, left_fmt, block, right, right_fmt, lo=0, hi=N):
            cols = slice(block * P, (block + 1) * P)
            nc.tensor.matmul_mx(
                out=dst,
                lhsT=left[0][:, cols].bitcast(left_fmt),
                lhsT_scale=left[1][:, cols],
                rhs=right[0][:, lo:hi].bitcast(right_fmt),
                rhs_scale=right[1][:, lo:hi],
                start=True,
                stop=True,
            )

        offsets = keep.tile([P, B * LIST_COLS], U16, name="offsets")
        k_planes = [load_plane(kT, "k_plane", 0)]
        nc.sync.dma_start(offsets[:], offs)
        k_planes.extend([load_plane(kT, "k_plane", j) for j in range(1, PACK)])
        qm0_start = N
        ds0_start = qm0_start + ROWS - LINK
        factor0_start = ds0_start + N - LINK
        around_qm0 = keep.tile([P, factor0_start + ROWS], F32, name="around_qm0", align_bytes=64)
        q_rows = [load_rows(qT[0], "q0_rows"), load_rows_into(around_qm0[:, factor0_start:], qT[1])]
        gate = keep.tile([P, B * PACK], F32, name="gate")
        nc.sync.dma_start(
            out=gate[:].rearrange("p (b t) -> p b t", b=B), in_=rw.rearrange("b (p t) o -> p b (t o)", t=PACK)
        )
        do0_rows = load_rows(doT[0], "do0_rows")
        v_planes = [load_plane(vT, "v_plane", j) for j in range(PACK)]
        qm0_rows = load_rows_into(around_qm0[:, qm0_start : qm0_start + ROWS], qm[0])
        do1_rows = load_rows(doT[1], "do1_rows")
        qm1_rows = load_rows(qm[1], "qm1_rows")

        placed = []
        for j in range(D // P):
            tile = keep.tile([P, T], F32, name="placed%d" % j)
            nc.gpsimd.memset(tile[:], 0.0)
            placed.append(tile)

        banks = [psum.tile([P, N], F32, name="bank%d" % i) for i in range(8)]
        factor1 = keep.tile([P, ROWS], F32, name="factor1", align_bytes=64)
        factors = [around_qm0[:, factor0_start:], factor1[:]]
        do1_qm1 = keep.tile([P, 3 * N - LINK], F32, name="do1_qm1", align_bytes=64)
        last = PACK - 1

        k0_packed = packed_tile("k0_packed", "packed0")
        key_rows = packed_tile("key_rows")
        for j in range(PACK):
            gather(k0_packed.rearrange("p (n j) -> p j n", j=PACK)[:, j, :], k_planes[j], 0)
            gather_on_scalar(row(key_rows, j), k_planes[j], 1)
        k1_packed = packed_tile("k1_packed")
        pack(nc.scalar.copy, k1_packed, key_rows.rearrange("p (j n) -> p j n", j=PACK), 0, N)
        k0_mx = mx_tiles("k0")
        quantize(k0_mx, E4M3, k0_packed)
        q_packed = [packed_tile("q%d_packed" % b) for b in range(B)]
        q_mx = [mx_tiles("q%d" % b) for b in range(B)]
        k_mx = [k0_mx, mx_tiles("k1", "q0_packed")]
        deal(nc.vector.tensor_copy, q_packed[0], q_rows[0])
        quantize(q_mx[0], E4M3, q_packed[0])
        quantize(k_mx[1], E4M3, k1_packed)
        deal(nc.scalar.copy, q_packed[1], q_rows[1], Q1_VECTOR, P)
        deal(nc.vector.tensor_copy, q_packed[1], q_rows[1], 0, Q1_VECTOR)
        quantize(q_mx[1], E4M3, q_packed[1])
        do0_packed = packed_tile("do0_packed")
        do_mx = [mx_tiles("do%d" % b) for b in range(B)]
        deal(nc.vector.tensor_copy, do0_packed, do0_rows)
        quantize(do_mx[0], E5M2, do0_packed)

        neg_gate = row(do0_packed.bitcast(F32), 1)[:, 0 : B * PACK]
        nc.gpsimd.tensor_scalar(neg_gate, gate[:], -1.0, 0.0, ALU.mult, ALU.add)

        def scores(b, t):
            product(banks[b * PACK + t][:], q_mx[b], E4M3, t, k_mx[b], E4M3)

        def make_factor(b, t):
            factor = row(factors[b], t)
            col = slice(b * PACK + t, b * PACK + t + 1)
            nc.scalar.activation(factor, banks[b * PACK + t][:], ACT.Tanh)
            nc.scalar.activation(factor, factor, ACT.Square)
            nc.gpsimd.tensor_scalar(factor, factor, neg_gate[:, col], gate[:, col], ALU.mult, ALU.add)

        for t in range(PACK):
            scores(0, t)
        for t in range(PACK):
            make_factor(0, t)
        for t in range(PACK):
            scores(1, t)
            make_factor(1, t)

        qm0_early = packed_tile("qm0_early", columns=HALF)
        do1_packed = do1_qm1[:, 0 : 2 * N].bitcast(BF16)
        qm1_early = do1_qm1[:, 2 * N - LINK :].bitcast(BF16)
        ds_halves = [
            [around_qm0[:, ds0_start : ds0_start + N].bitcast(BF16), qm0_early],
            [packed_tile("ds1_first", columns=HALF), qm1_early],
        ]

        value_pairs = [packed_tile("value_pairs0"), around_qm0[:, 0 : 2 * N].bitcast(BF16)]
        value_rows = keep.tile([P, 2 * N], BF16, name="value_rows")[:]
        for j in range(last):
            gather(pair_row(value_pairs[0], j), v_planes[j], 0)
            if j < 2:
                gather(pair_row(value_pairs[1], j), v_planes[j], 1)
        v0_packed = packed_tile("v0_packed", "packed0")
        v_mx = [mx_tiles("v%d" % b) for b in range(B)]
        for lo in (0, HALF):
            half_packed = v0_packed[:, lo * PACK : (lo + HALF) * PACK]
            gather(pair_row(value_pairs[0], last), v_planes[last], 0, lo, lo + HALF)
            weave(half_packed, value_pairs[0], lo)
            quantize(v_mx[0], E4M3, half_packed, lo, lo + HALF)
        for j in range(2, PACK):
            gather_on_scalar(row(value_rows, j - 2), v_planes[j], 1)

        qm_mx = [mx_tiles("qm%d" % b) for b in range(B)]
        qm0_late = packed_tile("qm0_late", columns=HALF)
        ds_mx = [mx_tiles("ds%d" % b) for b in range(B)]

        def value_products(b):
            for c in range(PACK):
                for t in range(PACK):
                    product(banks[c][:, t * P : (t + 1) * P], do_mx[b], E5M2, t, v_mx[b], E4M3, c * P, (c + 1) * P)

        def score_grad(b, c):
            nc.vector.tensor_tensor(
                row(ds_halves[b][c // 2], c % 2).rearrange("p (c i t) -> p c t i", i=PACK, t=PACK),
                banks[c][:].rearrange("p (t c i) -> p c t i", i=PACK, t=PACK),
                factors[b].rearrange("p (t c i) -> p c t i", i=PACK, t=PACK)[:, c * P // PACK : (c + 1) * P // PACK],
                ALU.mult,
            )

        def quantize_ds(b, h):
            quantize(ds_mx[b], E5M2, ds_halves[b][h], h * HALF, (h + 1) * HALF)

        def key_grad(dst, b, j, lo, hi):
            product(dst, qm_mx[b], E4M3, j, ds_mx[b], E5M2, lo, hi)

        def left(i):
            return banks[i][:, 0:HALF]

        def right(i):
            return banks[i][:, HALF:N]

        def scatter_on_vector(j, b, lo, hi, stage):
            nc.vector.tensor_copy(placed[j][:].indirect(entries(b, lo, hi)), stage)

        def scatter_on_scalar(j, b, lo, stage):
            nc.scalar.activation(placed[j][:].indirect(entries(b, lo, lo + HALF)), stage, ACT.Copy)

        def store(j):
            nc.sync.dma_start(out=out[j * P : (j + 1) * P, :], in_=placed[j][:])

        value_products(0)
        pack(nc.vector.tensor_copy, qm0_early, qm0_rows, HALF, N)
        pack(nc.scalar.copy, qm0_late, qm0_rows, 0, HALF)
        nc.scalar.copy(
            value_pairs[1][:, 2 * N :].rearrange("p (c i e) -> p c e i", i=RUN, e=2),
            value_rows.rearrange("p (e c i) -> p c e i", i=RUN, e=2),
        )
        deal(nc.scalar.copy, do1_packed, do1_rows, DO1_VECTOR, P)
        score_grad(0, 0)
        score_grad(0, 1)
        quantize(qm_mx[0], E4M3, qm0_early, HALF, N)
        quantize(qm_mx[0], E4M3, qm0_late, 0, HALF)
        quantize_ds(0, 0)
        v1_halves = [qm0_late, ds_halves[0][0]]
        weave(v1_halves[0], value_pairs[1], 0)
        nc.gpsimd.tensor_copy(
            v1_halves[1].bitcast(U32).rearrange("p (n u) -> p n u", u=2),
            value_pairs[1].bitcast(U32).rearrange("p (u n) -> p n u", u=2)[:, HALF:N],
        )
        key_grad(left(4), 0, 2, 0, HALF)
        key_grad(right(4), 0, 3, 0, HALF)
        key_grad(left(6), 0, 1, 0, HALF)
        score_grad(0, 2)
        score_grad(0, 3)
        deal(nc.vector.tensor_copy, do1_packed, do1_rows, 0, DO1_VECTOR)
        quantize(v_mx[1], E4M3, v1_halves[0], 0, HALF)
        quantize_ds(0, 1)
        key_grad(left(5), 0, 2, HALF, N)
        key_grad(right(5), 0, 1, HALF, N)
        quantize(v_mx[1], E4M3, v1_halves[1], HALF, N)
        vector_first = stage_tile("vector_first", HALF)
        nc.vector.tensor_copy(vector_first, left(6))
        quantize(do_mx[1], E5M2, do1_packed)
        pack_on_gpsimd(qm1_early, qm1_rows, P, P + HALF)

        opening = stage_tile("scalar_opening", N)
        later = [do1_rows[:, j, h * HALF : (h + 1) * HALF] for j in range(1, PACK) for h in range(2)]
        nc.scalar.copy(opening[:, 0:HALF], left(4))
        nc.scalar.copy(opening[:, HALF:N], right(4))
        value_products(1)
        scatter_on_vector(1, 0, 0, HALF, vector_first)
        scatter_on_scalar(2, 0, 0, opening[:, 0:HALF])
        scatter_on_scalar(3, 0, 0, opening[:, HALF:N])
        nc.scalar.copy(opening[:, 0:HALF], left(5))
        nc.scalar.copy(later[0], right(5))
        scatter_on_scalar(2, 0, HALF, opening[:, 0:HALF])
        scatter_on_scalar(1, 0, HALF, later[0])

        score_grad(1, 0)
        score_grad(1, 1)
        quantize(qm_mx[1], E4M3, qm1_early, P, P + HALF)
        quantize_ds(1, 0)
        key_grad(left(7), 1, 2, 0, HALF)
        key_grad(left(6), 1, 1, 0, HALF)
        score_grad(1, 2)
        score_grad(1, 3)
        nc.vector.tensor_copy(vector_first, left(6))
        quantize_ds(1, 1)
        qm1_late = {0: row(ds_halves[1][1], 0), last: row(ds_halves[1][1], 1)}
        for j in (0, last):
            pack_on_gpsimd(qm1_late[j], qm1_rows, j * P, (j + 1) * P)
        key_grad(left(1), 1, 1, HALF, N)
        key_grad(left(0), 1, 2, HALF, N)
        key_grad(right(0), 0, 3, HALF, N)
        key_grad(banks[2][:], 0, 0, 0, N)
        scatter_on_vector(1, 1, 0, HALF, vector_first)
        vector_second = stage_tile("vector_second", HALF)
        nc.vector.tensor_copy(vector_second, left(1))
        scatter_on_vector(1, 1, HALF, N, vector_second)
        for j in (0, last):
            quantize(qm_mx[1], E4M3, qm1_late[j], j * P, (j + 1) * P)
        key_grad(banks[3][:], 1, 0, 0, N)
        key_grad(banks[4][:], 1, 3, 0, N)
        nc.scalar.copy(later[1], left(7))
        scatter_on_scalar(2, 1, 0, later[1])
        nc.scalar.copy(later[2], left(0))
        nc.scalar.copy(later[3], right(0))
        scatter_on_scalar(2, 1, HALF, later[2])
        store(2)
        store(1)
        scatter_on_scalar(3, 0, HALF, later[3])
        nc.scalar.copy(later[4], left(4))
        nc.scalar.copy(later[5], right(4))
        scatter_on_scalar(3, 1, 0, later[4])
        scatter_on_scalar(3, 1, HALF, later[5])
        store(3)
        both = factors[1][:, 2 * N :]
        nc.vector.tensor_copy(row(both, 0), banks[2][:])
        nc.vector.tensor_copy(row(both, 1), banks[3][:])
        scatter_on_vector(0, 0, 0, 2 * N, both)
        store(0)
